import numpy as np
import ml_dtypes


def mxq(x, axis, fmt="e4m3"):
    dtype, down = {"e4m3": (ml_dtypes.float8_e4m3fn, 7), "e5m2": (ml_dtypes.float8_e5m2, 14)}[fmt]
    v = np.moveaxis(np.asarray(x, np.float32).astype(ml_dtypes.bfloat16).astype(np.float64), axis, -1)
    blocks = v.reshape(v.shape[:-1] + (-1, 32))
    amax = np.abs(blocks).max(-1, keepdims=True)
    byte = np.maximum(np.where(amax > 0, np.frexp(amax)[1] - 1 + 127, 0) - down, 1)
    scale = np.exp2(byte - 127.0)
    codes = (blocks / scale).astype(np.float32).astype(dtype).astype(np.float64)
    return np.moveaxis((codes * scale).reshape(v.shape), -1, axis)


WIDE = False


def mx_kscale(k):
    if not WIDE:
        return np.ones(k)
    levels = np.array([10, -10, 5, -5, 0])
    if k % 512:
        return np.exp2(np.random.permutation(np.resize(levels, k // 32))).repeat(32)
    a = np.empty((k // 512, 16))
    for p in range(k // 512):
        a[p, :8] = np.random.permutation(np.resize(levels, 8))
        for g in range(8):
            far = levels[np.abs(levels - a[p, g]) >= 10]
            a[p, g + 8] = far[np.random.randint(len(far))]
    return np.exp2(a.ravel()).repeat(32)


def f64(x):
    return np.asarray(x).astype(np.float64)


def striped(idx):
    return np.tile(idx.reshape(-1, 16).T, (8, 1)).astype(np.uint16)


def unstriped(offs):
    return offs[:16].T.reshape(-1).astype(np.int64)


E2M1 = np.array([0.0, 0.5, 1.0, 1.5, 2.0, 3.0, 4.0, 6.0, -0.0, -0.5, -1.0, -1.5, -2.0, -3.0, -4.0, -6.0])


def pack_weight(w, fmt):
    k, n = w.shape
    w = f64(np.asarray(w, np.float32).astype(ml_dtypes.bfloat16)).reshape(k // 32, 32, n)
    amax = np.abs(w).max(1)
    if fmt == "e4m3":
        byte = np.frexp(amax)[1] - 1 + 127 - 7
    else:
        mant, ex = np.frexp(amax / 6.0)
        byte = np.where(mant > 0.5, ex, ex - 1) + 127
    byte = np.clip(np.where(amax > 0, byte, 1), 1, 254)
    scaled = (w * np.exp2(127.0 - byte)[:, None, :]).reshape(k, n).astype(np.float32)
    by_word = np.ascontiguousarray(scaled.reshape(k // 512, 128, 4, n).transpose(0, 1, 3, 2))
    if fmt == "e4m3":
        words = by_word.astype(ml_dtypes.float8_e4m3fn).view(np.uint8)
    else:
        c = by_word.astype(ml_dtypes.float4_e2m1fn).view(np.uint8) & 0xF
        words = (c[..., 0::2] | (c[..., 1::2] << 4)).reshape(k // 512, 128, 2 * n)
    return np.ascontiguousarray(words), np.ascontiguousarray(byte.astype(np.uint8).reshape(k // 512, 16, n))


def unpack_weight(words, scales, fmt):
    g, _, n = scales.shape
    words = np.ascontiguousarray(words).reshape(g, 128, n, -1)
    if fmt == "e4m3":
        vals = words.view(ml_dtypes.float8_e4m3fn).astype(np.float64)
    else:
        nib = np.empty((g, 128, n, 4), np.uint8)
        nib[..., 0::2] = words & 0xF
        nib[..., 1::2] = words >> 4
        vals = E2M1[nib]
    vals = vals * np.repeat(np.exp2(scales.astype(np.float64) - 127.0), 8, axis=1)[..., None]
    return vals.transpose(0, 1, 3, 2).reshape(g * 512, n)


def gelu(v):
    return 0.5 * v * (1.0 + np.tanh(np.sqrt(2.0 / np.pi) * (v + 0.044715 * v**3)))


K, T, S, M, N = 1024, 2048, 1024, 512, 384

def setup_inputs():
    n = np.random.standard_normal
    s = mx_kscale(K)[:, None]
    u = mx_kscale(S)
    idx = np.random.permutation(T)[:S]
    tab_words, tab_scales = pack_weight(n((K, T)) * s / np.sqrt(K), "e4m3")
    tab2_words, tab2_scales = pack_weight(n((K, T)) * s / np.sqrt(K), "e4m3")
    ws_words, ws_scales = pack_weight(n((K, N)) * s / np.sqrt(K), "e2m1")
    wdT = n((N, T)) / np.sqrt(S)
    wdT[:, idx] /= u
    return {
        "x": (n((K, M)) / s).astype(np.float32),
        "tab_words": tab_words, "tab_scales": tab_scales,
        "tab2_words": tab2_words, "tab2_scales": tab2_scales,
        "offs": striped(idx),
        "g": (np.exp(0.3 * n(S)) * u).astype(np.float32),
        "wdT": wdT.astype(np.float32),
        "ws_words": ws_words, "ws_scales": ws_scales,
    }

def reference(x, tab_words, tab_scales, tab2_words, tab2_scales, offs, g, wdT, ws_words, ws_scales):
    v = unpack_weight(tab_words, tab_scales, "e4m3")[:, unstriped(offs)]
    v2 = unpack_weight(tab2_words, tab2_scales, "e4m3")[:, unstriped(offs)]
    ws = unpack_weight(ws_words, ws_scales, "e2m1")
    wd = f64(wdT)[:, unstriped(offs)]
    xq = mxq(f64(x), 0, "e4m3")
    a = v.T @ xq
    b = v2.T @ xq
    h = np.sqrt(a * a + b * b) * f64(g)[:, None]
    return mxq(wd, 1, "e4m3") @ mxq(h, 0, "e4m3") + ws.T @ xq

@@ -1,0 +1,264 @@
+from contextlib import ExitStack
+
+import concourse.mybir as mybir
+from concourse.masks import make_identity
+
+K, T, S, M, N = 1024, 2048, 1024, 512, 384
+FLOPS = 2 * (2 * K * S * M + S * N * M + K * N * M)
+
+F32 = mybir.dt.float32
+BF16 = mybir.dt.bfloat16
+I32 = mybir.dt.int32
+U32 = mybir.dt.uint32
+U16 = mybir.dt.uint16
+U8 = mybir.dt.uint8
+FP8X4 = mybir.dt.float8_e4m3fn_x4
+FP4X4 = mybir.dt.float4_e2m1fn_x4
+ACT = mybir.ActivationFunctionType
+MULT = mybir.AluOpType.mult
+
+P = 128
+PACK = 4
+PASS = P * PACK
+K_PASSES = K // PASS
+J_PASSES = S // PASS
+M_BLOCKS = M // P
+N_BLOCKS = N // P
+QUADRANTS = 4
+QUADRANT = P // QUADRANTS
+SCALE_ROWS = 4
+LIST_GROUP = 16
+BANK_BYTES = 2048
+BANKS = {"even": tuple(range(8)), "odd": (0, 1, 2), "energy": (3, 4, 5), "sums": (6, 7)}
+REGION_BYTES = 4 * T
+EVEN, ODD, WD = (0, 1), (2, 3), (4, 5, 6)
+X_LAST, SCALES = 7, 8
+
+
+def tile_list_motion_energy_pool_kernel(
+    tc, x, tab_words, tab_scales, tab2_words, tab2_scales, offs, g, wdT, ws_words, ws_scales, out
+):
+    nc = tc.nc
+    with ExitStack() as ctx:
+        keep = ctx.enter_context(tc.tile_pool(name="keep", bufs=1))
+        ring = ctx.enter_context(tc.tile_pool(name="ring", bufs=4))
+        reuse = ctx.enter_context(tc.tile_pool(name="reuse", bufs=1))
+        psum = ctx.enter_context(tc.psum_pool(name="psum", bufs=1))
+
+        def region_tile(region, part, shape, dtype, name):
+            return reuse.tile(shape, dtype, name=name, align_bytes=64, offset=region * REGION_BYTES + part)
+
+        turns = {"even": 0, "odd": 0, "energy": 0, "sums": 0}
+
+        def bank_tile(role, shape):
+            banks = BANKS[role]
+            turn = turns[role]
+            turns[role] = turn + 1
+            return psum.tile(shape, F32, name="%s%d" % (role, turn), offset=banks[turn % len(banks)] * BANK_BYTES)
+
+        offsets = keep.tile([P, S // LIST_GROUP], U16, name="offsets")
+        nc.sync.dma_start(offsets[:], offs)
+        gains = keep.tile([P, J_PASSES, PACK], F32, name="gains")
+        nc.sync.dma_start(gains[:], g.rearrange("(h p t) -> p h t", p=P, t=PACK))
+
+        def load_table_scales(name, scales, part):
+            rows = region_tile(SCALES, part * T, [P, T], U8, name)
+            nc.vector.memset(rows[:].bitcast(I32), 0)
+            for q in range(QUADRANTS):
+                nc.sync.dma_start(
+                    rows[QUADRANT * q : QUADRANT * q + K_PASSES * SCALE_ROWS, :].bitcast(I32),
+                    scales[:, SCALE_ROWS * q : SCALE_ROWS * (q + 1), :].bitcast(I32),
+                )
+            return rows
+
+        def load_table_words(name, words, a, regions):
+            tile_a = region_tile(regions[a], 0, [P, T], I32, "%s%d" % (name, a))
+            nc.sync.dma_start(tile_a[:], words[a].rearrange("p t i -> p (t i)").bitcast(I32))
+            return tile_a
+
+        def load_x(a):
+            raw = keep.tile([P, PACK, M], F32, name="x_raw%d" % a)
+            nc.sync.dma_start(raw[:], x[a * PASS : (a + 1) * PASS, :].rearrange("(p i) m -> p i m", i=PACK))
+            return raw
+
+        even_scale_rows = load_table_scales("even_scale_rows", tab_scales, 0)
+        even_words = [load_table_words("even_words", tab_words, 0, EVEN)]
+        x_raw = [load_x(0)]
+        odd_scale_rows = load_table_scales("odd_scale_rows", tab2_scales, 1)
+        x_raw.append(load_x(1))
+        even_words.append(load_table_words("even_words", tab_words, 1, EVEN))
+        odd_words = [load_table_words("odd_words", tab2_words, a, ODD) for a in range(K_PASSES)]
+
+        wd_rows = []
+        for nb in range(N_BLOCKS):
+            rows = region_tile(WD[nb], 0, [P, T], F32, "wd_rows%d" % nb)
+            nc.sync.dma_start(rows[:], wdT[nb * P : (nb + 1) * P, :])
+            wd_rows.append(rows)
+
+        ws_codes = keep.tile([P, K_PASSES, 2 * N], U8, name="ws_codes", align_bytes=64)
+        nc.sync.dma_start(ws_codes[:].bitcast(I32), ws_words.rearrange("a p c -> p a c").bitcast(I32))
+        ws_planes = keep.tile([P, K_PASSES, N], U8, name="ws_planes", align_bytes=64)
+        nc.gpsimd.memset(ws_planes[:].bitcast(I32), 0)
+        for q in range(QUADRANTS):
+            nc.sync.dma_start(
+                ws_planes[QUADRANT * q : QUADRANT * q + SCALE_ROWS, :, :].bitcast(I32),
+                ws_scales[:, SCALE_ROWS * q : SCALE_ROWS * (q + 1), :].rearrange("a r c -> r a c").bitcast(I32),
+            )
+
+        identity = keep.tile([P, P], F32, name="identity")
+        make_identity(nc, identity[:])
+
+        def gather_scales(name, rows):
+            picked = keep.tile([P, S], U8, name=name, align_bytes=64)
+            nc.vector.tensor_copy(picked[:], rows[:].indirect(offsets[:]))
+            return picked
+
+        def gather_words(picked, name, words, a, place, pieces):
+            width = S // pieces
+            for piece in range(pieces):
+                part = place(piece, [P, width], "%s%d%d" % (name, a, piece))
+                cols = width // LIST_GROUP
+                nc.vector.tensor_copy(part[:], words[:].bitcast(U32).indirect(offsets[:, piece * cols : (piece + 1) * cols]))
+                for jp in range(J_PASSES):
+                    start = jp * PASS - piece * width
+                    if 0 <= start < width:
+                        picked[a, jp] = part[:, start : start + PASS]
+
+        def on_region(region):
+            return lambda piece, shape, name: region_tile(region, 4 * shape[1] * piece, shape, U32, name)
+
+        def fresh(piece, shape, name):
+            return keep.tile(shape, U32, name=name, align_bytes=64)
+
+        def quantise(name, values, width, place=fresh):
+            codes = place(0, [P, width], name + "_codes")
+            plane = keep.tile([P, width], U8, name=name + "_plane", align_bytes=64)
+            nc.vector.quantize_mx(out=codes[:].bitcast(FP8X4), scales=plane[:], in_=values)
+            return codes, plane
+
+        even_planes = gather_scales("even_planes", even_scale_rows)
+        even_picked, odd_picked = {}, {}
+        gather_words(even_picked, "even_picked", even_words[0], 0, fresh, 1)
+        odd_planes = gather_scales("odd_planes", odd_scale_rows)
+
+        x_mx = []
+        for a in range(K_PASSES):
+            x_bf = region_tile(X_LAST, 2 * M * PACK * (K_PASSES - 1 - a), [P, M * PACK], BF16, "x_bf%d" % a)
+            nc.scalar.copy(
+                x_bf[:].rearrange("p (c e i) -> p c i e", e=4, i=PACK),
+                x_raw[a][:].rearrange("p i (c e) -> p c i e", e=4),
+            )
+            x_mx.append(quantise("x%d" % a, x_bf[:], M, fresh if a else lambda piece, shape, name: region_tile(SCALES, T, shape, U32, name)))
+
+        gather_words(even_picked, "even_picked", even_words[1], 1, on_region(X_LAST), 1)
+
+        def squared_response(role, picked, planes, mb, jp, squares):
+            bank = bank_tile(role, [P, PASS])
+            m_cols = slice(mb * P, (mb + 1) * P)
+            for a in range(K_PASSES):
+                x_codes, x_plane = x_mx[a]
+                nc.tensor.matmul_mx(
+                    out=bank[:],
+                    lhsT=x_codes[:, m_cols].bitcast(FP8X4),
+                    lhsT_scale=x_plane[:, m_cols],
+                    rhs=picked[a, jp].bitcast(FP8X4),
+                    rhs_scale=planes[SCALE_ROWS * a :, jp * PASS : (jp + 1) * PASS],
+                    start=(a == 0),
+                    stop=(a == K_PASSES - 1),
+                )
+            nc.scalar.activation(squares[:], bank[:].rearrange("p (q t) -> p t q", t=PACK), ACT.Square)
+
+        units = [(mb, jp) for mb in range(M_BLOCKS) for jp in range(J_PASSES)]
+        even_squares = {}
+        for mb, jp in units:
+            squares = keep.tile([P, PACK, P], F32, name="even_squares%d%d" % (mb, jp))
+            squared_response("even", even_picked, even_planes, mb, jp, squares)
+            even_squares[mb, jp] = squares
+
+        gather_words(odd_picked, "odd_picked", odd_words[0], 0, on_region(EVEN[1]), 1)
+        gather_words(odd_picked, "odd_picked", odd_words[1], 1, on_region(ODD[0]), J_PASSES)
+
+        def odd_part(mb, jp):
+            squares = ring.tile([P, PACK, P], F32, name="odd_squares")
+            squared_response("odd", odd_picked, odd_planes, mb, jp, squares)
+            return squares
+
+        def amplitude(mb, jp, odd_squares):
+            energy = bank_tile("energy", [P, PACK, P])
+            for t in range(PACK):
+                nc.tensor.matmul(energy[:, t, :], even_squares[mb, jp][:, t, :], identity[:], start=True, stop=False, is_transpose=True)
+                nc.tensor.matmul(energy[:, t, :], odd_squares[:, t, :], identity[:], start=False, stop=True, is_transpose=True)
+            root = keep.tile([P, P, PACK], F32, name="root%d%d" % (mb, jp))
+            nc.scalar.activation(root[:], energy[:].rearrange("p t m -> p m t"), ACT.Sqrt)
+            return root
+
+        def gained(mb, jp, root, h_unit):
+            nc.vector.tensor_tensor(h_unit.rearrange("p (m t) -> p m t", t=PACK), root[:], gains[:, jp, :].unsqueeze(1).to_broadcast([P, P, PACK]), MULT)
+
+        def pooling_weights(nb):
+            picked = region_tile(((ODD[1],) + WD)[nb], 0, [P, S], BF16, "wd_picked%d" % nb)
+            nc.vector.tensor_copy(picked[:], wd_rows[nb][:].indirect(offsets[:]))
+            pairs = picked[:].bitcast(F32)
+            turned = bank_tile("energy", [P, J_PASSES, 2, P])
+            for jp in range(J_PASSES):
+                for u in range(2):
+                    nc.tensor.transpose(turned[:, jp, u, :], pairs[:, 2 * P * jp + u : 2 * P * (jp + 1) : 2], identity[:])
+            wd_bf = keep.tile([P, J_PASSES * P * PACK], BF16, name="wd_bf%d" % nb, align_bytes=64)
+            nc.scalar.copy(
+                wd_bf[:].bitcast(F32).rearrange("p (h n u) -> p h n u", h=J_PASSES, u=2),
+                turned[:].rearrange("p h u n -> p h n u"),
+            )
+            return quantise("wd%d" % nb, wd_bf[:], J_PASSES * P)
+
+        def pool_block(mb):
+            m_cols = slice(mb * P, (mb + 1) * P)
+            sums = bank_tile("sums", [P, N_BLOCKS, P])
+            for a in range(K_PASSES):
+                x_codes, x_plane = x_mx[a]
+                for nb in range(N_BLOCKS):
+                    nc.tensor.matmul_mx(
+                        out=sums[:, nb, :],
+                        lhsT=ws_codes[:, a, 2 * P * nb : 2 * P * (nb + 1)].bitcast(FP4X4),
+                        lhsT_scale=ws_planes[:, a, nb * P : (nb + 1) * P],
+                        rhs=x_codes[:, m_cols].bitcast(FP8X4),
+                        rhs_scale=x_plane[:, m_cols],
+                        start=(a == 0 and nb == 0),
+                        stop=False,
+                    )
+            for jp in range(J_PASSES):
+                h_codes, h_plane = h_mx[mb, jp]
+                for nb in range(N_BLOCKS):
+                    wd_codes, wd_plane = wd_mx[nb]
+                    nc.tensor.matmul_mx(
+                        out=sums[:, nb, :],
+                        lhsT=wd_codes[:, jp * P : (jp + 1) * P].bitcast(FP8X4),
+                        lhsT_scale=wd_plane[:, jp * P : (jp + 1) * P],
+                        rhs=h_codes[:].bitcast(FP8X4),
+                        rhs_scale=h_plane[:],
+                        start=False,
+                        stop=(jp == J_PASSES - 1 and nb == N_BLOCKS - 1),
+                    )
+            result = ring.tile([P, N_BLOCKS, P], F32, name="result")
+            nc.scalar.copy(result[:], sums[:])
+            nc.sync.dma_start(out.rearrange("(b p) m -> p b m", p=P)[:, :, m_cols], result[:])
+
+        odd_squares, roots, wd_mx = {}, {}, []
+        for step in range(len(units) + 2):
+            if step < len(units):
+                odd_squares[step] = odd_part(*units[step])
+            if step >= 2:
+                roots[step - 2] = amplitude(*units[step - 2], odd_squares[step - 2])
+            if step in (4, 6, 7):
+                wd_mx.append(pooling_weights(len(wd_mx)))
+
+        h_bf = {}
+        h_mx = {}
+        for step in range(len(units) + 1):
+            if step < len(units):
+                h_bf[step] = region_tile(WD[2], 2 * PASS * step, [P, PASS], BF16, "h_bf%d" % step)
+                gained(*units[step], roots[step], h_bf[step][:])
+            if step >= 1:
+                mb, jp = units[step - 1]
+                h_mx[mb, jp] = quantise("h%d%d" % (mb, jp), h_bf[step - 1][:], P)
+                if jp == J_PASSES - 1:
+                    pool_block(mb)

@@ -16,6 +16,7 @@ FP8X4 = mybir.dt.float8_e4m3fn_x4
 FP4X4 = mybir.dt.float4_e2m1fn_x4
 ACT = mybir.ActivationFunctionType
 MULT = mybir.AluOpType.mult
+ADD = mybir.AluOpType.add
 
 P = 128
 PACK = 4
@@ -28,11 +29,17 @@ QUADRANTS = 4
 QUADRANT = P // QUADRANTS
 SCALE_ROWS = 4
 LIST_GROUP = 16
+RUN = 8
+BLOCKS = PASS // (PACK * RUN)
+HALF = M // 2
 BANK_BYTES = 2048
-BANKS = {"even": tuple(range(8)), "odd": (0, 1, 2), "energy": (3, 4, 5), "sums": (6, 7)}
+ODD_BANKS = ((0, 1), (2, 3), (4, 5), (0, 1))
+TURN_BANKS = ((4, 5), (0, 1), (4, 5))
+SUM_BANKS = (6, 7, 2, 3)
 REGION_BYTES = 4 * T
 EVEN, ODD, WD = (0, 1), (2, 3), (4, 5, 6)
-X_LAST, SCALES = 7, 8
+X_RAW = (7, 8)
+X_BF, SCALES, SQUARES = 9, 10, 11
 
 
 def tile_list_motion_energy_pool_kernel(
@@ -41,28 +48,23 @@ def tile_list_motion_energy_pool_kernel(
     nc = tc.nc
     with ExitStack() as ctx:
         keep = ctx.enter_context(tc.tile_pool(name="keep", bufs=1))
-        ring = ctx.enter_context(tc.tile_pool(name="ring", bufs=4))
         reuse = ctx.enter_context(tc.tile_pool(name="reuse", bufs=1))
         psum = ctx.enter_context(tc.psum_pool(name="psum", bufs=1))
 
-        def region_tile(region, part, shape, dtype, name):
-            return reuse.tile(shape, dtype, name=name, align_bytes=64, offset=region * REGION_BYTES + part)
+        def kept(name, shape, dtype):
+            return keep.tile(shape, dtype, name=name, align_bytes=64)
 
-        turns = {"even": 0, "odd": 0, "energy": 0, "sums": 0}
+        def placed(name, shape, dtype, region, start=0):
+            return reuse.tile(shape, dtype, name=name, align_bytes=64, offset=region * REGION_BYTES + start)
 
-        def bank_tile(role, shape):
-            banks = BANKS[role]
-            turn = turns[role]
-            turns[role] = turn + 1
-            return psum.tile(shape, F32, name="%s%d" % (role, turn), offset=banks[turn % len(banks)] * BANK_BYTES)
+        def bank_tile(name, shape, dtype, bank):
+            return psum.tile(shape, dtype, name=name, offset=bank * BANK_BYTES)
 
-        offsets = keep.tile([P, S // LIST_GROUP], U16, name="offsets")
-        nc.sync.dma_start(offsets[:], offs)
-        gains = keep.tile([P, J_PASSES, PACK], F32, name="gains")
-        nc.sync.dma_start(gains[:], g.rearrange("(h p t) -> p h t", p=P, t=PACK))
+        def list_part(jp):
+            cols = PASS // LIST_GROUP
+            return offsets[:, jp * cols : (jp + 1) * cols]
 
-        def load_table_scales(name, scales, part):
-            rows = region_tile(SCALES, part * T, [P, T], U8, name)
+        def load_table_scales(rows, scales):
             nc.vector.memset(rows[:].bitcast(I32), 0)
             for q in range(QUADRANTS):
                 nc.sync.dma_start(
@@ -71,148 +73,209 @@ def tile_list_motion_energy_pool_kernel(
                 )
             return rows
 
-        def load_table_words(name, words, a, regions):
-            tile_a = region_tile(regions[a], 0, [P, T], I32, "%s%d" % (name, a))
+        def load_table_words(name, words, a, region):
+            tile_a = placed("%s%d" % (name, a), [P, T], I32, region)
             nc.sync.dma_start(tile_a[:], words[a].rearrange("p t i -> p (t i)").bitcast(I32))
             return tile_a
 
         def load_x(a):
-            raw = keep.tile([P, PACK, M], F32, name="x_raw%d" % a)
+            raw = placed("x_raw%d" % a, [P, PACK, M], F32, X_RAW[a])
             nc.sync.dma_start(raw[:], x[a * PASS : (a + 1) * PASS, :].rearrange("(p i) m -> p i m", i=PACK))
             return raw
 
-        even_scale_rows = load_table_scales("even_scale_rows", tab_scales, 0)
-        even_words = [load_table_words("even_words", tab_words, 0, EVEN)]
+        offsets = keep.tile([P, S // LIST_GROUP], U16, name="offsets")
+        nc.sync.dma_start(offsets[:], offs)
+        even_words = [load_table_words("even_words", tab_words, 0, EVEN[0])]
+        even_scale_rows = load_table_scales(placed("even_scale_rows", [P, T], U8, SCALES, T), tab_scales)
         x_raw = [load_x(0)]
-        odd_scale_rows = load_table_scales("odd_scale_rows", tab2_scales, 1)
+        gain_rows = kept("gain_rows", [P, P], F32)
+        nc.gpsimd.memset(gain_rows[:], 0.0)
+        for jp in range(J_PASSES):
+            nc.sync.dma_start(
+                gain_rows[PACK * jp : PACK * (jp + 1), :].rearrange("t (b r) -> t b r", r=RUN),
+                g[jp * PASS : (jp + 1) * PASS].rearrange("(b t r) -> t b r", t=PACK, r=RUN),
+            )
+        odd_scale_rows = load_table_scales(placed("odd_scale_rows", [P, T], U8, SCALES), tab2_scales)
         x_raw.append(load_x(1))
-        even_words.append(load_table_words("even_words", tab_words, 1, EVEN))
-        odd_words = [load_table_words("odd_words", tab2_words, a, ODD) for a in range(K_PASSES)]
-
-        wd_rows = []
-        for nb in range(N_BLOCKS):
-            rows = region_tile(WD[nb], 0, [P, T], F32, "wd_rows%d" % nb)
-            nc.sync.dma_start(rows[:], wdT[nb * P : (nb + 1) * P, :])
-            wd_rows.append(rows)
-
-        ws_codes = keep.tile([P, K_PASSES, 2 * N], U8, name="ws_codes", align_bytes=64)
+        even_words.append(load_table_words("even_words", tab_words, 1, EVEN[1]))
+        odd_words = [load_table_words("odd_words", tab2_words, a, ODD[a]) for a in range(K_PASSES)]
+        ws_codes = kept("ws_codes", [P, K_PASSES, 2 * N], U8)
         nc.sync.dma_start(ws_codes[:].bitcast(I32), ws_words.rearrange("a p c -> p a c").bitcast(I32))
-        ws_planes = keep.tile([P, K_PASSES, N], U8, name="ws_planes", align_bytes=64)
+        ws_planes = kept("ws_planes", [P, K_PASSES, N], U8)
         nc.gpsimd.memset(ws_planes[:].bitcast(I32), 0)
         for q in range(QUADRANTS):
             nc.sync.dma_start(
                 ws_planes[QUADRANT * q : QUADRANT * q + SCALE_ROWS, :, :].bitcast(I32),
                 ws_scales[:, SCALE_ROWS * q : SCALE_ROWS * (q + 1), :].rearrange("a r c -> r a c").bitcast(I32),
             )
+        wd_rows = []
+        for nb in range(N_BLOCKS):
+            rows = placed("wd_rows%d" % nb, [P, T], F32, WD[nb])
+            nc.sync.dma_start(rows[:], wdT[nb * P : (nb + 1) * P, :])
+            wd_rows.append(rows)
 
-        identity = keep.tile([P, P], F32, name="identity")
-        make_identity(nc, identity[:])
+        half = kept("half", [P, 1], F32)
+        nc.vector.memset(half[:], 0.25)
+        nc.scalar.activation(half[:], half[:], ACT.Sqrt)
+        identity_f32 = kept("identity_f32", [P, P], F32)
+        make_identity(nc, identity_f32[:])
+        identity_bf = kept("identity_bf", [P, P], BF16)
+        make_identity(nc, identity_bf[:])
 
-        def gather_scales(name, rows):
-            picked = keep.tile([P, S], U8, name=name, align_bytes=64)
+        def gather_scales(name, rows, picked):
             nc.vector.tensor_copy(picked[:], rows[:].indirect(offsets[:]))
             return picked
 
-        def gather_words(picked, name, words, a, place, pieces):
-            width = S // pieces
-            for piece in range(pieces):
-                part = place(piece, [P, width], "%s%d%d" % (name, a, piece))
-                cols = width // LIST_GROUP
-                nc.vector.tensor_copy(part[:], words[:].bitcast(U32).indirect(offsets[:, piece * cols : (piece + 1) * cols]))
-                for jp in range(J_PASSES):
-                    start = jp * PASS - piece * width
-                    if 0 <= start < width:
-                        picked[a, jp] = part[:, start : start + PASS]
+        def deal_scales(name, picked):
+            planes = kept(name, [P, S], U8)
+            nc.vector.tensor_copy(
+                planes[:].bitcast(I32).rearrange("p (h t b w) -> p h t b w", h=J_PASSES, t=PACK, b=BLOCKS),
+                picked[:].bitcast(I32).rearrange("p (h b t w) -> p h t b w", h=J_PASSES, t=PACK, b=BLOCKS),
+            )
+            return planes
 
-        def on_region(region):
-            return lambda piece, shape, name: region_tile(region, 4 * shape[1] * piece, shape, U32, name)
+        def gather_words(picked, words, jp):
+            nc.vector.tensor_copy(
+                picked[:].rearrange("p (t b r) -> p b t r", t=PACK, r=RUN),
+                words[:].bitcast(U32).indirect(list_part(jp)),
+            )
+            return picked
 
-        def fresh(piece, shape, name):
-            return keep.tile(shape, U32, name=name, align_bytes=64)
-
-        def quantise(name, values, width, place=fresh):
-            codes = place(0, [P, width], name + "_codes")
-            plane = keep.tile([P, width], U8, name=name + "_plane", align_bytes=64)
+        def quantise(name, values, codes):
+            plane = kept(name + "_plane", list(codes.shape), U8)
             nc.vector.quantize_mx(out=codes[:].bitcast(FP8X4), scales=plane[:], in_=values)
             return codes, plane
 
-        even_planes = gather_scales("even_planes", even_scale_rows)
-        even_picked, odd_picked = {}, {}
-        gather_words(even_picked, "even_picked", even_words[0], 0, fresh, 1)
-        odd_planes = gather_scales("odd_planes", odd_scale_rows)
-
-        x_mx = []
-        for a in range(K_PASSES):
-            x_bf = region_tile(X_LAST, 2 * M * PACK * (K_PASSES - 1 - a), [P, M * PACK], BF16, "x_bf%d" % a)
+        def quantise_x(a, codes):
+            x_bf = placed("x_bf%d" % a, [P, M * PACK], BF16, X_BF, 2 * M * PACK * a)
             nc.scalar.copy(
                 x_bf[:].rearrange("p (c e i) -> p c i e", e=4, i=PACK),
                 x_raw[a][:].rearrange("p i (c e) -> p c i e", e=4),
             )
-            x_mx.append(quantise("x%d" % a, x_bf[:], M, fresh if a else lambda piece, shape, name: region_tile(SCALES, T, shape, U32, name)))
+            return quantise("x%d" % a, x_bf[:], codes)
 
-        gather_words(even_picked, "even_picked", even_words[1], 1, on_region(X_LAST), 1)
+        words_shape = [P, PASS]
+        words_size = 4 * PASS
+        even_picked, odd_picked = {}, {}
+        for jp in range(J_PASSES):
+            even_picked[0, jp] = gather_words(kept("even_picked0%d" % jp, words_shape, U32), even_words[0], jp)
+        even_scales = gather_scales("even", even_scale_rows, placed("even_scales", [P, S], U8, EVEN[0]))
+        even_planes = deal_scales("even_planes", even_scales)
+        x_mx = [quantise_x(0, placed("x_codes0", [P, M], U32, SCALES, T))]
+        odd_scales = gather_scales("odd", odd_scale_rows, placed("odd_scales", [P, S], U8, X_BF))
+        x_mx.append(quantise_x(1, placed("x_codes1", [P, M], U32, SCALES)))
+        odd_planes = deal_scales("odd_planes", odd_scales)
+        for jp in range(J_PASSES):
+            tile_jp = placed("even_picked1%d" % jp, words_shape, U32, X_BF, 2 * M * PACK + words_size * jp)
+            even_picked[1, jp] = gather_words(tile_jp, even_words[1], jp)
 
-        def squared_response(role, picked, planes, mb, jp, squares):
-            bank = bank_tile(role, [P, PASS])
-            m_cols = slice(mb * P, (mb + 1) * P)
+        slots = J_PASSES * PACK
+        gains_turned = bank_tile("gains_turned", [P, P], F32, 6)
+        nc.tensor.transpose(gains_turned[:], gain_rows[:], identity_f32[:])
+        gains = placed("gains", [P, slots], F32, X_RAW[1])
+        nc.scalar.copy(gains[:], gains_turned[:, :slots])
+        raw_signs = kept("raw_signs", [P, slots], F32)
+        nc.scalar.activation(raw_signs[:], gains[:], ACT.Sign)
+        signs = kept("signs", [P, slots], BF16)
+        nc.scalar.activation(signs[:], raw_signs[:], ACT.Sign, bias=half[:])
+        signs_spread = bank_tile("signs_spread", [P, slots, P], BF16, 7)
+        for slot in range(slots):
+            nc.tensor.transpose(signs_spread[:, slot, :], signs[:, slot : slot + 1].to_broadcast([P, P]), identity_bf[:])
+        sign_rows = kept("sign_rows", [P, slots * P], BF16)
+        nc.scalar.copy(sign_rows[:], signs_spread[:].rearrange("p s c -> p (s c)"))
+
+        def respond(out_ap, picked, planes, jp, t, m_cols):
             for a in range(K_PASSES):
                 x_codes, x_plane = x_mx[a]
                 nc.tensor.matmul_mx(
-                    out=bank[:],
-                    lhsT=x_codes[:, m_cols].bitcast(FP8X4),
-                    lhsT_scale=x_plane[:, m_cols],
-                    rhs=picked[a, jp].bitcast(FP8X4),
-                    rhs_scale=planes[SCALE_ROWS * a :, jp * PASS : (jp + 1) * PASS],
+                    out=out_ap,
+                    lhsT=picked[a, jp][:, t * P : (t + 1) * P].bitcast(FP8X4),
+                    lhsT_scale=planes[SCALE_ROWS * a :, jp * PASS + t * P : jp * PASS + (t + 1) * P],
+                    rhs=x_codes[:, m_cols].bitcast(FP8X4),
+                    rhs_scale=x_plane[:, m_cols],
                     start=(a == 0),
                     stop=(a == K_PASSES - 1),
                 )
-            nc.scalar.activation(squares[:], bank[:].rearrange("p (q t) -> p t q", t=PACK), ACT.Square)
 
-        units = [(mb, jp) for mb in range(M_BLOCKS) for jp in range(J_PASSES)]
-        even_squares = {}
-        for mb, jp in units:
-            squares = keep.tile([P, PACK, P], F32, name="even_squares%d%d" % (mb, jp))
-            squared_response("even", even_picked, even_planes, mb, jp, squares)
-            even_squares[mb, jp] = squares
+        def square(out_ap, response, jp, t):
+            slot = jp * PACK + t
+            nc.scalar.activation(out_ap, response, ACT.Square, scale=gains[:, slot : slot + 1])
 
-        gather_words(odd_picked, "odd_picked", odd_words[0], 0, on_region(EVEN[1]), 1)
-        gather_words(odd_picked, "odd_picked", odd_words[1], 1, on_region(ODD[0]), J_PASSES)
+        even_squares = []
+        for jp in range(J_PASSES):
+            squares = kept("even_squares%d" % jp, [P, PACK, M], F32)
+            for t in range(PACK):
+                bank = bank_tile("even%d%d" % (jp, t), [P, M], F32, jp * PACK + t)
+                respond(bank[:], even_picked, even_planes, jp, t, slice(0, M))
+                square(squares[:, t, :], bank[:], jp, t)
+            even_squares.append(squares)
 
-        def odd_part(mb, jp):
-            squares = ring.tile([P, PACK, P], F32, name="odd_squares")
-            squared_response("odd", odd_picked, odd_planes, mb, jp, squares)
+        for jp in range(J_PASSES):
+            tile_jp = placed("odd_picked0%d" % jp, words_shape, U32, EVEN[1], words_size * jp)
+            odd_picked[0, jp] = gather_words(tile_jp, odd_words[0], jp)
+        odd_picked[1, 0] = gather_words(placed("odd_picked10", words_shape, U32, ODD[0]), odd_words[1], 0)
+        odd_picked[1, 1] = gather_words(
+            placed("odd_picked11", words_shape, U32, X_BF, 2 * M * PACK + words_size), odd_words[1], 1
+        )
+
+        groups = [(mh, jp) for mh in range(2) for jp in range(J_PASSES)]
+        squares_size = 4 * PACK * HALF
+
+        def odd_group(index):
+            mh, jp = groups[index]
+            squares = placed("odd_squares%d" % index, [P, PACK, HALF], F32, SQUARES, squares_size * index)
+            for pair, bank_index in enumerate(ODD_BANKS[index]):
+                bank = bank_tile("odd%d%d" % (index, pair), [P, 2, HALF], F32, bank_index)
+                for e in range(2):
+                    respond(bank[:, e, :], odd_picked, odd_planes, jp, 2 * pair + e, slice(mh * HALF, (mh + 1) * HALF))
+                for e in range(2):
+                    square(squares[:, 2 * pair + e, :], bank[:, e, :], jp, 2 * pair + e)
             return squares
 
-        def amplitude(mb, jp, odd_squares):
-            energy = bank_tile("energy", [P, PACK, P])
-            for t in range(PACK):
-                nc.tensor.matmul(energy[:, t, :], even_squares[mb, jp][:, t, :], identity[:], start=True, stop=False, is_transpose=True)
-                nc.tensor.matmul(energy[:, t, :], odd_squares[:, t, :], identity[:], start=False, stop=True, is_transpose=True)
-            root = keep.tile([P, P, PACK], F32, name="root%d%d" % (mb, jp))
-            nc.scalar.activation(root[:], energy[:].rearrange("p t m -> p m t"), ACT.Sqrt)
-            return root
-
-        def gained(mb, jp, root, h_unit):
-            nc.vector.tensor_tensor(h_unit.rearrange("p (m t) -> p m t", t=PACK), root[:], gains[:, jp, :].unsqueeze(1).to_broadcast([P, P, PACK]), MULT)
-
-        def pooling_weights(nb):
-            picked = region_tile(((ODD[1],) + WD)[nb], 0, [P, S], BF16, "wd_picked%d" % nb)
-            nc.vector.tensor_copy(picked[:], wd_rows[nb][:].indirect(offsets[:]))
-            pairs = picked[:].bitcast(F32)
-            turned = bank_tile("energy", [P, J_PASSES, 2, P])
-            for jp in range(J_PASSES):
-                for u in range(2):
-                    nc.tensor.transpose(turned[:, jp, u, :], pairs[:, 2 * P * jp + u : 2 * P * (jp + 1) : 2], identity[:])
-            wd_bf = keep.tile([P, J_PASSES * P * PACK], BF16, name="wd_bf%d" % nb, align_bytes=64)
-            nc.scalar.copy(
-                wd_bf[:].bitcast(F32).rearrange("p (h n u) -> p h n u", h=J_PASSES, u=2),
-                turned[:].rearrange("p h u n -> p h n u"),
+        def energy(mb, jp, odd_squares, total):
+            part = mb % 2
+            nc.vector.tensor_tensor(
+                total[:],
+                even_squares[jp][:, :, mb * P : (mb + 1) * P],
+                odd_squares[:, :, part * P : (part + 1) * P],
+                ADD,
             )
-            return quantise("wd%d" % nb, wd_bf[:], J_PASSES * P)
+            return total
+
+        def amplitude(mb, jp, total, codes):
+            h_bf = kept("h_bf%d%d" % (mb, jp), [P, P * PACK], BF16)
+            nc.scalar.activation(
+                h_bf[:].rearrange("p (c e t) -> p c t e", e=4, t=PACK),
+                total[:].rearrange("p t (c e) -> p c t e", e=4),
+                ACT.Sqrt,
+            )
+            return quantise("h%d%d" % (mb, jp), h_bf[:], codes)
+
+        def pooling_weights(nb, region, start, codes_tile):
+            picked = []
+            for jp in range(J_PASSES):
+                part = placed("wd_picked%d%d" % (nb, jp), [P, PASS], BF16, region, start + 2 * PASS * jp)
+                nc.vector.tensor_copy(part[:], wd_rows[nb][:].indirect(list_part(jp)))
+                picked.append(part)
+            for jp in range(J_PASSES):
+                name = "%d%d" % (nb, jp)
+                signed = kept("wd_signed" + name, [P, PACK, P], BF16)
+                nc.vector.tensor_tensor(
+                    signed[:].rearrange("p t (b r) -> p t b r", r=RUN),
+                    picked[jp][:].rearrange("p (b t r) -> p t b r", t=PACK, r=RUN),
+                    sign_rows[:, jp * PASS : (jp + 1) * PASS].rearrange("p (t b r) -> p t b r", t=PACK, r=RUN),
+                    MULT,
+                )
+                turned = bank_tile("turned" + name, [P, PACK, P], BF16, TURN_BANKS[nb][jp])
+                for t in range(PACK):
+                    nc.tensor.transpose(turned[:, t, :], signed[:, t, :], identity_bf[:])
+                wd_bf = kept("wd_bf" + name, [P, P * PACK], BF16)
+                nc.scalar.copy(wd_bf[:].rearrange("p (n t) -> p n t", t=PACK), turned[:].rearrange("p t n -> p n t"))
+                wd_mx[nb, jp] = quantise("wd" + name, wd_bf[:], codes_tile("wd_codes" + name, jp))
 
         def pool_block(mb):
             m_cols = slice(mb * P, (mb + 1) * P)
-            sums = bank_tile("sums", [P, N_BLOCKS, P])
+            sums = bank_tile("sums%d" % mb, [P, N_BLOCKS, P], F32, SUM_BANKS[mb])
             for a in range(K_PASSES):
                 x_codes, x_plane = x_mx[a]
                 for nb in range(N_BLOCKS):
@@ -228,37 +291,55 @@ def tile_list_motion_energy_pool_kernel(
             for jp in range(J_PASSES):
                 h_codes, h_plane = h_mx[mb, jp]
                 for nb in range(N_BLOCKS):
-                    wd_codes, wd_plane = wd_mx[nb]
+                    wd_codes, wd_plane = wd_mx[nb, jp]
                     nc.tensor.matmul_mx(
                         out=sums[:, nb, :],
-                        lhsT=wd_codes[:, jp * P : (jp + 1) * P].bitcast(FP8X4),
-                        lhsT_scale=wd_plane[:, jp * P : (jp + 1) * P],
+                        lhsT=wd_codes[:].bitcast(FP8X4),
+                        lhsT_scale=wd_plane[:],
                         rhs=h_codes[:].bitcast(FP8X4),
                         rhs_scale=h_plane[:],
                         start=False,
                         stop=(jp == J_PASSES - 1 and nb == N_BLOCKS - 1),
                     )
-            result = ring.tile([P, N_BLOCKS, P], F32, name="result")
-            nc.scalar.copy(result[:], sums[:])
+            result = kept("result%d" % mb, [P, N_BLOCKS, P], F32)
+            if mb % 2:
+                nc.scalar.copy(result[:], sums[:])
+            else:
+                nc.vector.tensor_copy(result[:], sums[:])
             nc.sync.dma_start(out.rearrange("(b p) m -> p b m", p=P)[:, :, m_cols], result[:])
 
-        odd_squares, roots, wd_mx = {}, {}, []
-        for step in range(len(units) + 2):
-            if step < len(units):
-                odd_squares[step] = odd_part(*units[step])
-            if step >= 2:
-                roots[step - 2] = amplitude(*units[step - 2], odd_squares[step - 2])
-            if step in (4, 6, 7):
-                wd_mx.append(pooling_weights(len(wd_mx)))
+        h_mx, wd_mx = {}, {}
+        codes_size = 4 * P
 
-        h_bf = {}
-        h_mx = {}
-        for step in range(len(units) + 1):
-            if step < len(units):
-                h_bf[step] = region_tile(WD[2], 2 * PASS * step, [P, PASS], BF16, "h_bf%d" % step)
-                gained(*units[step], roots[step], h_bf[step][:])
-            if step >= 1:
-                mb, jp = units[step - 1]
-                h_mx[mb, jp] = quantise("h%d%d" % (mb, jp), h_bf[step - 1][:], P)
-                if jp == J_PASSES - 1:
-                    pool_block(mb)
+        def codes_kept(name, index):
+            return kept(name, [P, P], U32)
+
+        def codes_on(region, first):
+            return lambda name, index: placed(name, [P, P], U32, region, codes_size * (first + index))
+
+        def energy_kept(name, index):
+            return kept(name, [P, PACK, P], F32)
+
+        def energy_after_last_gather(name, index):
+            return placed(name, [P, PACK, P], F32, WD[2], REGION_BYTES // 2 + 4 * PASS * index)
+
+        def finish_group(index, energy_tile, codes_tile):
+            mh, jp = groups[index]
+            blocks = (2 * mh, 2 * mh + 1)
+            totals = [
+                energy(mb, jp, odd_squares[index], energy_tile("energy%d%d" % (mb, jp), part))
+                for part, mb in enumerate(blocks)
+            ]
+            for part, mb in enumerate(blocks):
+                h_mx[mb, jp] = amplitude(mb, jp, totals[part], codes_tile("h_codes%d%d" % (mb, jp), part))
+
+        odd_squares = [odd_group(index) for index in range(len(groups))]
+        pooling_weights(0, ODD[1], 0, codes_on(WD[1], 0))
+        finish_group(0, energy_kept, codes_on(WD[1], 2))
+        pooling_weights(1, SQUARES, 0, codes_on(WD[2], 0))
+        finish_group(1, energy_kept, codes_on(WD[2], 2))
+        finish_group(2, energy_kept, codes_on(WD[2], 4))
+        pooling_weights(2, SQUARES, 2 * squares_size, codes_kept)
+        finish_group(3, energy_after_last_gather, codes_kept)
+        for mb in range(M_BLOCKS):
+            pool_block(mb)

@@ -16,7 +16,6 @@ FP8X4 = mybir.dt.float8_e4m3fn_x4
 FP4X4 = mybir.dt.float4_e2m1fn_x4
 ACT = mybir.ActivationFunctionType
 MULT = mybir.AluOpType.mult
-ADD = mybir.AluOpType.add
 
 P = 128
 PACK = 4
@@ -29,17 +28,18 @@ QUADRANTS = 4
 QUADRANT = P // QUADRANTS
 SCALE_ROWS = 4
 LIST_GROUP = 16
-RUN = 8
-BLOCKS = PASS // (PACK * RUN)
-HALF = M // 2
 BANK_BYTES = 2048
-ODD_BANKS = ((0, 1), (2, 3), (4, 5), (0, 1))
-TURN_BANKS = ((4, 5), (0, 1), (4, 5))
-SUM_BANKS = (6, 7, 2, 3)
+BANKS = {
+    "even": (0, 1, 2, 3, 4, 5, 6, 7),
+    "odd": (5, 6, 7),
+    "energy": (0, 1, 2, 3, 4),
+    "turned": (3, 4),
+    "sums": (4, 3, 7, 5),
+}
+EARLY_UNITS = len(BANKS["energy"])
 REGION_BYTES = 4 * T
 EVEN, ODD, WD = (0, 1), (2, 3), (4, 5, 6)
-X_RAW = (7, 8)
-X_BF, SCALES, SQUARES = 9, 10, 11
+X_BF, SCALES = 7, 8
 
 
 def tile_list_motion_energy_pool_kernel(
@@ -48,24 +48,29 @@ def tile_list_motion_energy_pool_kernel(
     nc = tc.nc
     with ExitStack() as ctx:
         keep = ctx.enter_context(tc.tile_pool(name="keep", bufs=1))
+        ring = ctx.enter_context(tc.tile_pool(name="ring", bufs=4))
         reuse = ctx.enter_context(tc.tile_pool(name="reuse", bufs=1))
         psum = ctx.enter_context(tc.psum_pool(name="psum", bufs=1))
 
-        def kept(name, shape, dtype):
-            return keep.tile(shape, dtype, name=name, align_bytes=64)
+        def region_tile(region, part, shape, dtype, name):
+            return reuse.tile(shape, dtype, name=name, align_bytes=64, offset=region * REGION_BYTES + part)
 
-        def placed(name, shape, dtype, region, start=0):
-            return reuse.tile(shape, dtype, name=name, align_bytes=64, offset=region * REGION_BYTES + start)
+        turns = {role: 0 for role in BANKS}
 
-        def bank_tile(name, shape, dtype, bank):
-            return psum.tile(shape, dtype, name=name, offset=bank * BANK_BYTES)
+        def bank_tile(role, shape):
+            banks = BANKS[role]
+            turn = turns[role]
+            turns[role] = turn + 1
+            return psum.tile(shape, F32, name="%s%d" % (role, turn), offset=banks[turn % len(banks)] * BANK_BYTES)
 
-        def list_part(jp):
-            cols = PASS // LIST_GROUP
-            return offsets[:, jp * cols : (jp + 1) * cols]
+        offsets = keep.tile([P, S // LIST_GROUP], U16, name="offsets")
+        nc.sync.dma_start(offsets[:], offs)
+        gains = keep.tile([P, J_PASSES, PACK], F32, name="gains")
+        nc.sync.dma_start(gains[:], g.rearrange("(h p t) -> p h t", p=P, t=PACK))
 
-        def load_table_scales(rows, scales):
-            nc.vector.memset(rows[:].bitcast(I32), 0)
+        def load_table_scales(name, scales, part, clearing_engine):
+            rows = region_tile(SCALES, part * T, [P, T], U8, name)
+            clearing_engine.memset(rows[:].bitcast(I32), 0)
             for q in range(QUADRANTS):
                 nc.sync.dma_start(
                     rows[QUADRANT * q : QUADRANT * q + K_PASSES * SCALE_ROWS, :].bitcast(I32),
@@ -73,209 +78,166 @@ def tile_list_motion_energy_pool_kernel(
                 )
             return rows
 
-        def load_table_words(name, words, a, region):
-            tile_a = placed("%s%d" % (name, a), [P, T], I32, region)
+        def load_table_words(name, words, a, regions):
+            tile_a = region_tile(regions[a], 0, [P, T], I32, "%s%d" % (name, a))
             nc.sync.dma_start(tile_a[:], words[a].rearrange("p t i -> p (t i)").bitcast(I32))
             return tile_a
 
         def load_x(a):
-            raw = placed("x_raw%d" % a, [P, PACK, M], F32, X_RAW[a])
+            raw = keep.tile([P, PACK, M], F32, name="x_raw%d" % a)
             nc.sync.dma_start(raw[:], x[a * PASS : (a + 1) * PASS, :].rearrange("(p i) m -> p i m", i=PACK))
             return raw
 
-        offsets = keep.tile([P, S // LIST_GROUP], U16, name="offsets")
-        nc.sync.dma_start(offsets[:], offs)
-        even_words = [load_table_words("even_words", tab_words, 0, EVEN[0])]
-        even_scale_rows = load_table_scales(placed("even_scale_rows", [P, T], U8, SCALES, T), tab_scales)
+        even_scale_rows = load_table_scales("even_scale_rows", tab_scales, 0, nc.vector)
+        even_words = [load_table_words("even_words", tab_words, 0, EVEN)]
         x_raw = [load_x(0)]
-        gain_rows = kept("gain_rows", [P, P], F32)
-        nc.gpsimd.memset(gain_rows[:], 0.0)
-        for jp in range(J_PASSES):
-            nc.sync.dma_start(
-                gain_rows[PACK * jp : PACK * (jp + 1), :].rearrange("t (b r) -> t b r", r=RUN),
-                g[jp * PASS : (jp + 1) * PASS].rearrange("(b t r) -> t b r", t=PACK, r=RUN),
-            )
-        odd_scale_rows = load_table_scales(placed("odd_scale_rows", [P, T], U8, SCALES), tab2_scales)
+        odd_scale_rows = load_table_scales("odd_scale_rows", tab2_scales, 1, nc.vector)
         x_raw.append(load_x(1))
-        even_words.append(load_table_words("even_words", tab_words, 1, EVEN[1]))
-        odd_words = [load_table_words("odd_words", tab2_words, a, ODD[a]) for a in range(K_PASSES)]
-        ws_codes = kept("ws_codes", [P, K_PASSES, 2 * N], U8)
+        even_words.append(load_table_words("even_words", tab_words, 1, EVEN))
+        odd_words = [load_table_words("odd_words", tab2_words, a, ODD) for a in range(K_PASSES)]
+
+        wd_rows = []
+        for nb in range(N_BLOCKS):
+            rows = region_tile(WD[nb], 0, [P, T], F32, "wd_rows%d" % nb)
+            nc.sync.dma_start(rows[:], wdT[nb * P : (nb + 1) * P, :])
+            wd_rows.append(rows)
+
+        ws_codes = keep.tile([P, K_PASSES, 2 * N], U8, name="ws_codes", align_bytes=64)
         nc.sync.dma_start(ws_codes[:].bitcast(I32), ws_words.rearrange("a p c -> p a c").bitcast(I32))
-        ws_planes = kept("ws_planes", [P, K_PASSES, N], U8)
-        nc.gpsimd.memset(ws_planes[:].bitcast(I32), 0)
+        ws_planes = keep.tile([P, K_PASSES, N], U8, name="ws_planes", align_bytes=64)
+        nc.vector.memset(ws_planes[:].bitcast(I32), 0)
         for q in range(QUADRANTS):
             nc.sync.dma_start(
                 ws_planes[QUADRANT * q : QUADRANT * q + SCALE_ROWS, :, :].bitcast(I32),
                 ws_scales[:, SCALE_ROWS * q : SCALE_ROWS * (q + 1), :].rearrange("a r c -> r a c").bitcast(I32),
             )
-        wd_rows = []
-        for nb in range(N_BLOCKS):
-            rows = placed("wd_rows%d" % nb, [P, T], F32, WD[nb])
-            nc.sync.dma_start(rows[:], wdT[nb * P : (nb + 1) * P, :])
-            wd_rows.append(rows)
 
-        half = kept("half", [P, 1], F32)
-        nc.vector.memset(half[:], 0.25)
-        nc.scalar.activation(half[:], half[:], ACT.Sqrt)
-        identity_f32 = kept("identity_f32", [P, P], F32)
-        make_identity(nc, identity_f32[:])
-        identity_bf = kept("identity_bf", [P, P], BF16)
-        make_identity(nc, identity_bf[:])
+        warm = keep.tile([P, 1], F32, name="warm")
+        nc.vector.memset(warm[:], 1.0)
+        nc.scalar.activation(warm[:], warm[:], ACT.Sqrt)
+
+        identity = keep.tile([P, P], F32, name="identity")
+        make_identity(nc, identity[:])
 
         def gather_scales(name, rows, picked):
             nc.vector.tensor_copy(picked[:], rows[:].indirect(offsets[:]))
             return picked
 
-        def deal_scales(name, picked):
-            planes = kept(name, [P, S], U8)
-            nc.vector.tensor_copy(
-                planes[:].bitcast(I32).rearrange("p (h t b w) -> p h t b w", h=J_PASSES, t=PACK, b=BLOCKS),
-                picked[:].bitcast(I32).rearrange("p (h b t w) -> p h t b w", h=J_PASSES, t=PACK, b=BLOCKS),
-            )
-            return planes
+        def gather_words(picked, name, words, a, place, pieces):
+            width = S // pieces
+            for piece in range(pieces):
+                part = place(piece, [P, width], "%s%d%d" % (name, a, piece))
+                cols = width // LIST_GROUP
+                nc.vector.tensor_copy(part[:], words[:].bitcast(U32).indirect(offsets[:, piece * cols : (piece + 1) * cols]))
+                for jp in range(J_PASSES):
+                    start = jp * PASS - piece * width
+                    if 0 <= start < width:
+                        picked[a, jp] = part[:, start : start + PASS]
 
-        def gather_words(picked, words, jp):
-            nc.vector.tensor_copy(
-                picked[:].rearrange("p (t b r) -> p b t r", t=PACK, r=RUN),
-                words[:].bitcast(U32).indirect(list_part(jp)),
-            )
-            return picked
+        def on_region(region):
+            return lambda piece, shape, name: region_tile(region, 4 * shape[1] * piece, shape, U32, name)
 
-        def quantise(name, values, codes):
-            plane = kept(name + "_plane", list(codes.shape), U8)
+        def fresh(piece, shape, name):
+            return keep.tile(shape, U32, name=name, align_bytes=64)
+
+        def quantise(name, values, width, place=fresh):
+            codes = place(0, [P, width], name + "_codes")
+            plane = keep.tile([P, width], U8, name=name + "_plane", align_bytes=64)
             nc.vector.quantize_mx(out=codes[:].bitcast(FP8X4), scales=plane[:], in_=values)
             return codes, plane
 
-        def quantise_x(a, codes):
-            x_bf = placed("x_bf%d" % a, [P, M * PACK], BF16, X_BF, 2 * M * PACK * a)
+        def quantise_x(a):
+            x_bf = region_tile(X_BF, 2 * M * PACK * a, [P, M * PACK], BF16, "x_bf%d" % a)
             nc.scalar.copy(
                 x_bf[:].rearrange("p (c e i) -> p c i e", e=4, i=PACK),
                 x_raw[a][:].rearrange("p i (c e) -> p c i e", e=4),
             )
-            return quantise("x%d" % a, x_bf[:], codes)
+            return quantise("x%d" % a, x_bf[:], M, lambda piece, shape, name: region_tile(*((SCALES, T), (X_BF, 0))[a], shape, U32, name))
 
-        words_shape = [P, PASS]
-        words_size = 4 * PASS
+        def on_x_bf(piece, shape, name):
+            return region_tile(X_BF, 2 * M * PACK + 4 * shape[1] * piece, shape, U32, name)
+
         even_picked, odd_picked = {}, {}
-        for jp in range(J_PASSES):
-            even_picked[0, jp] = gather_words(kept("even_picked0%d" % jp, words_shape, U32), even_words[0], jp)
-        even_scales = gather_scales("even", even_scale_rows, placed("even_scales", [P, S], U8, EVEN[0]))
-        even_planes = deal_scales("even_planes", even_scales)
-        x_mx = [quantise_x(0, placed("x_codes0", [P, M], U32, SCALES, T))]
-        odd_scales = gather_scales("odd", odd_scale_rows, placed("odd_scales", [P, S], U8, X_BF))
-        x_mx.append(quantise_x(1, placed("x_codes1", [P, M], U32, SCALES)))
-        odd_planes = deal_scales("odd_planes", odd_scales)
-        for jp in range(J_PASSES):
-            tile_jp = placed("even_picked1%d" % jp, words_shape, U32, X_BF, 2 * M * PACK + words_size * jp)
-            even_picked[1, jp] = gather_words(tile_jp, even_words[1], jp)
+        even_planes = gather_scales("even_planes", even_scale_rows, keep.tile([P, S], U8, name="even_planes", align_bytes=64))
+        gather_words(even_picked, "even_picked", even_words[0], 0, fresh, 1)
+        odd_planes = gather_scales("odd_planes", odd_scale_rows, region_tile(EVEN[0], 0, [P, S], U8, "odd_planes"))
+        x_mx = [quantise_x(a) for a in range(K_PASSES)]
+        gather_words(even_picked, "even_picked", even_words[1], 1, on_x_bf, J_PASSES)
 
-        slots = J_PASSES * PACK
-        gains_turned = bank_tile("gains_turned", [P, P], F32, 6)
-        nc.tensor.transpose(gains_turned[:], gain_rows[:], identity_f32[:])
-        gains = placed("gains", [P, slots], F32, X_RAW[1])
-        nc.scalar.copy(gains[:], gains_turned[:, :slots])
-        raw_signs = kept("raw_signs", [P, slots], F32)
-        nc.scalar.activation(raw_signs[:], gains[:], ACT.Sign)
-        signs = kept("signs", [P, slots], BF16)
-        nc.scalar.activation(signs[:], raw_signs[:], ACT.Sign, bias=half[:])
-        signs_spread = bank_tile("signs_spread", [P, slots, P], BF16, 7)
-        for slot in range(slots):
-            nc.tensor.transpose(signs_spread[:, slot, :], signs[:, slot : slot + 1].to_broadcast([P, P]), identity_bf[:])
-        sign_rows = kept("sign_rows", [P, slots * P], BF16)
-        nc.scalar.copy(sign_rows[:], signs_spread[:].rearrange("p s c -> p (s c)"))
-
-        def respond(out_ap, picked, planes, jp, t, m_cols):
+        def squared_response(role, picked, planes, mb, jp, squares):
+            bank = bank_tile(role, [P, PASS])
+            m_cols = slice(mb * P, (mb + 1) * P)
             for a in range(K_PASSES):
                 x_codes, x_plane = x_mx[a]
                 nc.tensor.matmul_mx(
-                    out=out_ap,
-                    lhsT=picked[a, jp][:, t * P : (t + 1) * P].bitcast(FP8X4),
-                    lhsT_scale=planes[SCALE_ROWS * a :, jp * PASS + t * P : jp * PASS + (t + 1) * P],
-                    rhs=x_codes[:, m_cols].bitcast(FP8X4),
-                    rhs_scale=x_plane[:, m_cols],
+                    out=bank[:],
+                    lhsT=x_codes[:, m_cols].bitcast(FP8X4),
+                    lhsT_scale=x_plane[:, m_cols],
+                    rhs=picked[a, jp].bitcast(FP8X4),
+                    rhs_scale=planes[SCALE_ROWS * a :, jp * PASS : (jp + 1) * PASS],
                     start=(a == 0),
                     stop=(a == K_PASSES - 1),
                 )
+            nc.scalar.activation(squares[:], bank[:].rearrange("p (q t) -> p t q", t=PACK), ACT.Square)
 
-        def square(out_ap, response, jp, t):
-            slot = jp * PACK + t
-            nc.scalar.activation(out_ap, response, ACT.Square, scale=gains[:, slot : slot + 1])
+        units = [(mb, jp) for jp in range(J_PASSES) for mb in range(M_BLOCKS)]
+        even_squares = {}
+        for mb, jp in units:
+            squares = keep.tile([P, PACK, P], F32, name="even_squares%d%d" % (mb, jp))
+            squared_response("even", even_picked, even_planes, mb, jp, squares)
+            even_squares[mb, jp] = squares
 
-        even_squares = []
-        for jp in range(J_PASSES):
-            squares = kept("even_squares%d" % jp, [P, PACK, M], F32)
-            for t in range(PACK):
-                bank = bank_tile("even%d%d" % (jp, t), [P, M], F32, jp * PACK + t)
-                respond(bank[:], even_picked, even_planes, jp, t, slice(0, M))
-                square(squares[:, t, :], bank[:], jp, t)
-            even_squares.append(squares)
+        gather_words(odd_picked, "odd_picked", odd_words[0], 0, on_region(EVEN[1]), 1)
+        gather_words(odd_picked, "odd_picked", odd_words[1], 1, lambda piece, shape, name: (on_x_bf if piece else on_region(ODD[0]))(piece, shape, name), J_PASSES)
 
-        for jp in range(J_PASSES):
-            tile_jp = placed("odd_picked0%d" % jp, words_shape, U32, EVEN[1], words_size * jp)
-            odd_picked[0, jp] = gather_words(tile_jp, odd_words[0], jp)
-        odd_picked[1, 0] = gather_words(placed("odd_picked10", words_shape, U32, ODD[0]), odd_words[1], 0)
-        odd_picked[1, 1] = gather_words(
-            placed("odd_picked11", words_shape, U32, X_BF, 2 * M * PACK + words_size), odd_words[1], 1
-        )
-
-        groups = [(mh, jp) for mh in range(2) for jp in range(J_PASSES)]
-        squares_size = 4 * PACK * HALF
-
-        def odd_group(index):
-            mh, jp = groups[index]
-            squares = placed("odd_squares%d" % index, [P, PACK, HALF], F32, SQUARES, squares_size * index)
-            for pair, bank_index in enumerate(ODD_BANKS[index]):
-                bank = bank_tile("odd%d%d" % (index, pair), [P, 2, HALF], F32, bank_index)
-                for e in range(2):
-                    respond(bank[:, e, :], odd_picked, odd_planes, jp, 2 * pair + e, slice(mh * HALF, (mh + 1) * HALF))
-                for e in range(2):
-                    square(squares[:, 2 * pair + e, :], bank[:, e, :], jp, 2 * pair + e)
+        def odd_part(mb, jp):
+            squares = ring.tile([P, PACK, P], F32, name="odd_squares")
+            squared_response("odd", odd_picked, odd_planes, mb, jp, squares)
             return squares
 
-        def energy(mb, jp, odd_squares, total):
-            part = mb % 2
-            nc.vector.tensor_tensor(
-                total[:],
-                even_squares[jp][:, :, mb * P : (mb + 1) * P],
-                odd_squares[:, :, part * P : (part + 1) * P],
-                ADD,
-            )
-            return total
-
-        def amplitude(mb, jp, total, codes):
-            h_bf = kept("h_bf%d%d" % (mb, jp), [P, P * PACK], BF16)
-            nc.scalar.activation(
-                h_bf[:].rearrange("p (c e t) -> p c t e", e=4, t=PACK),
-                total[:].rearrange("p t (c e) -> p c t e", e=4),
-                ACT.Sqrt,
-            )
-            return quantise("h%d%d" % (mb, jp), h_bf[:], codes)
-
-        def pooling_weights(nb, region, start, codes_tile):
-            picked = []
-            for jp in range(J_PASSES):
-                part = placed("wd_picked%d%d" % (nb, jp), [P, PASS], BF16, region, start + 2 * PASS * jp)
-                nc.vector.tensor_copy(part[:], wd_rows[nb][:].indirect(list_part(jp)))
-                picked.append(part)
-            for jp in range(J_PASSES):
-                name = "%d%d" % (nb, jp)
-                signed = kept("wd_signed" + name, [P, PACK, P], BF16)
-                nc.vector.tensor_tensor(
-                    signed[:].rearrange("p t (b r) -> p t b r", r=RUN),
-                    picked[jp][:].rearrange("p (b t r) -> p t b r", t=PACK, r=RUN),
-                    sign_rows[:, jp * PASS : (jp + 1) * PASS].rearrange("p (t b r) -> p t b r", t=PACK, r=RUN),
-                    MULT,
+        def turn_squares(energy, squares, first):
+            for t in range(PACK):
+                nc.tensor.matmul(
+                    energy[:, t, :],
+                    squares[:, t, :],
+                    identity[:],
+                    start=(first and t == 0),
+                    stop=(not first and t == PACK - 1),
+                    is_transpose=True,
                 )
-                turned = bank_tile("turned" + name, [P, PACK, P], BF16, TURN_BANKS[nb][jp])
-                for t in range(PACK):
-                    nc.tensor.transpose(turned[:, t, :], signed[:, t, :], identity_bf[:])
-                wd_bf = kept("wd_bf" + name, [P, P * PACK], BF16)
-                nc.scalar.copy(wd_bf[:].rearrange("p (n t) -> p n t", t=PACK), turned[:].rearrange("p t n -> p n t"))
-                wd_mx[nb, jp] = quantise("wd" + name, wd_bf[:], codes_tile("wd_codes" + name, jp))
+
+        def open_energy(mb, jp):
+            energy = bank_tile("energy", [P, PACK, P])
+            turn_squares(energy, even_squares[mb, jp], True)
+            return energy
+
+        def amplitude(mb, jp, energy, odd_squares):
+            turn_squares(energy, odd_squares, False)
+            root = keep.tile([P, P, PACK], F32, name="root%d%d" % (mb, jp))
+            nc.scalar.activation(root[:], energy[:].rearrange("p t m -> p m t"), ACT.Sqrt)
+            return root
+
+        def gained(mb, jp, root, h_unit):
+            nc.vector.tensor_tensor(h_unit.rearrange("p (m t) -> p m t", t=PACK), root[:], gains[:, jp, :].unsqueeze(1).to_broadcast([P, P, PACK]), MULT)
+
+        def pooling_weights(nb):
+            picked = region_tile(((ODD[1],) + WD)[nb], 0, [P, S], BF16, "wd_picked%d" % nb)
+            nc.vector.tensor_copy(picked[:], wd_rows[nb][:].indirect(offsets[:]))
+            pairs = picked[:].bitcast(F32)
+            turned = bank_tile("turned", [P, J_PASSES, 2, P])
+            for jp in range(J_PASSES):
+                for u in range(2):
+                    nc.tensor.transpose(turned[:, jp, u, :], pairs[:, 2 * P * jp + u : 2 * P * (jp + 1) : 2], identity[:])
+            wd_bf = keep.tile([P, J_PASSES * P * PACK], BF16, name="wd_bf%d" % nb, align_bytes=64)
+            nc.scalar.copy(
+                wd_bf[:].bitcast(F32).rearrange("p (h n u) -> p h n u", h=J_PASSES, u=2),
+                turned[:].rearrange("p h u n -> p h n u"),
+            )
+            return quantise("wd%d" % nb, wd_bf[:], J_PASSES * P)
 
         def pool_block(mb):
             m_cols = slice(mb * P, (mb + 1) * P)
-            sums = bank_tile("sums%d" % mb, [P, N_BLOCKS, P], F32, SUM_BANKS[mb])
+            sums = bank_tile("sums", [P, N_BLOCKS, P])
             for a in range(K_PASSES):
                 x_codes, x_plane = x_mx[a]
                 for nb in range(N_BLOCKS):
@@ -291,55 +253,40 @@ def tile_list_motion_energy_pool_kernel(
             for jp in range(J_PASSES):
                 h_codes, h_plane = h_mx[mb, jp]
                 for nb in range(N_BLOCKS):
-                    wd_codes, wd_plane = wd_mx[nb, jp]
+                    wd_codes, wd_plane = wd_mx[nb]
                     nc.tensor.matmul_mx(
                         out=sums[:, nb, :],
-                        lhsT=wd_codes[:].bitcast(FP8X4),
-                        lhsT_scale=wd_plane[:],
+                        lhsT=wd_codes[:, jp * P : (jp + 1) * P].bitcast(FP8X4),
+                        lhsT_scale=wd_plane[:, jp * P : (jp + 1) * P],
                         rhs=h_codes[:].bitcast(FP8X4),
                         rhs_scale=h_plane[:],
                         start=False,
                         stop=(jp == J_PASSES - 1 and nb == N_BLOCKS - 1),
                     )
-            result = kept("result%d" % mb, [P, N_BLOCKS, P], F32)
-            if mb % 2:
-                nc.scalar.copy(result[:], sums[:])
-            else:
-                nc.vector.tensor_copy(result[:], sums[:])
+            result = ring.tile([P, N_BLOCKS, P], F32, name="result")
+            nc.scalar.copy(result[:], sums[:])
             nc.sync.dma_start(out.rearrange("(b p) m -> p b m", p=P)[:, :, m_cols], result[:])
 
-        h_mx, wd_mx = {}, {}
-        codes_size = 4 * P
+        energies = [open_energy(*unit) for unit in units[:EARLY_UNITS]]
+        odd_squares, roots, wd_mx = {}, {}, []
+        for step in range(len(units) + 2):
+            if step < len(units):
+                odd_squares[step] = odd_part(*units[step])
+            if step >= 2:
+                roots[step - 2] = amplitude(*units[step - 2], energies[step - 2], odd_squares[step - 2])
+                if len(energies) < len(units):
+                    energies.append(open_energy(*units[len(energies)]))
+            if step in (5, 6, 7):
+                wd_mx.append(pooling_weights(len(wd_mx)))
 
-        def codes_kept(name, index):
-            return kept(name, [P, P], U32)
-
-        def codes_on(region, first):
-            return lambda name, index: placed(name, [P, P], U32, region, codes_size * (first + index))
-
-        def energy_kept(name, index):
-            return kept(name, [P, PACK, P], F32)
-
-        def energy_after_last_gather(name, index):
-            return placed(name, [P, PACK, P], F32, WD[2], REGION_BYTES // 2 + 4 * PASS * index)
-
-        def finish_group(index, energy_tile, codes_tile):
-            mh, jp = groups[index]
-            blocks = (2 * mh, 2 * mh + 1)
-            totals = [
-                energy(mb, jp, odd_squares[index], energy_tile("energy%d%d" % (mb, jp), part))
-                for part, mb in enumerate(blocks)
-            ]
-            for part, mb in enumerate(blocks):
-                h_mx[mb, jp] = amplitude(mb, jp, totals[part], codes_tile("h_codes%d%d" % (mb, jp), part))
-
-        odd_squares = [odd_group(index) for index in range(len(groups))]
-        pooling_weights(0, ODD[1], 0, codes_on(WD[1], 0))
-        finish_group(0, energy_kept, codes_on(WD[1], 2))
-        pooling_weights(1, SQUARES, 0, codes_on(WD[2], 0))
-        finish_group(1, energy_kept, codes_on(WD[2], 2))
-        finish_group(2, energy_kept, codes_on(WD[2], 4))
-        pooling_weights(2, SQUARES, 2 * squares_size, codes_kept)
-        finish_group(3, energy_after_last_gather, codes_kept)
-        for mb in range(M_BLOCKS):
-            pool_block(mb)
+        h_bf = {}
+        h_mx = {}
+        for step in range(len(units) + 1):
+            if step < len(units):
+                h_bf[step] = region_tile(WD[2], 2 * PASS * step, [P, PASS], BF16, "h_bf%d" % step)
+                gained(*units[step], roots[step], h_bf[step][:])
+            if step >= 1:
+                mb, jp = units[step - 1]
+                h_mx[mb, jp] = quantise("h%d%d" % (mb, jp), h_bf[step - 1][:], P)
+                if jp == J_PASSES - 1:
+                    pool_block(mb)

@@ -16,6 +16,7 @@ FP8X4 = mybir.dt.float8_e4m3fn_x4
 FP4X4 = mybir.dt.float4_e2m1fn_x4
 ACT = mybir.ActivationFunctionType
 MULT = mybir.AluOpType.mult
+ADD = mybir.AluOpType.add
 
 P = 128
 PACK = 4
@@ -28,18 +29,12 @@ QUADRANTS = 4
 QUADRANT = P // QUADRANTS
 SCALE_ROWS = 4
 LIST_GROUP = 16
+LINE = 4
 BANK_BYTES = 2048
-BANKS = {
-    "even": (0, 1, 2, 3, 4, 5, 6, 7),
-    "odd": (5, 6, 7),
-    "energy": (0, 1, 2, 3, 4),
-    "turned": (3, 4),
-    "sums": (4, 3, 7, 5),
-}
-EARLY_UNITS = len(BANKS["energy"])
-REGION_BYTES = 4 * T
-EVEN, ODD, WD = (0, 1), (2, 3), (4, 5, 6)
-X_BF, SCALES = 7, 8
+TURN_BANKS = (5, 6, 7)
+SUM_BANKS = (0, 1, 2, 3)
+REGION = 4 * T
+ODD_LISTED, EVEN_WORDS, X_ROUNDED, WD_ROWS = 0, REGION, 2 * REGION, (3 * REGION, 4 * REGION, 5 * REGION)
 
 
 def tile_list_motion_energy_pool_kernel(
@@ -48,28 +43,24 @@ def tile_list_motion_energy_pool_kernel(
     nc = tc.nc
     with ExitStack() as ctx:
         keep = ctx.enter_context(tc.tile_pool(name="keep", bufs=1))
-        ring = ctx.enter_context(tc.tile_pool(name="ring", bufs=4))
         reuse = ctx.enter_context(tc.tile_pool(name="reuse", bufs=1))
         psum = ctx.enter_context(tc.psum_pool(name="psum", bufs=1))
 
-        def region_tile(region, part, shape, dtype, name):
-            return reuse.tile(shape, dtype, name=name, align_bytes=64, offset=region * REGION_BYTES + part)
+        def sbuf(name, shape, dtype, place=None):
+            if place is None:
+                return keep.tile(shape, dtype, name=name, align_bytes=64)
+            return reuse.tile(shape, dtype, name=name, align_bytes=64, offset=place)
 
-        turns = {role: 0 for role in BANKS}
-
-        def bank_tile(role, shape):
-            banks = BANKS[role]
-            turn = turns[role]
-            turns[role] = turn + 1
-            return psum.tile(shape, F32, name="%s%d" % (role, turn), offset=banks[turn % len(banks)] * BANK_BYTES)
+        def bank(name, index, shape):
+            return psum.tile(shape, F32, name=name, offset=index * BANK_BYTES)
 
         offsets = keep.tile([P, S // LIST_GROUP], U16, name="offsets")
         nc.sync.dma_start(offsets[:], offs)
-        gains = keep.tile([P, J_PASSES, PACK], F32, name="gains")
+        gains = sbuf("gains", [P, J_PASSES, PACK], F32)
         nc.sync.dma_start(gains[:], g.rearrange("(h p t) -> p h t", p=P, t=PACK))
 
-        def load_table_scales(name, scales, part, clearing_engine):
-            rows = region_tile(SCALES, part * T, [P, T], U8, name)
+        def load_table_scales(name, scales, clearing_engine):
+            rows = sbuf(name, [P, T], U8)
             clearing_engine.memset(rows[:].bitcast(I32), 0)
             for q in range(QUADRANTS):
                 nc.sync.dma_start(
@@ -78,166 +69,175 @@ def tile_list_motion_energy_pool_kernel(
                 )
             return rows
 
-        def load_table_words(name, words, a, regions):
-            tile_a = region_tile(regions[a], 0, [P, T], I32, "%s%d" % (name, a))
+        def load_table_words(name, words, a, place=None):
+            tile_a = sbuf("%s%d" % (name, a), [P, T], I32, place)
             nc.sync.dma_start(tile_a[:], words[a].rearrange("p t i -> p (t i)").bitcast(I32))
             return tile_a
 
         def load_x(a):
-            raw = keep.tile([P, PACK, M], F32, name="x_raw%d" % a)
+            raw = sbuf("x_raw%d" % a, [P, PACK, M], F32)
             nc.sync.dma_start(raw[:], x[a * PASS : (a + 1) * PASS, :].rearrange("(p i) m -> p i m", i=PACK))
             return raw
 
-        even_scale_rows = load_table_scales("even_scale_rows", tab_scales, 0, nc.vector)
-        even_words = [load_table_words("even_words", tab_words, 0, EVEN)]
+        even_scale_rows = load_table_scales("even_scale_rows", tab_scales, nc.vector)
         x_raw = [load_x(0)]
-        odd_scale_rows = load_table_scales("odd_scale_rows", tab2_scales, 1, nc.vector)
+        odd_scale_rows = load_table_scales("odd_scale_rows", tab2_scales, nc.gpsimd)
+        even_words = [load_table_words("even_words", tab_words, 0, EVEN_WORDS)]
         x_raw.append(load_x(1))
-        even_words.append(load_table_words("even_words", tab_words, 1, EVEN))
-        odd_words = [load_table_words("odd_words", tab2_words, a, ODD) for a in range(K_PASSES)]
+        even_words.append(load_table_words("even_words", tab_words, 1))
+        odd_words = [load_table_words("odd_words", tab2_words, a) for a in range(K_PASSES)]
 
-        wd_rows = []
-        for nb in range(N_BLOCKS):
-            rows = region_tile(WD[nb], 0, [P, T], F32, "wd_rows%d" % nb)
-            nc.sync.dma_start(rows[:], wdT[nb * P : (nb + 1) * P, :])
-            wd_rows.append(rows)
-
-        ws_codes = keep.tile([P, K_PASSES, 2 * N], U8, name="ws_codes", align_bytes=64)
+        ws_codes = sbuf("ws_codes", [P, K_PASSES, 2 * N], U8)
         nc.sync.dma_start(ws_codes[:].bitcast(I32), ws_words.rearrange("a p c -> p a c").bitcast(I32))
-        ws_planes = keep.tile([P, K_PASSES, N], U8, name="ws_planes", align_bytes=64)
-        nc.vector.memset(ws_planes[:].bitcast(I32), 0)
+        ws_planes = sbuf("ws_planes", [P, K_PASSES, N], U8)
+        nc.gpsimd.memset(ws_planes[:].bitcast(I32), 0)
         for q in range(QUADRANTS):
             nc.sync.dma_start(
                 ws_planes[QUADRANT * q : QUADRANT * q + SCALE_ROWS, :, :].bitcast(I32),
                 ws_scales[:, SCALE_ROWS * q : SCALE_ROWS * (q + 1), :].rearrange("a r c -> r a c").bitcast(I32),
             )
 
-        warm = keep.tile([P, 1], F32, name="warm")
-        nc.vector.memset(warm[:], 1.0)
+        wd_rows = []
+        for nb in range(N_BLOCKS):
+            rows = sbuf("wd_rows%d" % nb, [P, T], F32, WD_ROWS[nb])
+            nc.sync.dma_start(rows[:], wdT[nb * P : (nb + 1) * P, :])
+            wd_rows.append(rows)
+
+        warm = sbuf("warm", [P, 1], F32)
+        nc.gpsimd.memset(warm[:], 1.0)
         nc.scalar.activation(warm[:], warm[:], ACT.Sqrt)
 
-        identity = keep.tile([P, P], F32, name="identity")
+        identity = sbuf("identity", [P, P], F32)
         make_identity(nc, identity[:])
 
-        def gather_scales(name, rows, picked):
-            nc.vector.tensor_copy(picked[:], rows[:].indirect(offsets[:]))
+        def gather_scales(name, rows, place=None):
+            listed = sbuf(name + "_listed", [P, S], U8, place)
+            nc.vector.tensor_copy(listed[:], rows[:].indirect(offsets[:]))
+            dealt = sbuf(name, [P, S], U8)
+            nc.vector.tensor_copy(
+                dealt[:].rearrange("p (h t q) -> p h t q", h=J_PASSES, t=PACK),
+                listed[:].rearrange("p (h q t) -> p h t q", h=J_PASSES, t=PACK),
+            )
+            return dealt
+
+        def gather_words(name, words, places):
+            picked = {}
+            pieces = len(places)
+            halves = J_PASSES // pieces
+            cols = S // pieces // LIST_GROUP
+            for piece in range(pieces):
+                part = sbuf("%s%d" % (name, piece), [P, S // pieces], U32, places[piece])
+                nc.vector.tensor_copy(
+                    part[:].rearrange("p (h t q) -> p h q t", h=halves, t=PACK),
+                    words[:].bitcast(U32).indirect(offsets[:, piece * cols : (piece + 1) * cols]),
+                )
+                for h in range(halves):
+                    picked[piece * halves + h] = part[:, h * PASS : (h + 1) * PASS]
             return picked
 
-        def gather_words(picked, name, words, a, place, pieces):
-            width = S // pieces
-            for piece in range(pieces):
-                part = place(piece, [P, width], "%s%d%d" % (name, a, piece))
-                cols = width // LIST_GROUP
-                nc.vector.tensor_copy(part[:], words[:].bitcast(U32).indirect(offsets[:, piece * cols : (piece + 1) * cols]))
-                for jp in range(J_PASSES):
-                    start = jp * PASS - piece * width
-                    if 0 <= start < width:
-                        picked[a, jp] = part[:, start : start + PASS]
-
-        def on_region(region):
-            return lambda piece, shape, name: region_tile(region, 4 * shape[1] * piece, shape, U32, name)
-
-        def fresh(piece, shape, name):
-            return keep.tile(shape, U32, name=name, align_bytes=64)
-
-        def quantise(name, values, width, place=fresh):
-            codes = place(0, [P, width], name + "_codes")
-            plane = keep.tile([P, width], U8, name=name + "_plane", align_bytes=64)
+        def quantise(name, values, width, place=None):
+            codes = sbuf(name + "_codes", [P, width], U32, place)
+            plane = sbuf(name + "_plane", [P, width], U8)
             nc.vector.quantize_mx(out=codes[:].bitcast(FP8X4), scales=plane[:], in_=values)
             return codes, plane
 
-        def quantise_x(a):
-            x_bf = region_tile(X_BF, 2 * M * PACK * a, [P, M * PACK], BF16, "x_bf%d" % a)
+        def round_x(a):
             nc.scalar.copy(
-                x_bf[:].rearrange("p (c e i) -> p c i e", e=4, i=PACK),
-                x_raw[a][:].rearrange("p i (c e) -> p c i e", e=4),
+                x_bf[a][:].rearrange("p (c e i) -> p c i e", e=LINE, i=PACK),
+                x_raw[a][:].rearrange("p i (c e) -> p c i e", e=LINE),
             )
-            return quantise("x%d" % a, x_bf[:], M, lambda piece, shape, name: region_tile(*((SCALES, T), (X_BF, 0))[a], shape, U32, name))
 
-        def on_x_bf(piece, shape, name):
-            return region_tile(X_BF, 2 * M * PACK + 4 * shape[1] * piece, shape, U32, name)
+        even_planes = gather_scales("even_planes", even_scale_rows)
+        odd_planes = gather_scales("odd_planes", odd_scale_rows, ODD_LISTED)
+        x_bf = [sbuf("x_bf%d" % a, [P, M * PACK], BF16, (None, X_ROUNDED)[a]) for a in range(K_PASSES)]
+        round_x(0)
+        even_picked = [gather_words("even_picked0", even_words[0], (ODD_LISTED,))]
+        x_mx = [quantise("x0", x_bf[0][:], M, EVEN_WORDS)]
+        signs = sbuf("signs", [P, J_PASSES, PACK], BF16)
+        nc.scalar.activation(signs[:], gains[:], ACT.Sign)
+        round_x(1)
+        x_mx.append(quantise("x1", x_bf[1][:], M))
+        even_picked.append(gather_words("even_picked1", even_words[1], (None, X_ROUNDED)))
 
-        even_picked, odd_picked = {}, {}
-        even_planes = gather_scales("even_planes", even_scale_rows, keep.tile([P, S], U8, name="even_planes", align_bytes=64))
-        gather_words(even_picked, "even_picked", even_words[0], 0, fresh, 1)
-        odd_planes = gather_scales("odd_planes", odd_scale_rows, region_tile(EVEN[0], 0, [P, S], U8, "odd_planes"))
-        x_mx = [quantise_x(a) for a in range(K_PASSES)]
-        gather_words(even_picked, "even_picked", even_words[1], 1, on_x_bf, J_PASSES)
+        units = [(jp, t) for jp in range(J_PASSES) for t in range(PACK)]
 
-        def squared_response(role, picked, planes, mb, jp, squares):
-            bank = bank_tile(role, [P, PASS])
+        def response_pass(target, picked, planes, jp, t, a):
+            x_codes, x_plane = x_mx[a]
+            nc.tensor.matmul_mx(
+                out=target[:],
+                lhsT=picked[a][jp][:, t * P : (t + 1) * P].bitcast(FP8X4),
+                lhsT_scale=planes[SCALE_ROWS * a :, jp * PASS + t * P : jp * PASS + (t + 1) * P],
+                rhs=x_codes[:].bitcast(FP8X4),
+                rhs_scale=x_plane[:],
+                start=(a == 0),
+                stop=(a == K_PASSES - 1),
+            )
+
+        def square(squares, response, jp, t):
+            nc.scalar.activation(squares[jp][:, t, :], response[:], ACT.Square, scale=gains[:, jp, t : t + 1])
+
+        even_squares = [sbuf("even_squares%d" % jp, [P, PACK, M], F32) for jp in range(J_PASSES)]
+        odd_squares = [sbuf("odd_squares%d" % jp, [P, PACK, M], F32) for jp in range(J_PASSES)]
+
+        even_banks = [bank("even%d" % u, u, [P, M]) for u in range(len(units))]
+        for u, (jp, t) in enumerate(units[:PACK]):
+            response_pass(even_banks[u], even_picked, even_planes, jp, t, 0)
+        for u, (jp, t) in enumerate(units):
+            response_pass(even_banks[u], even_picked, even_planes, jp, t, 1)
+            square(even_squares, even_banks[u], jp, t)
+            if jp == 0:
+                response_pass(even_banks[u + PACK], even_picked, even_planes, 1, t, 0)
+
+        odd_picked = [gather_words("odd_picked0", odd_words[0], (None,))]
+        odd_banks = [bank("odd%d" % u, u, [P, M]) for u in range(len(units))]
+        for u, (jp, t) in enumerate(units):
+            response_pass(odd_banks[u], odd_picked, odd_planes, jp, t, 0)
+        odd_picked.append(gather_words("odd_picked1", odd_words[1], (None, None)))
+
+        first_energy = sbuf("first_energy", [P, PACK, M], F32)
+
+        def add_slot(engine, t):
+            engine.tensor_tensor(first_energy[:, t, :], even_squares[0][:, t, :], odd_squares[0][:, t, :], ADD)
+
+        def add_block(engine, mb):
+            energy = sbuf("second_energy%d" % mb, [P, PACK, P], F32)
             m_cols = slice(mb * P, (mb + 1) * P)
-            for a in range(K_PASSES):
-                x_codes, x_plane = x_mx[a]
-                nc.tensor.matmul_mx(
-                    out=bank[:],
-                    lhsT=x_codes[:, m_cols].bitcast(FP8X4),
-                    lhsT_scale=x_plane[:, m_cols],
-                    rhs=picked[a, jp].bitcast(FP8X4),
-                    rhs_scale=planes[SCALE_ROWS * a :, jp * PASS : (jp + 1) * PASS],
-                    start=(a == 0),
-                    stop=(a == K_PASSES - 1),
-                )
-            nc.scalar.activation(squares[:], bank[:].rearrange("p (q t) -> p t q", t=PACK), ACT.Square)
-
-        units = [(mb, jp) for jp in range(J_PASSES) for mb in range(M_BLOCKS)]
-        even_squares = {}
-        for mb, jp in units:
-            squares = keep.tile([P, PACK, P], F32, name="even_squares%d%d" % (mb, jp))
-            squared_response("even", even_picked, even_planes, mb, jp, squares)
-            even_squares[mb, jp] = squares
-
-        gather_words(odd_picked, "odd_picked", odd_words[0], 0, on_region(EVEN[1]), 1)
-        gather_words(odd_picked, "odd_picked", odd_words[1], 1, lambda piece, shape, name: (on_x_bf if piece else on_region(ODD[0]))(piece, shape, name), J_PASSES)
-
-        def odd_part(mb, jp):
-            squares = ring.tile([P, PACK, P], F32, name="odd_squares")
-            squared_response("odd", odd_picked, odd_planes, mb, jp, squares)
-            return squares
-
-        def turn_squares(energy, squares, first):
-            for t in range(PACK):
-                nc.tensor.matmul(
-                    energy[:, t, :],
-                    squares[:, t, :],
-                    identity[:],
-                    start=(first and t == 0),
-                    stop=(not first and t == PACK - 1),
-                    is_transpose=True,
-                )
-
-        def open_energy(mb, jp):
-            energy = bank_tile("energy", [P, PACK, P])
-            turn_squares(energy, even_squares[mb, jp], True)
+            engine.tensor_tensor(energy[:], even_squares[1][:, :, m_cols], odd_squares[1][:, :, m_cols], ADD)
             return energy
 
-        def amplitude(mb, jp, energy, odd_squares):
-            turn_squares(energy, odd_squares, False)
-            root = keep.tile([P, P, PACK], F32, name="root%d%d" % (mb, jp))
-            nc.scalar.activation(root[:], energy[:].rearrange("p t m -> p m t"), ACT.Sqrt)
-            return root
+        def amplitude(name, energy, width):
+            h_bf = sbuf(name, [P, PACK * width], BF16)
+            nc.scalar.activation(
+                h_bf[:].rearrange("p (c e t) -> p c t e", e=LINE, t=PACK),
+                energy.rearrange("p t (c e) -> p c t e", e=LINE),
+                ACT.Sqrt,
+            )
+            return h_bf
 
-        def gained(mb, jp, root, h_unit):
-            nc.vector.tensor_tensor(h_unit.rearrange("p (m t) -> p m t", t=PACK), root[:], gains[:, jp, :].unsqueeze(1).to_broadcast([P, P, PACK]), MULT)
-
-        def pooling_weights(nb):
-            picked = region_tile(((ODD[1],) + WD)[nb], 0, [P, S], BF16, "wd_picked%d" % nb)
+        def pick_pooling_weights(nb):
+            picked = sbuf("wd_picked%d" % nb, [P, S], BF16)
             nc.vector.tensor_copy(picked[:], wd_rows[nb][:].indirect(offsets[:]))
             pairs = picked[:].bitcast(F32)
-            turned = bank_tile("turned", [P, J_PASSES, 2, P])
+            turned = bank("turned%d" % nb, TURN_BANKS[nb], [P, J_PASSES, 2, P])
             for jp in range(J_PASSES):
                 for u in range(2):
                     nc.tensor.transpose(turned[:, jp, u, :], pairs[:, 2 * P * jp + u : 2 * P * (jp + 1) : 2], identity[:])
-            wd_bf = keep.tile([P, J_PASSES * P * PACK], BF16, name="wd_bf%d" % nb, align_bytes=64)
-            nc.scalar.copy(
-                wd_bf[:].bitcast(F32).rearrange("p (h n u) -> p h n u", h=J_PASSES, u=2),
-                turned[:].rearrange("p h u n -> p h n u"),
-            )
-            return quantise("wd%d" % nb, wd_bf[:], J_PASSES * P)
+            return turned
 
-        def pool_block(mb):
+        def sign_pooling_weights(nb, turned, place=None):
+            wd_bf = sbuf("wd_bf%d" % nb, [P, J_PASSES * PASS], BF16, place)
+            for jp in range(J_PASSES):
+                nc.vector.tensor_tensor(
+                    wd_bf[:, jp * PASS : (jp + 1) * PASS].rearrange("p (n u e) -> p n u e", u=2, e=2),
+                    turned[:, jp, :, :].bitcast(BF16).rearrange("p u (n e) -> p n u e", e=2),
+                    signs[:, jp, :].rearrange("p (u e) -> p u e", e=2).unsqueeze(1).to_broadcast([P, P, 2, 2]),
+                    MULT,
+                )
+            return wd_bf
+
+        def drive_block(mb):
             m_cols = slice(mb * P, (mb + 1) * P)
-            sums = bank_tile("sums", [P, N_BLOCKS, P])
+            sums = bank("sums%d" % mb, SUM_BANKS[mb], [P, N_BLOCKS, P])
             for a in range(K_PASSES):
                 x_codes, x_plane = x_mx[a]
                 for nb in range(N_BLOCKS):
@@ -250,43 +250,53 @@ def tile_list_motion_energy_pool_kernel(
                         start=(a == 0 and nb == 0),
                         stop=False,
                     )
-            for jp in range(J_PASSES):
-                h_codes, h_plane = h_mx[mb, jp]
-                for nb in range(N_BLOCKS):
-                    wd_codes, wd_plane = wd_mx[nb]
-                    nc.tensor.matmul_mx(
-                        out=sums[:, nb, :],
-                        lhsT=wd_codes[:, jp * P : (jp + 1) * P].bitcast(FP8X4),
-                        lhsT_scale=wd_plane[:, jp * P : (jp + 1) * P],
-                        rhs=h_codes[:].bitcast(FP8X4),
-                        rhs_scale=h_plane[:],
-                        start=False,
-                        stop=(jp == J_PASSES - 1 and nb == N_BLOCKS - 1),
-                    )
-            result = ring.tile([P, N_BLOCKS, P], F32, name="result")
+            return sums
+
+        def pool_pass(sums, mb, jp, nb):
+            h_codes, h_plane = h_mx[mb, jp]
+            wd_codes, wd_plane = wd_mx[nb]
+            nc.tensor.matmul_mx(
+                out=sums[:, nb, :],
+                lhsT=wd_codes[:, jp * P : (jp + 1) * P].bitcast(FP8X4),
+                lhsT_scale=wd_plane[:, jp * P : (jp + 1) * P],
+                rhs=h_codes.bitcast(FP8X4),
+                rhs_scale=h_plane,
+                start=False,
+                stop=(jp == J_PASSES - 1 and nb == N_BLOCKS - 1),
+            )
+
+        def store_block(sums, mb):
+            result = sbuf("result%d" % mb, [P, N_BLOCKS, P], F32)
             nc.scalar.copy(result[:], sums[:])
-            nc.sync.dma_start(out.rearrange("(b p) m -> p b m", p=P)[:, :, m_cols], result[:])
+            nc.sync.dma_start(out.rearrange("(b p) m -> p b m", p=P)[:, :, mb * P : (mb + 1) * P], result[:])
 
-        energies = [open_energy(*unit) for unit in units[:EARLY_UNITS]]
-        odd_squares, roots, wd_mx = {}, {}, []
-        for step in range(len(units) + 2):
-            if step < len(units):
-                odd_squares[step] = odd_part(*units[step])
-            if step >= 2:
-                roots[step - 2] = amplitude(*units[step - 2], energies[step - 2], odd_squares[step - 2])
-                if len(energies) < len(units):
-                    energies.append(open_energy(*units[len(energies)]))
-            if step in (5, 6, 7):
-                wd_mx.append(pooling_weights(len(wd_mx)))
-
-        h_bf = {}
-        h_mx = {}
-        for step in range(len(units) + 1):
-            if step < len(units):
-                h_bf[step] = region_tile(WD[2], 2 * PASS * step, [P, PASS], BF16, "h_bf%d" % step)
-                gained(*units[step], roots[step], h_bf[step][:])
-            if step >= 1:
-                mb, jp = units[step - 1]
-                h_mx[mb, jp] = quantise("h%d%d" % (mb, jp), h_bf[step - 1][:], P)
-                if jp == J_PASSES - 1:
-                    pool_block(mb)
+        wd_mx, h_mx = [], {}
+        for u, (jp, t) in enumerate(units):
+            response_pass(odd_banks[u], odd_picked, odd_planes, jp, t, 1)
+            square(odd_squares, odd_banks[u], jp, t)
+            if jp == 0:
+                add_slot(nc.gpsimd, t)
+        sums = [drive_block(mb) for mb in range(M_BLOCKS)]
+        turned = [pick_pooling_weights(nb) for nb in range(2)]
+        h_first = [amplitude("h_first%d" % half, first_energy[:, :, half * 2 * P : (half + 1) * 2 * P], 2 * P) for half in range(2)]
+        wd_bf = [sign_pooling_weights(0, turned[0], WD_ROWS[1])]
+        turned.append(pick_pooling_weights(2))
+        wd_mx.append(quantise("wd0", wd_bf[0][:], J_PASSES * P, WD_ROWS[2]))
+        wd_bf.append(sign_pooling_weights(1, turned[1], WD_ROWS[1]))
+        wd_mx.append(quantise("wd1", wd_bf[1][:], J_PASSES * P))
+        for half in range(2):
+            codes, plane = quantise("h0%d" % half, h_first[half][:], 2 * P, WD_ROWS[1] + 4 * 2 * P * half)
+            for mb in range(2):
+                h_mx[2 * half + mb, 0] = codes[:, mb * P : (mb + 1) * P], plane[:, mb * P : (mb + 1) * P]
+        wd_bf.append(sign_pooling_weights(2, turned[2], WD_ROWS[0]))
+        h_second = [amplitude("h_second%d" % mb, add_block(nc.gpsimd, mb)[:], P) for mb in range(M_BLOCKS)]
+        wd_mx.append(quantise("wd2", wd_bf[2][:], J_PASSES * P))
+        for nb in range(N_BLOCKS):
+            for mb in range(M_BLOCKS):
+                pool_pass(sums[mb], mb, 0, nb)
+        for mb in range(M_BLOCKS):
+            codes, plane = quantise("h1%d" % mb, h_second[mb][:], P, WD_ROWS[0] + 4 * P * mb)
+            h_mx[mb, 1] = codes[:], plane[:]
+            for nb in range(N_BLOCKS):
+                pool_pass(sums[mb], mb, 1, nb)
+            store_block(sums[mb], mb)

@@ -31,10 +31,15 @@ SCALE_ROWS = 4
 LIST_GROUP = 16
 LINE = 4
 BANK_BYTES = 2048
-TURN_BANKS = (5, 6, 7)
-SUM_BANKS = (0, 1, 2, 3)
+ENERGY_BANKS = (0, 1, 2, 3)
+ODD_BANKS = (4, 5, 6, 7)
+RETURN_BANKS = (4, 5)
+TURN_BANKS = (0, 1, 2)
+SUM_BANKS = (6, 7, 3)
 REGION = 4 * T
-ODD_LISTED, EVEN_WORDS, X_ROUNDED, WD_ROWS = 0, REGION, 2 * REGION, (3 * REGION, 4 * REGION, 5 * REGION)
+ODD_LISTED, EVEN_WORDS, X_ROUNDED, WD_ROWS = 0, REGION, (2 * REGION, 2 * REGION + REGION // 2), (3 * REGION, 4 * REGION, 5 * REGION)
+LAST_SQUARES = 7 * REGION
+BEHIND_WD = WD_ROWS[2] + 64 - 4 * PASS
 
 
 def tile_list_motion_energy_pool_kernel(
@@ -79,9 +84,9 @@ def tile_list_motion_energy_pool_kernel(
             nc.sync.dma_start(raw[:], x[a * PASS : (a + 1) * PASS, :].rearrange("(p i) m -> p i m", i=PACK))
             return raw
 
-        even_scale_rows = load_table_scales("even_scale_rows", tab_scales, nc.vector)
+        even_scale_rows = load_table_scales("even_scale_rows", tab_scales, nc.gpsimd)
         x_raw = [load_x(0)]
-        odd_scale_rows = load_table_scales("odd_scale_rows", tab2_scales, nc.gpsimd)
+        odd_scale_rows = load_table_scales("odd_scale_rows", tab2_scales, nc.vector)
         even_words = [load_table_words("even_words", tab_words, 0, EVEN_WORDS)]
         x_raw.append(load_x(1))
         even_words.append(load_table_words("even_words", tab_words, 1))
@@ -110,15 +115,14 @@ def tile_list_motion_energy_pool_kernel(
         identity = sbuf("identity", [P, P], F32)
         make_identity(nc, identity[:])
 
-        def gather_scales(name, rows, place=None):
-            listed = sbuf(name + "_listed", [P, S], U8, place)
-            nc.vector.tensor_copy(listed[:], rows[:].indirect(offsets[:]))
-            dealt = sbuf(name, [P, S], U8)
+        def gather_scales(name, rows, dealt, first, last, place=None):
+            listed = sbuf(name, [P, (last - first) * PASS], U8, place)
+            cols = PASS // LIST_GROUP
+            nc.vector.tensor_copy(listed[:], rows[:].indirect(offsets[:, first * cols : last * cols]))
             nc.vector.tensor_copy(
-                dealt[:].rearrange("p (h t q) -> p h t q", h=J_PASSES, t=PACK),
-                listed[:].rearrange("p (h q t) -> p h t q", h=J_PASSES, t=PACK),
+                dealt[:, first * PASS : last * PASS].rearrange("p (h t q) -> p h t q", q=P, t=PACK),
+                listed[:].rearrange("p (h q t) -> p h t q", q=P, t=PACK),
             )
-            return dealt
 
         def gather_words(name, words, places):
             picked = {}
@@ -136,8 +140,8 @@ def tile_list_motion_energy_pool_kernel(
             return picked
 
         def quantise(name, values, width, place=None):
-            codes = sbuf(name + "_codes", [P, width], U32, place)
-            plane = sbuf(name + "_plane", [P, width], U8)
+            codes = sbuf(name + "_codes", [P, width], U32)
+            plane = sbuf(name + "_plane", [P, width], U8, place)
             nc.vector.quantize_mx(out=codes[:].bitcast(FP8X4), scales=plane[:], in_=values)
             return codes, plane
 
@@ -147,17 +151,20 @@ def tile_list_motion_energy_pool_kernel(
                 x_raw[a][:].rearrange("p i (c e) -> p c i e", e=LINE),
             )
 
-        even_planes = gather_scales("even_planes", even_scale_rows)
-        odd_planes = gather_scales("odd_planes", odd_scale_rows, ODD_LISTED)
-        x_bf = [sbuf("x_bf%d" % a, [P, M * PACK], BF16, (None, X_ROUNDED)[a]) for a in range(K_PASSES)]
+        even_planes = sbuf("even_planes", [P, S], U8)
+        odd_planes = sbuf("odd_planes", [P, S], U8)
+        gather_scales("even_listed", even_scale_rows, even_planes, 0, J_PASSES)
+        gather_scales("odd_listed0", odd_scale_rows, odd_planes, 0, 1, ODD_LISTED)
+        x_bf = [sbuf("x_bf%d" % a, [P, M * PACK], BF16, X_ROUNDED[a]) for a in range(K_PASSES)]
         round_x(0)
         even_picked = [gather_words("even_picked0", even_words[0], (ODD_LISTED,))]
         x_mx = [quantise("x0", x_bf[0][:], M, EVEN_WORDS)]
+        gather_scales("odd_listed1", odd_scale_rows, odd_planes, 1, 2, X_ROUNDED[0])
         signs = sbuf("signs", [P, J_PASSES, PACK], BF16)
         nc.scalar.activation(signs[:], gains[:], ACT.Sign)
         round_x(1)
         x_mx.append(quantise("x1", x_bf[1][:], M))
-        even_picked.append(gather_words("even_picked1", even_words[1], (None, X_ROUNDED)))
+        even_picked.append(gather_words("even_picked1", even_words[1], X_ROUNDED))
 
         units = [(jp, t) for jp in range(J_PASSES) for t in range(PACK)]
 
@@ -176,52 +183,86 @@ def tile_list_motion_energy_pool_kernel(
         def square(squares, response, jp, t):
             nc.scalar.activation(squares[jp][:, t, :], response[:], ACT.Square, scale=gains[:, jp, t : t + 1])
 
-        even_squares = [sbuf("even_squares%d" % jp, [P, PACK, M], F32) for jp in range(J_PASSES)]
+        even_squares = [sbuf("even_squares%d" % jp, [P, PACK, M], F32, (None, LAST_SQUARES)[jp]) for jp in range(J_PASSES)]
         odd_squares = [sbuf("odd_squares%d" % jp, [P, PACK, M], F32) for jp in range(J_PASSES)]
 
+        def turn_squares(energy, squares, mb, first):
+            for t in range(PACK):
+                nc.tensor.matmul(
+                    energy[:, t, :],
+                    squares[:, t, mb * P : (mb + 1) * P],
+                    identity[:],
+                    start=(first and t == 0),
+                    stop=(not first and t == PACK - 1),
+                    is_transpose=True,
+                )
+
         even_banks = [bank("even%d" % u, u, [P, M]) for u in range(len(units))]
-        for u, (jp, t) in enumerate(units[:PACK]):
+        for u, (jp, t) in enumerate(units):
             response_pass(even_banks[u], even_picked, even_planes, jp, t, 0)
         for u, (jp, t) in enumerate(units):
             response_pass(even_banks[u], even_picked, even_planes, jp, t, 1)
             square(even_squares, even_banks[u], jp, t)
-            if jp == 0:
-                response_pass(even_banks[u + PACK], even_picked, even_planes, 1, t, 0)
+        energies = [bank("energy%d" % mb, ENERGY_BANKS[mb], [P, PACK, P]) for mb in range(M_BLOCKS)]
+        for mb in range(M_BLOCKS):
+            turn_squares(energies[mb], even_squares[0], mb, True)
 
         odd_picked = [gather_words("odd_picked0", odd_words[0], (None,))]
-        odd_banks = [bank("odd%d" % u, u, [P, M]) for u in range(len(units))]
-        for u, (jp, t) in enumerate(units):
-            response_pass(odd_banks[u], odd_picked, odd_planes, jp, t, 0)
         odd_picked.append(gather_words("odd_picked1", odd_words[1], (None, None)))
 
-        first_energy = sbuf("first_energy", [P, PACK, M], F32)
+        def odd_part(u):
+            jp, t = units[u]
+            response = bank("odd%d" % u, ODD_BANKS[t], [P, M])
+            for a in range(K_PASSES):
+                response_pass(response, odd_picked, odd_planes, jp, t, a)
+            square(odd_squares, response, jp, t)
 
-        def add_slot(engine, t):
-            engine.tensor_tensor(first_energy[:, t, :], even_squares[0][:, t, :], odd_squares[0][:, t, :], ADD)
+        h_bf = [sbuf("h_bf%d" % jp, [P, M * PACK], BF16) for jp in range(J_PASSES)]
+
+        def turned_amplitude(mb):
+            roots = sbuf("roots%d" % mb, [P, PASS], BF16)
+            nc.scalar.activation(
+                roots[:].rearrange("p (u q e) -> p u q e", u=2, e=2),
+                energies[mb][:].rearrange("p (u e) q -> p u q e", e=2),
+                ACT.Sqrt,
+            )
+            return roots
+
+        def turn_back(half, roots):
+            returned = bank("returned%d" % half, RETURN_BANKS[half], [P, 2, 2, P])
+            for b in range(2):
+                pairs = roots[2 * half + b][:].bitcast(F32)
+                for u in range(2):
+                    nc.tensor.transpose(returned[:, b, u, :], pairs[:, u * P : (u + 1) * P], identity[:])
+            nc.scalar.copy(
+                h_bf[0][:, half * 2 * PASS : (half + 1) * 2 * PASS].bitcast(F32).rearrange("p (b m u) -> p b m u", b=2, u=2),
+                returned[:].rearrange("p b u m -> p b m u"),
+            )
 
         def add_block(engine, mb):
-            energy = sbuf("second_energy%d" % mb, [P, PACK, P], F32)
+            energy = sbuf("second_energy%d" % mb, [P, PACK, P], F32, BEHIND_WD + 4 * PASS * mb)
             m_cols = slice(mb * P, (mb + 1) * P)
             engine.tensor_tensor(energy[:], even_squares[1][:, :, m_cols], odd_squares[1][:, :, m_cols], ADD)
             return energy
 
-        def amplitude(name, energy, width):
-            h_bf = sbuf(name, [P, PACK * width], BF16)
+        def amplitude(mb, energy):
             nc.scalar.activation(
-                h_bf[:].rearrange("p (c e t) -> p c t e", e=LINE, t=PACK),
-                energy.rearrange("p t (c e) -> p c t e", e=LINE),
+                h_bf[1][:, mb * PASS : (mb + 1) * PASS].rearrange("p (c e t) -> p c t e", e=LINE, t=PACK),
+                energy[:].rearrange("p t (c e) -> p c t e", e=LINE),
                 ACT.Sqrt,
             )
-            return h_bf
 
         def pick_pooling_weights(nb):
             picked = sbuf("wd_picked%d" % nb, [P, S], BF16)
-            nc.vector.tensor_copy(picked[:], wd_rows[nb][:].indirect(offsets[:]))
+            nc.vector.tensor_copy(
+                picked[:].rearrange("p (h u q e) -> p h q u e", h=J_PASSES, u=2, e=2),
+                wd_rows[nb][:].indirect(offsets[:]),
+            )
             pairs = picked[:].bitcast(F32)
             turned = bank("turned%d" % nb, TURN_BANKS[nb], [P, J_PASSES, 2, P])
             for jp in range(J_PASSES):
                 for u in range(2):
-                    nc.tensor.transpose(turned[:, jp, u, :], pairs[:, 2 * P * jp + u : 2 * P * (jp + 1) : 2], identity[:])
+                    nc.tensor.transpose(turned[:, jp, u, :], pairs[:, P * (2 * jp + u) : P * (2 * jp + u + 1)], identity[:])
             return turned
 
         def sign_pooling_weights(nb, turned, place=None):
@@ -235,68 +276,59 @@ def tile_list_motion_energy_pool_kernel(
                 )
             return wd_bf
 
-        def drive_block(mb):
-            m_cols = slice(mb * P, (mb + 1) * P)
-            sums = bank("sums%d" % mb, SUM_BANKS[mb], [P, N_BLOCKS, P])
+        def drive_block(nb):
+            sums = bank("sums%d" % nb, SUM_BANKS[nb], [P, M])
             for a in range(K_PASSES):
                 x_codes, x_plane = x_mx[a]
-                for nb in range(N_BLOCKS):
-                    nc.tensor.matmul_mx(
-                        out=sums[:, nb, :],
-                        lhsT=ws_codes[:, a, 2 * P * nb : 2 * P * (nb + 1)].bitcast(FP4X4),
-                        lhsT_scale=ws_planes[:, a, nb * P : (nb + 1) * P],
-                        rhs=x_codes[:, m_cols].bitcast(FP8X4),
-                        rhs_scale=x_plane[:, m_cols],
-                        start=(a == 0 and nb == 0),
-                        stop=False,
-                    )
+                nc.tensor.matmul_mx(
+                    out=sums[:],
+                    lhsT=ws_codes[:, a, 2 * P * nb : 2 * P * (nb + 1)].bitcast(FP4X4),
+                    lhsT_scale=ws_planes[:, a, nb * P : (nb + 1) * P],
+                    rhs=x_codes[:].bitcast(FP8X4),
+                    rhs_scale=x_plane[:],
+                    start=(a == 0),
+                    stop=False,
+                )
             return sums
 
-        def pool_pass(sums, mb, jp, nb):
-            h_codes, h_plane = h_mx[mb, jp]
+        def pool_block(nb):
             wd_codes, wd_plane = wd_mx[nb]
-            nc.tensor.matmul_mx(
-                out=sums[:, nb, :],
-                lhsT=wd_codes[:, jp * P : (jp + 1) * P].bitcast(FP8X4),
-                lhsT_scale=wd_plane[:, jp * P : (jp + 1) * P],
-                rhs=h_codes.bitcast(FP8X4),
-                rhs_scale=h_plane,
-                start=False,
-                stop=(jp == J_PASSES - 1 and nb == N_BLOCKS - 1),
-            )
+            for jp in range(J_PASSES):
+                h_codes, h_plane = h_mx[jp]
+                nc.tensor.matmul_mx(
+                    out=sums[nb][:],
+                    lhsT=wd_codes[:, jp * P : (jp + 1) * P].bitcast(FP8X4),
+                    lhsT_scale=wd_plane[:, jp * P : (jp + 1) * P],
+                    rhs=h_codes[:].bitcast(FP8X4),
+                    rhs_scale=h_plane[:],
+                    start=False,
+                    stop=(jp == J_PASSES - 1),
+                )
+            result = sbuf("result%d" % nb, [P, M], F32)
+            nc.scalar.copy(result[:], sums[nb][:])
+            nc.sync.dma_start(out[nb * P : (nb + 1) * P, :], result[:])
 
-        def store_block(sums, mb):
-            result = sbuf("result%d" % mb, [P, N_BLOCKS, P], F32)
-            nc.scalar.copy(result[:], sums[:])
-            nc.sync.dma_start(out.rearrange("(b p) m -> p b m", p=P)[:, :, mb * P : (mb + 1) * P], result[:])
-
-        wd_mx, h_mx = [], {}
-        for u, (jp, t) in enumerate(units):
-            response_pass(odd_banks[u], odd_picked, odd_planes, jp, t, 1)
-            square(odd_squares, odd_banks[u], jp, t)
-            if jp == 0:
-                add_slot(nc.gpsimd, t)
-        sums = [drive_block(mb) for mb in range(M_BLOCKS)]
-        turned = [pick_pooling_weights(nb) for nb in range(2)]
-        h_first = [amplitude("h_first%d" % half, first_energy[:, :, half * 2 * P : (half + 1) * 2 * P], 2 * P) for half in range(2)]
-        wd_bf = [sign_pooling_weights(0, turned[0], WD_ROWS[1])]
-        turned.append(pick_pooling_weights(2))
-        wd_mx.append(quantise("wd0", wd_bf[0][:], J_PASSES * P, WD_ROWS[2]))
-        wd_bf.append(sign_pooling_weights(1, turned[1], WD_ROWS[1]))
-        wd_mx.append(quantise("wd1", wd_bf[1][:], J_PASSES * P))
-        for half in range(2):
-            codes, plane = quantise("h0%d" % half, h_first[half][:], 2 * P, WD_ROWS[1] + 4 * 2 * P * half)
-            for mb in range(2):
-                h_mx[2 * half + mb, 0] = codes[:, mb * P : (mb + 1) * P], plane[:, mb * P : (mb + 1) * P]
-        wd_bf.append(sign_pooling_weights(2, turned[2], WD_ROWS[0]))
-        h_second = [amplitude("h_second%d" % mb, add_block(nc.gpsimd, mb)[:], P) for mb in range(M_BLOCKS)]
-        wd_mx.append(quantise("wd2", wd_bf[2][:], J_PASSES * P))
-        for nb in range(N_BLOCKS):
-            for mb in range(M_BLOCKS):
-                pool_pass(sums[mb], mb, 0, nb)
+        wd_mx, h_mx = [], []
+        for u in range(len(units)):
+            odd_part(u)
         for mb in range(M_BLOCKS):
-            codes, plane = quantise("h1%d" % mb, h_second[mb][:], P, WD_ROWS[0] + 4 * P * mb)
-            h_mx[mb, 1] = codes[:], plane[:]
-            for nb in range(N_BLOCKS):
-                pool_pass(sums[mb], mb, 1, nb)
-            store_block(sums[mb], mb)
+            turn_squares(energies[mb], odd_squares[0], mb, False)
+        roots = [turned_amplitude(mb) for mb in range(M_BLOCKS)]
+        turned = [pick_pooling_weights(nb) for nb in range(N_BLOCKS)]
+        for half in range(2):
+            turn_back(half, roots)
+        sums = [drive_block(nb) for nb in range(N_BLOCKS)]
+        for mb in range(M_BLOCKS):
+            amplitude(mb, add_block(nc.vector, mb))
+        signed_place = BEHIND_WD + 4 * PASS * M_BLOCKS
+        wd_bf = [sign_pooling_weights(0, turned[0], signed_place)]
+        h_mx.append(quantise("h0", h_bf[0][:], M, LAST_SQUARES))
+        wd_mx.append(quantise("wd0", wd_bf[0][:], J_PASSES * P))
+        wd_bf.append(sign_pooling_weights(1, turned[1], signed_place))
+        h_mx.append(quantise("h1", h_bf[1][:], M))
+        pool_block(0)
+        wd_mx.append(quantise("wd1", wd_bf[1][:], J_PASSES * P))
+        pool_block(1)
+        wd_bf.append(sign_pooling_weights(2, turned[2], signed_place))
+        wd_mx.append(quantise("wd2", wd_bf[2][:], J_PASSES * P))
+        pool_block(2)

@@ -35,11 +35,9 @@ ENERGY_BANKS = (0, 1, 2, 3)
 ODD_BANKS = (4, 5, 6, 7)
 RETURN_BANKS = (4, 5)
 TURN_BANKS = (0, 1, 2)
-SUM_BANKS = (6, 7, 3)
+SUM_BANKS = (5, 0, 1)
 REGION = 4 * T
-ODD_LISTED, EVEN_WORDS, X_ROUNDED, WD_ROWS = 0, REGION, (2 * REGION, 2 * REGION + REGION // 2), (3 * REGION, 4 * REGION, 5 * REGION)
-LAST_SQUARES = 7 * REGION
-BEHIND_WD = WD_ROWS[2] + 64 - 4 * PASS
+ODD_ROWS, LAST_WD_ROWS, LAST_SQUARES = 0, REGION, 3 * REGION
 
 
 def tile_list_motion_energy_pool_kernel(
@@ -64,8 +62,8 @@ def tile_list_motion_energy_pool_kernel(
         gains = sbuf("gains", [P, J_PASSES, PACK], F32)
         nc.sync.dma_start(gains[:], g.rearrange("(h p t) -> p h t", p=P, t=PACK))
 
-        def load_table_scales(name, scales, clearing_engine):
-            rows = sbuf(name, [P, T], U8)
+        def load_table_scales(name, scales, clearing_engine, place=None):
+            rows = sbuf(name, [P, T], U8, place)
             clearing_engine.memset(rows[:].bitcast(I32), 0)
             for q in range(QUADRANTS):
                 nc.sync.dma_start(
@@ -74,8 +72,8 @@ def tile_list_motion_energy_pool_kernel(
                 )
             return rows
 
-        def load_table_words(name, words, a, place=None):
-            tile_a = sbuf("%s%d" % (name, a), [P, T], I32, place)
+        def load_table_words(name, words, a):
+            tile_a = sbuf("%s%d" % (name, a), [P, T], I32)
             nc.sync.dma_start(tile_a[:], words[a].rearrange("p t i -> p (t i)").bitcast(I32))
             return tile_a
 
@@ -86,8 +84,8 @@ def tile_list_motion_energy_pool_kernel(
 
         even_scale_rows = load_table_scales("even_scale_rows", tab_scales, nc.gpsimd)
         x_raw = [load_x(0)]
-        odd_scale_rows = load_table_scales("odd_scale_rows", tab2_scales, nc.vector)
-        even_words = [load_table_words("even_words", tab_words, 0, EVEN_WORDS)]
+        odd_scale_rows = load_table_scales("odd_scale_rows", tab2_scales, nc.vector, ODD_ROWS)
+        even_words = [load_table_words("even_words", tab_words, 0)]
         x_raw.append(load_x(1))
         even_words.append(load_table_words("even_words", tab_words, 1))
         odd_words = [load_table_words("odd_words", tab2_words, a) for a in range(K_PASSES)]
@@ -104,7 +102,7 @@ def tile_list_motion_energy_pool_kernel(
 
         wd_rows = []
         for nb in range(N_BLOCKS):
-            rows = sbuf("wd_rows%d" % nb, [P, T], F32, WD_ROWS[nb])
+            rows = sbuf("wd_rows%d" % nb, [P, T], F32, LAST_WD_ROWS if nb == N_BLOCKS - 1 else None)
             nc.sync.dma_start(rows[:], wdT[nb * P : (nb + 1) * P, :])
             wd_rows.append(rows)
 
@@ -115,14 +113,15 @@ def tile_list_motion_energy_pool_kernel(
         identity = sbuf("identity", [P, P], F32)
         make_identity(nc, identity[:])
 
-        def gather_scales(name, rows, dealt, first, last, place=None):
-            listed = sbuf(name, [P, (last - first) * PASS], U8, place)
-            cols = PASS // LIST_GROUP
-            nc.vector.tensor_copy(listed[:], rows[:].indirect(offsets[:, first * cols : last * cols]))
+        def gather_scales(name, rows):
+            listed = sbuf(name + "_listed", [P, S], U8)
+            nc.vector.tensor_copy(listed[:], rows[:].indirect(offsets[:]))
+            dealt = sbuf(name, [P, S], U8)
             nc.vector.tensor_copy(
-                dealt[:, first * PASS : last * PASS].rearrange("p (h t q) -> p h t q", q=P, t=PACK),
+                dealt[:].rearrange("p (h t q) -> p h t q", q=P, t=PACK),
                 listed[:].rearrange("p (h q t) -> p h t q", q=P, t=PACK),
             )
+            return dealt
 
         def gather_words(name, words, places):
             picked = {}
@@ -151,20 +150,17 @@ def tile_list_motion_energy_pool_kernel(
                 x_raw[a][:].rearrange("p i (c e) -> p c i e", e=LINE),
             )
 
-        even_planes = sbuf("even_planes", [P, S], U8)
-        odd_planes = sbuf("odd_planes", [P, S], U8)
-        gather_scales("even_listed", even_scale_rows, even_planes, 0, J_PASSES)
-        gather_scales("odd_listed0", odd_scale_rows, odd_planes, 0, 1, ODD_LISTED)
-        x_bf = [sbuf("x_bf%d" % a, [P, M * PACK], BF16, X_ROUNDED[a]) for a in range(K_PASSES)]
+        even_planes = gather_scales("even_planes", even_scale_rows)
+        odd_planes = gather_scales("odd_planes", odd_scale_rows)
+        x_bf = [sbuf("x_bf%d" % a, [P, M * PACK], BF16) for a in range(K_PASSES)]
         round_x(0)
-        even_picked = [gather_words("even_picked0", even_words[0], (ODD_LISTED,))]
-        x_mx = [quantise("x0", x_bf[0][:], M, EVEN_WORDS)]
-        gather_scales("odd_listed1", odd_scale_rows, odd_planes, 1, 2, X_ROUNDED[0])
-        signs = sbuf("signs", [P, J_PASSES, PACK], BF16)
-        nc.scalar.activation(signs[:], gains[:], ACT.Sign)
+        even_picked = [gather_words("even_picked0", even_words[0], (ODD_ROWS + M,))]
+        x_mx = [quantise("x0", x_bf[0][:], M, ODD_ROWS)]
+        signs = sbuf("signs", [P, J_PASSES, P, PACK], BF16)
+        nc.scalar.activation(signs[:], gains[:].unsqueeze(2).to_broadcast([P, J_PASSES, P, PACK]), ACT.Sign)
         round_x(1)
+        even_picked.append(gather_words("even_picked1", even_words[1], (None,)))
         x_mx.append(quantise("x1", x_bf[1][:], M))
-        even_picked.append(gather_words("even_picked1", even_words[1], X_ROUNDED))
 
         units = [(jp, t) for jp in range(J_PASSES) for t in range(PACK)]
 
@@ -239,15 +235,15 @@ def tile_list_motion_energy_pool_kernel(
                 returned[:].rearrange("p b u m -> p b m u"),
             )
 
-        def add_block(engine, mb):
-            energy = sbuf("second_energy%d" % mb, [P, PACK, P], F32, BEHIND_WD + 4 * PASS * mb)
-            m_cols = slice(mb * P, (mb + 1) * P)
-            engine.tensor_tensor(energy[:], even_squares[1][:, :, m_cols], odd_squares[1][:, :, m_cols], ADD)
+        def add_half(half):
+            energy = sbuf("second_energy%d" % half, [P, PACK, M // 2], F32, LAST_WD_ROWS + 2 * S + 2 * PACK * M * half)
+            m_cols = slice(half * M // 2, (half + 1) * M // 2)
+            nc.vector.tensor_tensor(energy[:], even_squares[1][:, :, m_cols], odd_squares[1][:, :, m_cols], ADD)
             return energy
 
-        def amplitude(mb, energy):
+        def amplitude(half, energy):
             nc.scalar.activation(
-                h_bf[1][:, mb * PASS : (mb + 1) * PASS].rearrange("p (c e t) -> p c t e", e=LINE, t=PACK),
+                h_bf[1][:, half * 2 * PASS : (half + 1) * 2 * PASS].rearrange("p (c e t) -> p c t e", e=LINE, t=PACK),
                 energy[:].rearrange("p t (c e) -> p c t e", e=LINE),
                 ACT.Sqrt,
             )
@@ -259,21 +255,20 @@ def tile_list_motion_energy_pool_kernel(
                 wd_rows[nb][:].indirect(offsets[:]),
             )
             pairs = picked[:].bitcast(F32)
-            turned = bank("turned%d" % nb, TURN_BANKS[nb], [P, J_PASSES, 2, P])
+            turned = bank("turned%d" % nb, TURN_BANKS[nb], [P, 2, J_PASSES, P])
             for jp in range(J_PASSES):
                 for u in range(2):
-                    nc.tensor.transpose(turned[:, jp, u, :], pairs[:, P * (2 * jp + u) : P * (2 * jp + u + 1)], identity[:])
+                    nc.tensor.transpose(turned[:, u, jp, :], pairs[:, P * (2 * jp + u) : P * (2 * jp + u + 1)], identity[:])
             return turned
 
-        def sign_pooling_weights(nb, turned, place=None):
+        def sign_pooling_weights(nb, place=None):
             wd_bf = sbuf("wd_bf%d" % nb, [P, J_PASSES * PASS], BF16, place)
-            for jp in range(J_PASSES):
-                nc.vector.tensor_tensor(
-                    wd_bf[:, jp * PASS : (jp + 1) * PASS].rearrange("p (n u e) -> p n u e", u=2, e=2),
-                    turned[:, jp, :, :].bitcast(BF16).rearrange("p u (n e) -> p n u e", e=2),
-                    signs[:, jp, :].rearrange("p (u e) -> p u e", e=2).unsqueeze(1).to_broadcast([P, P, 2, 2]),
-                    MULT,
-                )
+            nc.vector.tensor_tensor(
+                wd_bf[:].rearrange("p (c u e) -> p c u e", u=2, e=2),
+                turned[nb][:].rearrange("p u h n -> p u (h n)").bitcast(BF16).rearrange("p u (c e) -> p c u e", e=2),
+                signs[:].rearrange("p h n (u e) -> p (h n) u e", e=2),
+                MULT,
+            )
             return wd_bf
 
         def drive_block(nb):
@@ -317,18 +312,19 @@ def tile_list_motion_energy_pool_kernel(
         turned = [pick_pooling_weights(nb) for nb in range(N_BLOCKS)]
         for half in range(2):
             turn_back(half, roots)
-        sums = [drive_block(nb) for nb in range(N_BLOCKS)]
-        for mb in range(M_BLOCKS):
-            amplitude(mb, add_block(nc.vector, mb))
-        signed_place = BEHIND_WD + 4 * PASS * M_BLOCKS
-        wd_bf = [sign_pooling_weights(0, turned[0], signed_place)]
+        sums = [drive_block(0)]
+        amplitude(0, add_half(0))
+        wd_bf = [sign_pooling_weights(0, LAST_WD_ROWS)]
+        sums.append(drive_block(1))
+        amplitude(1, add_half(1))
         h_mx.append(quantise("h0", h_bf[0][:], M, LAST_SQUARES))
-        wd_mx.append(quantise("wd0", wd_bf[0][:], J_PASSES * P))
-        wd_bf.append(sign_pooling_weights(1, turned[1], signed_place))
+        wd_bf.append(sign_pooling_weights(1, LAST_SQUARES + M))
+        sums.append(drive_block(2))
+        wd_mx.append(quantise("wd0", wd_bf[0][:], J_PASSES * P, LAST_SQUARES + M + 2 * S))
         h_mx.append(quantise("h1", h_bf[1][:], M))
         pool_block(0)
+        wd_bf.append(sign_pooling_weights(2, LAST_WD_ROWS))
         wd_mx.append(quantise("wd1", wd_bf[1][:], J_PASSES * P))
         pool_block(1)
-        wd_bf.append(sign_pooling_weights(2, turned[2], signed_place))
         wd_mx.append(quantise("wd2", wd_bf[2][:], J_PASSES * P))
         pool_block(2)

@@ -35,9 +35,9 @@ ENERGY_BANKS = (0, 1, 2, 3)
 ODD_BANKS = (4, 5, 6, 7)
 RETURN_BANKS = (4, 5)
 TURN_BANKS = (0, 1, 2)
-SUM_BANKS = (5, 0, 1)
+SUM_BANKS = (4, 5, 0, 1, 3)
 REGION = 4 * T
-ODD_ROWS, LAST_WD_ROWS, LAST_SQUARES = 0, REGION, 3 * REGION
+ODD_ROWS, LAST_WD_ROWS, LAST_SQUARES, X_ROUNDED = 0, REGION, 3 * REGION, 4 * REGION
 
 
 def tile_list_motion_energy_pool_kernel(
@@ -144,6 +144,12 @@ def tile_list_motion_energy_pool_kernel(
             nc.vector.quantize_mx(out=codes[:].bitcast(FP8X4), scales=plane[:], in_=values)
             return codes, plane
 
+        def quantise_columns(target, values, first, last):
+            codes, plane = target
+            nc.vector.quantize_mx(
+                out=codes[:, first:last].bitcast(FP8X4), scales=plane[:, first:last], in_=values[:, PACK * first : PACK * last]
+            )
+
         def round_x(a):
             nc.scalar.copy(
                 x_bf[a][:].rearrange("p (c e i) -> p c i e", e=LINE, i=PACK),
@@ -152,15 +158,15 @@ def tile_list_motion_energy_pool_kernel(
 
         even_planes = gather_scales("even_planes", even_scale_rows)
         odd_planes = gather_scales("odd_planes", odd_scale_rows)
-        x_bf = [sbuf("x_bf%d" % a, [P, M * PACK], BF16) for a in range(K_PASSES)]
+        x_bf = [sbuf("x_bf%d" % a, [P, M * PACK], BF16, (None, X_ROUNDED)[a]) for a in range(K_PASSES)]
         round_x(0)
         even_picked = [gather_words("even_picked0", even_words[0], (ODD_ROWS + M,))]
         x_mx = [quantise("x0", x_bf[0][:], M, ODD_ROWS)]
         signs = sbuf("signs", [P, J_PASSES, P, PACK], BF16)
         nc.scalar.activation(signs[:], gains[:].unsqueeze(2).to_broadcast([P, J_PASSES, P, PACK]), ACT.Sign)
         round_x(1)
-        even_picked.append(gather_words("even_picked1", even_words[1], (None,)))
         x_mx.append(quantise("x1", x_bf[1][:], M))
+        even_picked.append(gather_words("even_picked1", even_words[1], (None, X_ROUNDED)))
 
         units = [(jp, t) for jp in range(J_PASSES) for t in range(PACK)]
 
@@ -271,39 +277,51 @@ def tile_list_motion_energy_pool_kernel(
             )
             return wd_bf
 
-        def drive_block(nb):
-            sums = bank("sums%d" % nb, SUM_BANKS[nb], [P, M])
+        pieces = [(0, 0, M // 2), (0, M // 2, M), (1, 0, M), (2, 0, M // 2), (2, M // 2, M)]
+
+        def drive_piece(piece):
+            nb, first, last = pieces[piece]
+            sums = bank("sums%d" % piece, SUM_BANKS[piece], [P, last - first])
             for a in range(K_PASSES):
                 x_codes, x_plane = x_mx[a]
                 nc.tensor.matmul_mx(
                     out=sums[:],
                     lhsT=ws_codes[:, a, 2 * P * nb : 2 * P * (nb + 1)].bitcast(FP4X4),
                     lhsT_scale=ws_planes[:, a, nb * P : (nb + 1) * P],
-                    rhs=x_codes[:].bitcast(FP8X4),
-                    rhs_scale=x_plane[:],
+                    rhs=x_codes[:, first:last].bitcast(FP8X4),
+                    rhs_scale=x_plane[:, first:last],
                     start=(a == 0),
                     stop=False,
                 )
             return sums
 
-        def pool_block(nb):
-            wd_codes, wd_plane = wd_mx[nb]
-            for jp in range(J_PASSES):
-                h_codes, h_plane = h_mx[jp]
-                nc.tensor.matmul_mx(
-                    out=sums[nb][:],
-                    lhsT=wd_codes[:, jp * P : (jp + 1) * P].bitcast(FP8X4),
-                    lhsT_scale=wd_plane[:, jp * P : (jp + 1) * P],
-                    rhs=h_codes[:].bitcast(FP8X4),
-                    rhs_scale=h_plane[:],
-                    start=False,
-                    stop=(jp == J_PASSES - 1),
-                )
-            result = sbuf("result%d" % nb, [P, M], F32)
-            nc.scalar.copy(result[:], sums[nb][:])
-            nc.sync.dma_start(out[nb * P : (nb + 1) * P, :], result[:])
+        def pool_pass(piece, jp):
+            nb, first, last = pieces[piece]
+            wd_codes, wd_plane = wd_mx[nb, jp]
+            h_codes, h_plane = h_mx[jp]
+            nc.tensor.matmul_mx(
+                out=sums[piece][:],
+                lhsT=wd_codes.bitcast(FP8X4),
+                lhsT_scale=wd_plane,
+                rhs=h_codes[:, first:last].bitcast(FP8X4),
+                rhs_scale=h_plane[:, first:last],
+                start=False,
+                stop=(jp == J_PASSES - 1),
+            )
 
-        wd_mx, h_mx = [], []
+        def store_piece(piece, copy, queue):
+            nb, first, last = pieces[piece]
+            result = sbuf("result%d" % piece, [P, last - first], F32)
+            copy(result[:], sums[piece][:])
+            queue.dma_start(out[nb * P : (nb + 1) * P, first:last], result[:])
+
+        def quantise_wd(nb, first, last, place=None):
+            codes, plane = quantise("wd%d%d" % (nb, first), wd_bf[nb][:, first * PASS : last * PASS], (last - first) * P, place)
+            for jp in range(first, last):
+                cols = slice((jp - first) * P, (jp - first + 1) * P)
+                wd_mx[nb, jp] = codes[:, cols], plane[:, cols]
+
+        wd_mx, h_mx = {}, []
         for u in range(len(units)):
             odd_part(u)
         for mb in range(M_BLOCKS):
@@ -312,19 +330,32 @@ def tile_list_motion_energy_pool_kernel(
         turned = [pick_pooling_weights(nb) for nb in range(N_BLOCKS)]
         for half in range(2):
             turn_back(half, roots)
-        sums = [drive_block(0)]
-        amplitude(0, add_half(0))
+        sums = [drive_piece(piece) for piece in range(2)]
+        for half in range(2):
+            amplitude(half, add_half(half))
         wd_bf = [sign_pooling_weights(0, LAST_WD_ROWS)]
-        sums.append(drive_block(1))
-        amplitude(1, add_half(1))
+        sums.append(drive_piece(2))
         h_mx.append(quantise("h0", h_bf[0][:], M, LAST_SQUARES))
-        wd_bf.append(sign_pooling_weights(1, LAST_SQUARES + M))
-        sums.append(drive_block(2))
-        wd_mx.append(quantise("wd0", wd_bf[0][:], J_PASSES * P, LAST_SQUARES + M + 2 * S))
-        h_mx.append(quantise("h1", h_bf[1][:], M))
-        pool_block(0)
+        quantise_wd(0, 0, J_PASSES, LAST_SQUARES + M)
+        h_mx.append((sbuf("h1_codes", [P, M], U32), sbuf("h1_plane", [P, M], U8, LAST_SQUARES + 2 * M)))
+        for half in range(2):
+            pool_pass(half, 0)
+        quantise_columns(h_mx[1], h_bf[1], 0, M // 2)
+        pool_pass(0, 1)
+        store_piece(0, nc.scalar.copy, nc.sync)
+        wd_bf.append(sign_pooling_weights(1, LAST_WD_ROWS))
+        sums.extend(drive_piece(piece) for piece in (3, 4))
+        quantise_columns(h_mx[1], h_bf[1], M // 2, M)
+        pool_pass(1, 1)
+        store_piece(1, nc.scalar.copy, nc.sync)
+        quantise_wd(1, 0, J_PASSES)
+        for jp in range(J_PASSES):
+            pool_pass(2, jp)
+        store_piece(2, nc.scalar.copy, nc.sync)
         wd_bf.append(sign_pooling_weights(2, LAST_WD_ROWS))
-        wd_mx.append(quantise("wd1", wd_bf[1][:], J_PASSES * P))
-        pool_block(1)
-        wd_mx.append(quantise("wd2", wd_bf[2][:], J_PASSES * P))
-        pool_block(2)
+        for jp in range(J_PASSES):
+            quantise_wd(2, jp, jp + 1)
+            for piece in (3, 4):
+                pool_pass(piece, jp)
+        store_piece(3, nc.vector.tensor_copy, nc.sync)
+        store_piece(4, nc.scalar.copy, nc.scalar)

@@ -35,9 +35,10 @@ ENERGY_BANKS = (0, 1, 2, 3)
 ODD_BANKS = (4, 5, 6, 7)
 RETURN_BANKS = (4, 5)
 TURN_BANKS = (0, 1, 2)
-SUM_BANKS = (4, 5, 0, 1, 3)
+SUM_BANKS = (0, 1, 4, 5, 3)
 REGION = 4 * T
-ODD_ROWS, LAST_WD_ROWS, LAST_SQUARES, X_ROUNDED = 0, REGION, 3 * REGION, 4 * REGION
+ODD_ROWS, LAST_WD_ROWS, LAST_SQUARES, X_ROUNDED = 0, REGION, 3 * REGION, (4 * REGION, 5 * REGION)
+TURNED_SQUARES = 6 * REGION
 
 
 def tile_list_motion_energy_pool_kernel(
@@ -123,20 +124,14 @@ def tile_list_motion_energy_pool_kernel(
             )
             return dealt
 
-        def gather_words(name, words, places):
-            picked = {}
-            pieces = len(places)
-            halves = J_PASSES // pieces
-            cols = S // pieces // LIST_GROUP
-            for piece in range(pieces):
-                part = sbuf("%s%d" % (name, piece), [P, S // pieces], U32, places[piece])
-                nc.vector.tensor_copy(
-                    part[:].rearrange("p (h t q) -> p h q t", h=halves, t=PACK),
-                    words[:].bitcast(U32).indirect(offsets[:, piece * cols : (piece + 1) * cols]),
-                )
-                for h in range(halves):
-                    picked[piece * halves + h] = part[:, h * PASS : (h + 1) * PASS]
-            return picked
+        def gather_words(name, words, first, last, place=None):
+            cols = PASS // LIST_GROUP
+            part = sbuf("%s%d" % (name, first), [P, (last - first) * PASS], U32, place)
+            nc.vector.tensor_copy(
+                part[:].rearrange("p (h t q) -> p h q t", q=P, t=PACK),
+                words[:].bitcast(U32).indirect(offsets[:, first * cols : last * cols]),
+            )
+            return [part[:, h * PASS : (h + 1) * PASS] for h in range(last - first)]
 
         def quantise(name, values, width, place=None):
             codes = sbuf(name + "_codes", [P, width], U32)
@@ -158,15 +153,17 @@ def tile_list_motion_energy_pool_kernel(
 
         even_planes = gather_scales("even_planes", even_scale_rows)
         odd_planes = gather_scales("odd_planes", odd_scale_rows)
-        x_bf = [sbuf("x_bf%d" % a, [P, M * PACK], BF16, (None, X_ROUNDED)[a]) for a in range(K_PASSES)]
+        x_bf = [sbuf("x_bf%d" % a, [P, M * PACK], BF16, X_ROUNDED[a]) for a in range(K_PASSES)]
         round_x(0)
-        even_picked = [gather_words("even_picked0", even_words[0], (ODD_ROWS + M,))]
+        even_picked = [gather_words("even_picked0", even_words[0], 0, 1, ODD_ROWS + M)]
         x_mx = [quantise("x0", x_bf[0][:], M, ODD_ROWS)]
+        even_picked[0].extend(gather_words("even_picked0", even_words[0], 1, 2, X_ROUNDED[0]))
         signs = sbuf("signs", [P, J_PASSES, P, PACK], BF16)
         nc.scalar.activation(signs[:], gains[:].unsqueeze(2).to_broadcast([P, J_PASSES, P, PACK]), ACT.Sign)
         round_x(1)
         x_mx.append(quantise("x1", x_bf[1][:], M))
-        even_picked.append(gather_words("even_picked1", even_words[1], (None, X_ROUNDED)))
+        even_picked.append(gather_words("even_picked1", even_words[1], 0, 1))
+        even_picked[1].extend(gather_words("even_picked1", even_words[1], 1, 2, X_ROUNDED[1]))
 
         units = [(jp, t) for jp in range(J_PASSES) for t in range(PACK)]
 
@@ -186,7 +183,7 @@ def tile_list_motion_energy_pool_kernel(
             nc.scalar.activation(squares[jp][:, t, :], response[:], ACT.Square, scale=gains[:, jp, t : t + 1])
 
         even_squares = [sbuf("even_squares%d" % jp, [P, PACK, M], F32, (None, LAST_SQUARES)[jp]) for jp in range(J_PASSES)]
-        odd_squares = [sbuf("odd_squares%d" % jp, [P, PACK, M], F32) for jp in range(J_PASSES)]
+        odd_squares = [sbuf("odd_squares%d" % jp, [P, PACK, M], F32, (TURNED_SQUARES, None)[jp]) for jp in range(J_PASSES)]
 
         def turn_squares(energy, squares, mb, first):
             for t in range(PACK):
@@ -209,8 +206,8 @@ def tile_list_motion_energy_pool_kernel(
         for mb in range(M_BLOCKS):
             turn_squares(energies[mb], even_squares[0], mb, True)
 
-        odd_picked = [gather_words("odd_picked0", odd_words[0], (None,))]
-        odd_picked.append(gather_words("odd_picked1", odd_words[1], (None, None)))
+        odd_picked = [gather_words("odd_picked0", odd_words[0], 0, J_PASSES)]
+        odd_picked.append(gather_words("odd_picked1", odd_words[1], 0, 1) + gather_words("odd_picked1", odd_words[1], 1, 2))
 
         def odd_part(u):
             jp, t = units[u]
@@ -219,7 +216,7 @@ def tile_list_motion_energy_pool_kernel(
                 response_pass(response, odd_picked, odd_planes, jp, t, a)
             square(odd_squares, response, jp, t)
 
-        h_bf = [sbuf("h_bf%d" % jp, [P, M * PACK], BF16) for jp in range(J_PASSES)]
+        h_bf = [sbuf("h_bf%d" % jp, [P, M * PACK], BF16, (None, TURNED_SQUARES)[jp]) for jp in range(J_PASSES)]
 
         def turned_amplitude(mb):
             roots = sbuf("roots%d" % mb, [P, PASS], BF16)
@@ -241,10 +238,10 @@ def tile_list_motion_energy_pool_kernel(
                 returned[:].rearrange("p b u m -> p b m u"),
             )
 
-        def add_half(half):
-            energy = sbuf("second_energy%d" % half, [P, PACK, M // 2], F32, LAST_WD_ROWS + 2 * S + 2 * PACK * M * half)
+        def add_half(half, engine, place=None):
+            energy = sbuf("second_energy%d" % half, [P, PACK, M // 2], F32, place)
             m_cols = slice(half * M // 2, (half + 1) * M // 2)
-            nc.vector.tensor_tensor(energy[:], even_squares[1][:, :, m_cols], odd_squares[1][:, :, m_cols], ADD)
+            engine.tensor_tensor(energy[:], even_squares[1][:, :, m_cols], odd_squares[1][:, :, m_cols], ADD)
             return energy
 
         def amplitude(half, energy):
@@ -330,11 +327,10 @@ def tile_list_motion_energy_pool_kernel(
         turned = [pick_pooling_weights(nb) for nb in range(N_BLOCKS)]
         for half in range(2):
             turn_back(half, roots)
-        sums = [drive_piece(piece) for piece in range(2)]
-        for half in range(2):
-            amplitude(half, add_half(half))
-        wd_bf = [sign_pooling_weights(0, LAST_WD_ROWS)]
-        sums.append(drive_piece(2))
+        amplitude(0, add_half(0, nc.gpsimd))
+        wd_bf = [sign_pooling_weights(nb, LAST_WD_ROWS + 2 * S * nb) for nb in range(2)]
+        amplitude(1, add_half(1, nc.vector, LAST_WD_ROWS + 4 * S))
+        sums = [drive_piece(piece) for piece in range(len(pieces))]
         h_mx.append(quantise("h0", h_bf[0][:], M, LAST_SQUARES))
         quantise_wd(0, 0, J_PASSES, LAST_SQUARES + M)
         h_mx.append((sbuf("h1_codes", [P, M], U32), sbuf("h1_plane", [P, M], U8, LAST_SQUARES + 2 * M)))
@@ -343,16 +339,14 @@ def tile_list_motion_energy_pool_kernel(
         quantise_columns(h_mx[1], h_bf[1], 0, M // 2)
         pool_pass(0, 1)
         store_piece(0, nc.scalar.copy, nc.sync)
-        wd_bf.append(sign_pooling_weights(1, LAST_WD_ROWS))
-        sums.extend(drive_piece(piece) for piece in (3, 4))
+        quantise_wd(1, 0, J_PASSES, LAST_WD_ROWS)
+        pool_pass(2, 0)
         quantise_columns(h_mx[1], h_bf[1], M // 2, M)
         pool_pass(1, 1)
         store_piece(1, nc.scalar.copy, nc.sync)
-        quantise_wd(1, 0, J_PASSES)
-        for jp in range(J_PASSES):
-            pool_pass(2, jp)
+        pool_pass(2, 1)
         store_piece(2, nc.scalar.copy, nc.sync)
-        wd_bf.append(sign_pooling_weights(2, LAST_WD_ROWS))
+        wd_bf.append(sign_pooling_weights(2, LAST_WD_ROWS + 2 * S))
         for jp in range(J_PASSES):
             quantise_wd(2, jp, jp + 1)
             for piece in (3, 4):

@@ -35,10 +35,10 @@ ENERGY_BANKS = (0, 1, 2, 3)
 ODD_BANKS = (4, 5, 6, 7)
 RETURN_BANKS = (4, 5)
 TURN_BANKS = (0, 1, 2)
-SUM_BANKS = (0, 1, 4, 5, 3)
+SUM_BANKS = (3, 0, 4, 1, 5, 6)
 REGION = 4 * T
 ODD_ROWS, LAST_WD_ROWS, LAST_SQUARES, X_ROUNDED = 0, REGION, 3 * REGION, (4 * REGION, 5 * REGION)
-TURNED_SQUARES = 6 * REGION
+LAST_ROOTS = 6 * REGION
 
 
 def tile_list_motion_energy_pool_kernel(
@@ -86,6 +86,9 @@ def tile_list_motion_energy_pool_kernel(
         even_scale_rows = load_table_scales("even_scale_rows", tab_scales, nc.gpsimd)
         x_raw = [load_x(0)]
         odd_scale_rows = load_table_scales("odd_scale_rows", tab2_scales, nc.vector, ODD_ROWS)
+        gain_rows = sbuf("gain_rows", [P, P], F32)
+        nc.gpsimd.memset(gain_rows[:], 0.0)
+        nc.sync.dma_start(gain_rows[:PACK, :], g[:PASS].rearrange("(c p) -> c p", p=P))
         even_words = [load_table_words("even_words", tab_words, 0)]
         x_raw.append(load_x(1))
         even_words.append(load_table_words("even_words", tab_words, 1))
@@ -117,21 +120,21 @@ def tile_list_motion_energy_pool_kernel(
         def gather_scales(name, rows):
             listed = sbuf(name + "_listed", [P, S], U8)
             nc.vector.tensor_copy(listed[:], rows[:].indirect(offsets[:]))
-            dealt = sbuf(name, [P, S], U8)
+            dealt = sbuf(name, [P, PASS], U8)
             nc.vector.tensor_copy(
-                dealt[:].rearrange("p (h t q) -> p h t q", q=P, t=PACK),
-                listed[:].rearrange("p (h q t) -> p h t q", q=P, t=PACK),
+                dealt[:].rearrange("p (t q) -> p t q", t=PACK),
+                listed[:, PASS:].rearrange("p (q t) -> p t q", t=PACK),
             )
-            return dealt
+            return [listed[:, :PASS], dealt[:]]
 
-        def gather_words(name, words, first, last, place=None):
+        def gather_words(name, words, jp, place=None):
             cols = PASS // LIST_GROUP
-            part = sbuf("%s%d" % (name, first), [P, (last - first) * PASS], U32, place)
+            part = sbuf("%s%d" % (name, jp), [P, PASS], U32, place)
             nc.vector.tensor_copy(
-                part[:].rearrange("p (h t q) -> p h q t", q=P, t=PACK),
-                words[:].bitcast(U32).indirect(offsets[:, first * cols : last * cols]),
+                part[:].rearrange("p (t q) -> p q t", t=PACK) if jp else part[:],
+                words[:].bitcast(U32).indirect(offsets[:, jp * cols : (jp + 1) * cols]),
             )
-            return [part[:, h * PASS : (h + 1) * PASS] for h in range(last - first)]
+            return part
 
         def quantise(name, values, width, place=None):
             codes = sbuf(name + "_codes", [P, width], U32)
@@ -155,15 +158,20 @@ def tile_list_motion_energy_pool_kernel(
         odd_planes = gather_scales("odd_planes", odd_scale_rows)
         x_bf = [sbuf("x_bf%d" % a, [P, M * PACK], BF16, X_ROUNDED[a]) for a in range(K_PASSES)]
         round_x(0)
-        even_picked = [gather_words("even_picked0", even_words[0], 0, 1, ODD_ROWS + M)]
+        even_picked = [[gather_words("even_picked0", even_words[0], 0, ODD_ROWS + M)]]
         x_mx = [quantise("x0", x_bf[0][:], M, ODD_ROWS)]
-        even_picked[0].extend(gather_words("even_picked0", even_words[0], 1, 2, X_ROUNDED[0]))
+        even_picked[0].append(gather_words("even_picked0", even_words[0], 1, X_ROUNDED[0]))
         signs = sbuf("signs", [P, J_PASSES, P, PACK], BF16)
         nc.scalar.activation(signs[:], gains[:].unsqueeze(2).to_broadcast([P, J_PASSES, P, PACK]), ACT.Sign)
+        turned_gains = bank("turned_gains", ODD_BANKS[-1], [P, P])
+        nc.tensor.transpose(turned_gains[:], gain_rows[:], identity[:])
+        listed_gains = sbuf("listed_gains", [P, PACK], F32)
+        nc.scalar.copy(listed_gains[:], turned_gains[:, :PACK])
+        slot_gains = [listed_gains[:], gains[:, 1, :]]
         round_x(1)
         x_mx.append(quantise("x1", x_bf[1][:], M))
-        even_picked.append(gather_words("even_picked1", even_words[1], 0, 1))
-        even_picked[1].extend(gather_words("even_picked1", even_words[1], 1, 2, X_ROUNDED[1]))
+        even_picked.append([gather_words("even_picked1", even_words[1], 0)])
+        even_picked[1].append(gather_words("even_picked1", even_words[1], 1, X_ROUNDED[1]))
 
         units = [(jp, t) for jp in range(J_PASSES) for t in range(PACK)]
 
@@ -172,7 +180,7 @@ def tile_list_motion_energy_pool_kernel(
             nc.tensor.matmul_mx(
                 out=target[:],
                 lhsT=picked[a][jp][:, t * P : (t + 1) * P].bitcast(FP8X4),
-                lhsT_scale=planes[SCALE_ROWS * a :, jp * PASS + t * P : jp * PASS + (t + 1) * P],
+                lhsT_scale=planes[jp][SCALE_ROWS * a :, t * P : (t + 1) * P],
                 rhs=x_codes[:].bitcast(FP8X4),
                 rhs_scale=x_plane[:],
                 start=(a == 0),
@@ -180,10 +188,10 @@ def tile_list_motion_energy_pool_kernel(
             )
 
         def square(squares, response, jp, t):
-            nc.scalar.activation(squares[jp][:, t, :], response[:], ACT.Square, scale=gains[:, jp, t : t + 1])
+            nc.scalar.activation(squares[jp][:, t, :], response[:], ACT.Square, scale=slot_gains[jp][:, t : t + 1])
 
-        even_squares = [sbuf("even_squares%d" % jp, [P, PACK, M], F32, (None, LAST_SQUARES)[jp]) for jp in range(J_PASSES)]
-        odd_squares = [sbuf("odd_squares%d" % jp, [P, PACK, M], F32, (TURNED_SQUARES, None)[jp]) for jp in range(J_PASSES)]
+        even_squares = [sbuf("even_squares%d" % jp, [P, PACK, M], F32) for jp in range(J_PASSES)]
+        odd_squares = [sbuf("odd_squares%d" % jp, [P, PACK, M], F32) for jp in range(J_PASSES)]
 
         def turn_squares(energy, squares, mb, first):
             for t in range(PACK):
@@ -206,8 +214,7 @@ def tile_list_motion_energy_pool_kernel(
         for mb in range(M_BLOCKS):
             turn_squares(energies[mb], even_squares[0], mb, True)
 
-        odd_picked = [gather_words("odd_picked0", odd_words[0], 0, J_PASSES)]
-        odd_picked.append(gather_words("odd_picked1", odd_words[1], 0, 1) + gather_words("odd_picked1", odd_words[1], 1, 2))
+        odd_picked = [[gather_words("odd_picked%d" % a, odd_words[a], jp) for jp in range(J_PASSES)] for a in range(K_PASSES)]
 
         def odd_part(u):
             jp, t = units[u]
@@ -216,13 +223,13 @@ def tile_list_motion_energy_pool_kernel(
                 response_pass(response, odd_picked, odd_planes, jp, t, a)
             square(odd_squares, response, jp, t)
 
-        h_bf = [sbuf("h_bf%d" % jp, [P, M * PACK], BF16, (None, TURNED_SQUARES)[jp]) for jp in range(J_PASSES)]
+        h_bf = [sbuf("h_bf0", [P, M * PACK], BF16)]
 
         def turned_amplitude(mb):
-            roots = sbuf("roots%d" % mb, [P, PASS], BF16)
+            roots = sbuf("roots%d" % mb, [P, PASS], BF16, LAST_ROOTS if mb == M_BLOCKS - 1 else None)
             nc.scalar.activation(
                 roots[:].rearrange("p (u q e) -> p u q e", u=2, e=2),
-                energies[mb][:].rearrange("p (u e) q -> p u q e", e=2),
+                energies[mb][:].rearrange("p c j -> p (c j)").rearrange("p (q u e) -> p u q e", u=2, e=2),
                 ACT.Sqrt,
             )
             return roots
@@ -238,16 +245,15 @@ def tile_list_motion_energy_pool_kernel(
                 returned[:].rearrange("p b u m -> p b m u"),
             )
 
-        def add_half(half, engine, place=None):
-            energy = sbuf("second_energy%d" % half, [P, PACK, M // 2], F32, place)
-            m_cols = slice(half * M // 2, (half + 1) * M // 2)
-            engine.tensor_tensor(energy[:], even_squares[1][:, :, m_cols], odd_squares[1][:, :, m_cols], ADD)
-            return energy
+        second_energy = sbuf("second_energy", [P, PACK, M], F32)
 
-        def amplitude(half, energy):
+        def add_slot(t):
+            nc.gpsimd.tensor_tensor(second_energy[:, t, :], even_squares[1][:, t, :], odd_squares[1][:, t, :], ADD)
+
+        def amplitude(half):
             nc.scalar.activation(
                 h_bf[1][:, half * 2 * PASS : (half + 1) * 2 * PASS].rearrange("p (c e t) -> p c t e", e=LINE, t=PACK),
-                energy[:].rearrange("p t (c e) -> p c t e", e=LINE),
+                second_energy[:, :, half * M // 2 : (half + 1) * M // 2].rearrange("p t (c e) -> p c t e", e=LINE),
                 ACT.Sqrt,
             )
 
@@ -274,7 +280,7 @@ def tile_list_motion_energy_pool_kernel(
             )
             return wd_bf
 
-        pieces = [(0, 0, M // 2), (0, M // 2, M), (1, 0, M), (2, 0, M // 2), (2, M // 2, M)]
+        pieces = [(nb, half * M // 2, (half + 1) * M // 2) for half in range(2) for nb in range(N_BLOCKS)]
 
         def drive_piece(piece):
             nb, first, last = pieces[piece]
@@ -319,37 +325,45 @@ def tile_list_motion_energy_pool_kernel(
                 wd_mx[nb, jp] = codes[:, cols], plane[:, cols]
 
         wd_mx, h_mx = {}, []
-        for u in range(len(units)):
+        for u, (jp, t) in enumerate(units):
             odd_part(u)
+            if jp == 1:
+                add_slot(t)
         for mb in range(M_BLOCKS):
             turn_squares(energies[mb], odd_squares[0], mb, False)
         roots = [turned_amplitude(mb) for mb in range(M_BLOCKS)]
         turned = [pick_pooling_weights(nb) for nb in range(N_BLOCKS)]
         for half in range(2):
             turn_back(half, roots)
-        amplitude(0, add_half(0, nc.gpsimd))
-        wd_bf = [sign_pooling_weights(nb, LAST_WD_ROWS + 2 * S * nb) for nb in range(2)]
-        amplitude(1, add_half(1, nc.vector, LAST_WD_ROWS + 4 * S))
-        sums = [drive_piece(piece) for piece in range(len(pieces))]
-        h_mx.append(quantise("h0", h_bf[0][:], M, LAST_SQUARES))
-        quantise_wd(0, 0, J_PASSES, LAST_SQUARES + M)
-        h_mx.append((sbuf("h1_codes", [P, M], U32), sbuf("h1_plane", [P, M], U8, LAST_SQUARES + 2 * M)))
+        h_bf.append(sbuf("h_bf1", [P, M * PACK], BF16, LAST_ROOTS))
         for half in range(2):
-            pool_pass(half, 0)
+            amplitude(half)
+        wd_bf = [sign_pooling_weights(nb, LAST_WD_ROWS + 2 * S * nb) for nb in range(2)]
+        sums = [drive_piece(piece) for piece in range(len(pieces))]
+        quantise_wd(0, 0, J_PASSES)
+        h_mx.append(quantise("h0", h_bf[0][:], M, LAST_WD_ROWS + 2 * S * N_BLOCKS))
+        h_mx.append((sbuf("h1_codes", [P, M], U32), sbuf("h1_plane", [P, M], U8, LAST_WD_ROWS)))
+
+        def finish_piece(piece, copy, queue):
+            pool_pass(piece, 1)
+            store_piece(piece, copy, queue)
+
+        def open_block(nb, last):
+            quantise_wd(nb, 0, last)
+            for half in range(2):
+                pool_pass(half * N_BLOCKS + nb, 0)
+
+        for half in range(2):
+            pool_pass(half * N_BLOCKS, 0)
         quantise_columns(h_mx[1], h_bf[1], 0, M // 2)
-        pool_pass(0, 1)
-        store_piece(0, nc.scalar.copy, nc.sync)
-        quantise_wd(1, 0, J_PASSES, LAST_WD_ROWS)
-        pool_pass(2, 0)
-        quantise_columns(h_mx[1], h_bf[1], M // 2, M)
-        pool_pass(1, 1)
-        store_piece(1, nc.scalar.copy, nc.sync)
-        pool_pass(2, 1)
-        store_piece(2, nc.scalar.copy, nc.sync)
+        finish_piece(0, nc.scalar.copy, nc.sync)
+        open_block(1, J_PASSES)
+        finish_piece(1, nc.scalar.copy, nc.sync)
         wd_bf.append(sign_pooling_weights(2, LAST_WD_ROWS + 2 * S))
-        for jp in range(J_PASSES):
-            quantise_wd(2, jp, jp + 1)
-            for piece in (3, 4):
-                pool_pass(piece, jp)
-        store_piece(3, nc.vector.tensor_copy, nc.sync)
-        store_piece(4, nc.scalar.copy, nc.scalar)
+        quantise_columns(h_mx[1], h_bf[1], M // 2, M)
+        for nb in range(2):
+            finish_piece(N_BLOCKS + nb, nc.scalar.copy, nc.sync)
+        open_block(2, 1)
+        quantise_wd(2, 1, J_PASSES)
+        finish_piece(2, nc.vector.tensor_copy, nc.sync)
+        finish_piece(N_BLOCKS + 2, nc.scalar.copy, nc.sync)

@@ -247,8 +247,10 @@ def tile_list_motion_energy_pool_kernel(
 
         second_energy = sbuf("second_energy", [P, PACK, M], F32)
 
-        def add_slot(t):
-            nc.gpsimd.tensor_tensor(second_energy[:, t, :], even_squares[1][:, t, :], odd_squares[1][:, t, :], ADD)
+        def add_slot(t, first, last):
+            nc.gpsimd.tensor_tensor(
+                second_energy[:, t, first:last], even_squares[1][:, t, first:last], odd_squares[1][:, t, first:last], ADD
+            )
 
         def amplitude(half):
             nc.scalar.activation(
@@ -328,7 +330,8 @@ def tile_list_motion_energy_pool_kernel(
         for u, (jp, t) in enumerate(units):
             odd_part(u)
             if jp == 1:
-                add_slot(t)
+                add_slot(t, 0, M if t < PACK - 1 else M // 2)
+        add_slot(PACK - 1, M // 2, M)
         for mb in range(M_BLOCKS):
             turn_squares(energies[mb], odd_squares[0], mb, False)
         roots = [turned_amplitude(mb) for mb in range(M_BLOCKS)]
@@ -365,5 +368,5 @@ def tile_list_motion_energy_pool_kernel(
             finish_piece(N_BLOCKS + nb, nc.scalar.copy, nc.sync)
         open_block(2, 1)
         quantise_wd(2, 1, J_PASSES)
-        finish_piece(2, nc.vector.tensor_copy, nc.sync)
-        finish_piece(N_BLOCKS + 2, nc.scalar.copy, nc.sync)
+        finish_piece(2, nc.scalar.copy, nc.sync)
+        finish_piece(N_BLOCKS + 2, nc.vector.tensor_copy, nc.sync)

@@ -30,15 +30,16 @@ QUADRANT = P // QUADRANTS
 SCALE_ROWS = 4
 LIST_GROUP = 16
 LINE = 4
+HEAD_COLUMNS = T // 4
 BANK_BYTES = 2048
 ENERGY_BANKS = (0, 1, 2, 3)
 ODD_BANKS = (4, 5, 6, 7)
-RETURN_BANKS = (4, 5)
-TURN_BANKS = (0, 1, 2)
-SUM_BANKS = (3, 0, 4, 1, 5, 6)
+RETURN_BANKS = (7, 0)
+TURN_BANKS = (4, 5, 6)
+SUM_BANKS = (1, 2, 3, 7, 0, 4)
 REGION = 4 * T
-ODD_ROWS, LAST_WD_ROWS, LAST_SQUARES, X_ROUNDED = 0, REGION, 3 * REGION, (4 * REGION, 5 * REGION)
-LAST_ROOTS = 6 * REGION
+ODD_ROWS, LAST_WD_ROWS, LAST_X_ROWS, LAST_X, LAST_ROOTS = (REGION * i for i in range(5))
+RUN = 8
 
 
 def tile_list_motion_energy_pool_kernel(
@@ -60,8 +61,9 @@ def tile_list_motion_energy_pool_kernel(
 
         offsets = keep.tile([P, S // LIST_GROUP], U16, name="offsets")
         nc.sync.dma_start(offsets[:], offs)
-        gains = sbuf("gains", [P, J_PASSES, PACK], F32)
-        nc.sync.dma_start(gains[:], g.rearrange("(h p t) -> p h t", p=P, t=PACK))
+        first_words = sbuf("even_words0", [P, T], I32)
+        first_rows = tab_words[0].rearrange("p t i -> p (t i)").bitcast(I32)
+        nc.sync.dma_start(first_words[:, :HEAD_COLUMNS], first_rows[:, :HEAD_COLUMNS])
 
         def load_table_scales(name, scales, clearing_engine, place=None):
             rows = sbuf(name, [P, T], U8, place)
@@ -73,31 +75,38 @@ def tile_list_motion_energy_pool_kernel(
                 )
             return rows
 
-        def load_table_words(name, words, a):
-            tile_a = sbuf("%s%d" % (name, a), [P, T], I32)
+        def load_table_words(name, words, a, place=None):
+            tile_a = sbuf("%s%d" % (name, a), [P, T], I32, place)
             nc.sync.dma_start(tile_a[:], words[a].rearrange("p t i -> p (t i)").bitcast(I32))
             return tile_a
 
-        def load_x(a):
-            raw = sbuf("x_raw%d" % a, [P, PACK, M], F32)
+        def load_x(a, place=None):
+            raw = sbuf("x_raw%d" % a, [P, PACK, M], F32, place)
             nc.sync.dma_start(raw[:], x[a * PASS : (a + 1) * PASS, :].rearrange("(p i) m -> p i m", i=PACK))
             return raw
 
         even_scale_rows = load_table_scales("even_scale_rows", tab_scales, nc.gpsimd)
         x_raw = [load_x(0)]
+        warm = sbuf("warm", [P, 1], F32)
+        nc.vector.memset(warm[:], 1.0)
+        nc.scalar.activation(warm[:], warm[:], ACT.Sqrt)
         odd_scale_rows = load_table_scales("odd_scale_rows", tab2_scales, nc.vector, ODD_ROWS)
         gain_rows = sbuf("gain_rows", [P, P], F32)
-        nc.gpsimd.memset(gain_rows[:], 0.0)
-        nc.sync.dma_start(gain_rows[:PACK, :], g[:PASS].rearrange("(c p) -> c p", p=P))
-        even_words = [load_table_words("even_words", tab_words, 0)]
-        x_raw.append(load_x(1))
-        even_words.append(load_table_words("even_words", tab_words, 1))
+        nc.vector.memset(gain_rows[:], 0.0)
+        for jp in range(J_PASSES):
+            nc.sync.dma_start(
+                gain_rows[jp * PACK : (jp + 1) * PACK, :].rearrange("t (b r) -> t b r", r=RUN),
+                g[jp * PASS : (jp + 1) * PASS].rearrange("(b t r) -> t b r", t=PACK, r=RUN),
+            )
+        nc.sync.dma_start(first_words[:, HEAD_COLUMNS:], first_rows[:, HEAD_COLUMNS:])
+        x_raw.append(load_x(1, LAST_X_ROWS))
+        even_words = [first_words, load_table_words("even_words", tab_words, 1)]
         odd_words = [load_table_words("odd_words", tab2_words, a) for a in range(K_PASSES)]
 
         ws_codes = sbuf("ws_codes", [P, K_PASSES, 2 * N], U8)
         nc.sync.dma_start(ws_codes[:].bitcast(I32), ws_words.rearrange("a p c -> p a c").bitcast(I32))
         ws_planes = sbuf("ws_planes", [P, K_PASSES, N], U8)
-        nc.gpsimd.memset(ws_planes[:].bitcast(I32), 0)
+        nc.vector.memset(ws_planes[:].bitcast(I32), 0)
         for q in range(QUADRANTS):
             nc.sync.dma_start(
                 ws_planes[QUADRANT * q : QUADRANT * q + SCALE_ROWS, :, :].bitcast(I32),
@@ -110,31 +119,31 @@ def tile_list_motion_energy_pool_kernel(
             nc.sync.dma_start(rows[:], wdT[nb * P : (nb + 1) * P, :])
             wd_rows.append(rows)
 
-        warm = sbuf("warm", [P, 1], F32)
-        nc.gpsimd.memset(warm[:], 1.0)
-        nc.scalar.activation(warm[:], warm[:], ACT.Sqrt)
-
         identity = sbuf("identity", [P, P], F32)
-        make_identity(nc, identity[:])
+        nc.vector.memset(identity[:], 0.0)
+        make_identity(nc, identity[:], nomemset=True)
 
         def gather_scales(name, rows):
-            listed = sbuf(name + "_listed", [P, S], U8)
+            listed = sbuf(name, [P, S], U8)
             nc.vector.tensor_copy(listed[:], rows[:].indirect(offsets[:]))
-            dealt = sbuf(name, [P, PASS], U8)
-            nc.vector.tensor_copy(
-                dealt[:].rearrange("p (t q) -> p t q", t=PACK),
-                listed[:, PASS:].rearrange("p (q t) -> p t q", t=PACK),
-            )
-            return [listed[:, :PASS], dealt[:]]
+            return listed
 
-        def gather_words(name, words, jp, place=None):
-            cols = PASS // LIST_GROUP
-            part = sbuf("%s%d" % (name, jp), [P, PASS], U32, place)
+        def deal_scales(name, listed, place):
+            dealt = sbuf(name, [P, J_PASSES, PASS], U8, place)
             nc.vector.tensor_copy(
-                part[:].rearrange("p (t q) -> p q t", t=PACK) if jp else part[:],
-                words[:].bitcast(U32).indirect(offsets[:, jp * cols : (jp + 1) * cols]),
+                dealt[:].rearrange("p h c -> p (h c)").bitcast(I32).rearrange("p (h t b k) -> p h t b k", h=J_PASSES, t=PACK, k=RUN // 4),
+                listed[:].bitcast(I32).rearrange("p (h b t k) -> p h t b k", h=J_PASSES, t=PACK, k=RUN // 4),
             )
-            return part
+            return dealt
+
+        def gather_words(name, words, first, last, place=None):
+            cols = PASS // LIST_GROUP
+            part = sbuf("%s%d" % (name, first), [P, last - first, PASS], U32, place)
+            nc.vector.tensor_copy(
+                part[:].rearrange("p h (t b r) -> p h b t r", t=PACK, r=RUN),
+                words[:].bitcast(U32).indirect(offsets[:, first * cols : last * cols]),
+            )
+            return [part[:, h, :] for h in range(last - first)]
 
         def quantise(name, values, width, place=None):
             codes = sbuf(name + "_codes", [P, width], U32)
@@ -148,30 +157,38 @@ def tile_list_motion_energy_pool_kernel(
                 out=codes[:, first:last].bitcast(FP8X4), scales=plane[:, first:last], in_=values[:, PACK * first : PACK * last]
             )
 
-        def round_x(a):
+        def round_x(a, last):
             nc.scalar.copy(
-                x_bf[a][:].rearrange("p (c e i) -> p c i e", e=LINE, i=PACK),
-                x_raw[a][:].rearrange("p i (c e) -> p c i e", e=LINE),
+                x_bf[a][:, : PACK * last].rearrange("p (c e i) -> p c i e", e=LINE, i=PACK),
+                x_raw[a][:, :, :last].rearrange("p i (c e) -> p c i e", e=LINE),
             )
+            if last < M:
+                nc.gpsimd.tensor_scalar(
+                    x_bf[a][:, PACK * last :].rearrange("p (m i) -> p m i", i=PACK),
+                    x_raw[a][:, :, last:].rearrange("p i m -> p m i"),
+                    1.0,
+                    0.0,
+                    MULT,
+                    ADD,
+                )
 
-        even_planes = gather_scales("even_planes", even_scale_rows)
-        odd_planes = gather_scales("odd_planes", odd_scale_rows)
-        x_bf = [sbuf("x_bf%d" % a, [P, M * PACK], BF16, X_ROUNDED[a]) for a in range(K_PASSES)]
-        round_x(0)
-        even_picked = [[gather_words("even_picked0", even_words[0], 0, ODD_ROWS + M)]]
+        even_planes = deal_scales("even_planes", gather_scales("even_listed", even_scale_rows), None)
+        odd_listed = gather_scales("odd_listed", odd_scale_rows)
+        x_bf = [sbuf("x_bf%d" % a, [P, M * PACK], BF16, (None, LAST_X)[a]) for a in range(K_PASSES)]
+        round_x(0, M)
         x_mx = [quantise("x0", x_bf[0][:], M, ODD_ROWS)]
-        even_picked[0].append(gather_words("even_picked0", even_words[0], 1, X_ROUNDED[0]))
-        signs = sbuf("signs", [P, J_PASSES, P, PACK], BF16)
-        nc.scalar.activation(signs[:], gains[:].unsqueeze(2).to_broadcast([P, J_PASSES, P, PACK]), ACT.Sign)
+        even_picked = [gather_words("even_picked0", even_words[0], 0, 1) + gather_words("even_picked0", even_words[0], 1, 2)]
         turned_gains = bank("turned_gains", ODD_BANKS[-1], [P, P])
         nc.tensor.transpose(turned_gains[:], gain_rows[:], identity[:])
-        listed_gains = sbuf("listed_gains", [P, PACK], F32)
-        nc.scalar.copy(listed_gains[:], turned_gains[:, :PACK])
-        slot_gains = [listed_gains[:], gains[:, 1, :]]
-        round_x(1)
+        slot_gains = sbuf("slot_gains", [P, J_PASSES, PACK], F32)
+        nc.scalar.copy(slot_gains[:].rearrange("p h t -> p (h t)"), turned_gains[:, : J_PASSES * PACK])
+        round_x(1, M // 2)
+        signs = sbuf("signs", [P, J_PASSES, PACK], BF16)
+        nc.scalar.activation(signs[:], slot_gains[:], ACT.Sign)
+
         x_mx.append(quantise("x1", x_bf[1][:], M))
-        even_picked.append([gather_words("even_picked1", even_words[1], 0)])
-        even_picked[1].append(gather_words("even_picked1", even_words[1], 1, X_ROUNDED[1]))
+        odd_planes = deal_scales("odd_planes", odd_listed, LAST_X_ROWS)
+        even_picked.append(gather_words("even_picked1", even_words[1], 0, 1) + gather_words("even_picked1", even_words[1], 1, 2, LAST_X))
 
         units = [(jp, t) for jp in range(J_PASSES) for t in range(PACK)]
 
@@ -180,7 +197,7 @@ def tile_list_motion_energy_pool_kernel(
             nc.tensor.matmul_mx(
                 out=target[:],
                 lhsT=picked[a][jp][:, t * P : (t + 1) * P].bitcast(FP8X4),
-                lhsT_scale=planes[jp][SCALE_ROWS * a :, t * P : (t + 1) * P],
+                lhsT_scale=planes[SCALE_ROWS * a :, jp, t * P : (t + 1) * P],
                 rhs=x_codes[:].bitcast(FP8X4),
                 rhs_scale=x_plane[:],
                 start=(a == 0),
@@ -188,7 +205,7 @@ def tile_list_motion_energy_pool_kernel(
             )
 
         def square(squares, response, jp, t):
-            nc.scalar.activation(squares[jp][:, t, :], response[:], ACT.Square, scale=slot_gains[jp][:, t : t + 1])
+            nc.scalar.activation(squares[jp][:, t, :], response[:], ACT.Square, scale=slot_gains[:, jp, t : t + 1])
 
         even_squares = [sbuf("even_squares%d" % jp, [P, PACK, M], F32) for jp in range(J_PASSES)]
         odd_squares = [sbuf("odd_squares%d" % jp, [P, PACK, M], F32) for jp in range(J_PASSES)]
@@ -210,15 +227,15 @@ def tile_list_motion_energy_pool_kernel(
         for u, (jp, t) in enumerate(units):
             response_pass(even_banks[u], even_picked, even_planes, jp, t, 1)
             square(even_squares, even_banks[u], jp, t)
-        energies = [bank("energy%d" % mb, ENERGY_BANKS[mb], [P, PACK, P]) for mb in range(M_BLOCKS)]
-        for mb in range(M_BLOCKS):
-            turn_squares(energies[mb], even_squares[0], mb, True)
 
-        odd_picked = [[gather_words("odd_picked%d" % a, odd_words[a], jp) for jp in range(J_PASSES)] for a in range(K_PASSES)]
+        odd_picked = [
+            gather_words("odd_picked0", odd_words[0], 0, J_PASSES),
+            gather_words("odd_picked1", odd_words[1], 0, 1) + gather_words("odd_picked1", odd_words[1], 1, 2),
+        ]
 
         def odd_part(u):
             jp, t = units[u]
-            response = bank("odd%d" % u, ODD_BANKS[t], [P, M])
+            response = bank("odd%d" % u, u, [P, M])
             for a in range(K_PASSES):
                 response_pass(response, odd_picked, odd_planes, jp, t, a)
             square(odd_squares, response, jp, t)
@@ -229,7 +246,7 @@ def tile_list_motion_energy_pool_kernel(
             roots = sbuf("roots%d" % mb, [P, PASS], BF16, LAST_ROOTS if mb == M_BLOCKS - 1 else None)
             nc.scalar.activation(
                 roots[:].rearrange("p (u q e) -> p u q e", u=2, e=2),
-                energies[mb][:].rearrange("p c j -> p (c j)").rearrange("p (q u e) -> p u q e", u=2, e=2),
+                energies[mb][:].rearrange("p (u e) q -> p u q e", e=2),
                 ACT.Sqrt,
             )
             return roots
@@ -247,9 +264,9 @@ def tile_list_motion_energy_pool_kernel(
 
         second_energy = sbuf("second_energy", [P, PACK, M], F32)
 
-        def add_slot(t, first, last):
+        def add_squares(slots, first, last):
             nc.gpsimd.tensor_tensor(
-                second_energy[:, t, first:last], even_squares[1][:, t, first:last], odd_squares[1][:, t, first:last], ADD
+                second_energy[:, slots, first:last], even_squares[1][:, slots, first:last], odd_squares[1][:, slots, first:last], ADD
             )
 
         def amplitude(half):
@@ -262,22 +279,21 @@ def tile_list_motion_energy_pool_kernel(
         def pick_pooling_weights(nb):
             picked = sbuf("wd_picked%d" % nb, [P, S], BF16)
             nc.vector.tensor_copy(
-                picked[:].rearrange("p (h u q e) -> p h q u e", h=J_PASSES, u=2, e=2),
-                wd_rows[nb][:].indirect(offsets[:]),
+                picked[:].rearrange("p (u c r e) -> p c u e r", u=2, r=RUN, e=2), wd_rows[nb][:].indirect(offsets[:])
             )
             pairs = picked[:].bitcast(F32)
             turned = bank("turned%d" % nb, TURN_BANKS[nb], [P, 2, J_PASSES, P])
             for jp in range(J_PASSES):
                 for u in range(2):
-                    nc.tensor.transpose(turned[:, u, jp, :], pairs[:, P * (2 * jp + u) : P * (2 * jp + u + 1)], identity[:])
+                    nc.tensor.transpose(turned[:, u, jp, :], pairs[:, P * (2 * u + jp) : P * (2 * u + jp + 1)], identity[:])
             return turned
 
         def sign_pooling_weights(nb, place=None):
             wd_bf = sbuf("wd_bf%d" % nb, [P, J_PASSES * PASS], BF16, place)
             nc.vector.tensor_tensor(
-                wd_bf[:].rearrange("p (c u e) -> p c u e", u=2, e=2),
-                turned[nb][:].rearrange("p u h n -> p u (h n)").bitcast(BF16).rearrange("p u (c e) -> p c u e", e=2),
-                signs[:].rearrange("p h n (u e) -> p (h n) u e", e=2),
+                wd_bf[:].rearrange("p (h n u e) -> p h n u e", h=J_PASSES, u=2, e=2),
+                turned[nb][:].bitcast(BF16).rearrange("p u h (n e) -> p h n u e", e=2),
+                signs[:].rearrange("p h (u e) -> p h u e", e=2).unsqueeze(2).to_broadcast([P, J_PASSES, P, 2, 2]),
                 MULT,
             )
             return wd_bf
@@ -330,9 +346,11 @@ def tile_list_motion_energy_pool_kernel(
         for u, (jp, t) in enumerate(units):
             odd_part(u)
             if jp == 1:
-                add_slot(t, 0, M if t < PACK - 1 else M // 2)
-        add_slot(PACK - 1, M // 2, M)
+                add_squares(slice(t, t + 1), 0, M // 2)
+        add_squares(slice(0, PACK), M // 2, M)
+        energies = [bank("energy%d" % mb, ENERGY_BANKS[mb], [P, PACK, P]) for mb in range(M_BLOCKS)]
         for mb in range(M_BLOCKS):
+            turn_squares(energies[mb], even_squares[0], mb, True)
             turn_squares(energies[mb], odd_squares[0], mb, False)
         roots = [turned_amplitude(mb) for mb in range(M_BLOCKS)]
         turned = [pick_pooling_weights(nb) for nb in range(N_BLOCKS)]
@@ -358,14 +376,12 @@ def tile_list_motion_energy_pool_kernel(
 
         for half in range(2):
             pool_pass(half * N_BLOCKS, 0)
-        quantise_columns(h_mx[1], h_bf[1], 0, M // 2)
-        finish_piece(0, nc.scalar.copy, nc.sync)
         open_block(1, J_PASSES)
-        finish_piece(1, nc.scalar.copy, nc.sync)
         wd_bf.append(sign_pooling_weights(2, LAST_WD_ROWS + 2 * S))
-        quantise_columns(h_mx[1], h_bf[1], M // 2, M)
-        for nb in range(2):
-            finish_piece(N_BLOCKS + nb, nc.scalar.copy, nc.sync)
+        for half in range(2):
+            quantise_columns(h_mx[1], h_bf[1], half * M // 2, (half + 1) * M // 2)
+            for nb in range(2):
+                finish_piece(half * N_BLOCKS + nb, nc.scalar.copy, nc.sync)
         open_block(2, 1)
         quantise_wd(2, 1, J_PASSES)
         finish_piece(2, nc.scalar.copy, nc.sync)

@@ -32,11 +32,11 @@ LIST_GROUP = 16
 LINE = 4
 HEAD_COLUMNS = T // 4
 BANK_BYTES = 2048
-ENERGY_BANKS = (0, 1, 2, 3)
-ODD_BANKS = (4, 5, 6, 7)
-RETURN_BANKS = (7, 0)
-TURN_BANKS = (4, 5, 6)
-SUM_BANKS = (1, 2, 3, 7, 0, 4)
+ENERGY_BANKS = (4, 5, 6, 7)
+GAIN_BANK = 7
+RETURN_BANKS = (3, 4)
+TURN_BANKS = (0, 1, 2)
+SUM_BANKS = (5, 6, 7, 3, 4, 0)
 REGION = 4 * T
 ODD_ROWS, LAST_WD_ROWS, LAST_X_ROWS, LAST_X, LAST_ROOTS = (REGION * i for i in range(5))
 RUN = 8
@@ -174,11 +174,11 @@ def tile_list_motion_energy_pool_kernel(
 
         even_planes = deal_scales("even_planes", gather_scales("even_listed", even_scale_rows), None)
         odd_listed = gather_scales("odd_listed", odd_scale_rows)
-        x_bf = [sbuf("x_bf%d" % a, [P, M * PACK], BF16, (None, LAST_X)[a]) for a in range(K_PASSES)]
+        x_bf = [sbuf("x_bf%d" % a, [P, M * PACK], BF16, LAST_X) for a in range(K_PASSES)]
         round_x(0, M)
         x_mx = [quantise("x0", x_bf[0][:], M, ODD_ROWS)]
         even_picked = [gather_words("even_picked0", even_words[0], 0, 1) + gather_words("even_picked0", even_words[0], 1, 2)]
-        turned_gains = bank("turned_gains", ODD_BANKS[-1], [P, P])
+        turned_gains = bank("turned_gains", GAIN_BANK, [P, P])
         nc.tensor.transpose(turned_gains[:], gain_rows[:], identity[:])
         slot_gains = sbuf("slot_gains", [P, J_PASSES, PACK], F32)
         nc.scalar.copy(slot_gains[:].rearrange("p h t -> p (h t)"), turned_gains[:, : J_PASSES * PACK])
@@ -221,12 +221,11 @@ def tile_list_motion_energy_pool_kernel(
                     is_transpose=True,
                 )
 
-        even_banks = [bank("even%d" % u, u, [P, M]) for u in range(len(units))]
         for u, (jp, t) in enumerate(units):
-            response_pass(even_banks[u], even_picked, even_planes, jp, t, 0)
-        for u, (jp, t) in enumerate(units):
-            response_pass(even_banks[u], even_picked, even_planes, jp, t, 1)
-            square(even_squares, even_banks[u], jp, t)
+            response = bank("even%d" % u, t, [P, M])
+            for a in range(K_PASSES):
+                response_pass(response, even_picked, even_planes, jp, t, a)
+            square(even_squares, response, jp, t)
 
         odd_picked = [
             gather_words("odd_picked0", odd_words[0], 0, J_PASSES),
@@ -235,7 +234,7 @@ def tile_list_motion_energy_pool_kernel(
 
         def odd_part(u):
             jp, t = units[u]
-            response = bank("odd%d" % u, u, [P, M])
+            response = bank("odd%d" % u, (u + PACK) % len(units), [P, M])
             for a in range(K_PASSES):
                 response_pass(response, odd_picked, odd_planes, jp, t, a)
             square(odd_squares, response, jp, t)

@@ -40,6 +40,7 @@ SUM_BANKS = (5, 6, 7, 3, 4, 0)
 REGION = 4 * T
 ODD_ROWS, LAST_WD_ROWS, LAST_X_ROWS, LAST_X, LAST_ROOTS = (REGION * i for i in range(5))
 RUN = 8
+SCALAR_COLUMNS = 352
 
 
 def tile_list_motion_energy_pool_kernel(
@@ -182,7 +183,7 @@ def tile_list_motion_energy_pool_kernel(
         nc.tensor.transpose(turned_gains[:], gain_rows[:], identity[:])
         slot_gains = sbuf("slot_gains", [P, J_PASSES, PACK], F32)
         nc.scalar.copy(slot_gains[:].rearrange("p h t -> p (h t)"), turned_gains[:, : J_PASSES * PACK])
-        round_x(1, M // 2)
+        round_x(1, SCALAR_COLUMNS)
         signs = sbuf("signs", [P, J_PASSES, PACK], BF16)
         nc.scalar.activation(signs[:], slot_gains[:], ACT.Sign)
 

@@ -66,14 +66,16 @@ def tile_list_motion_energy_pool_kernel(
         first_rows = tab_words[0].rearrange("p t i -> p (t i)").bitcast(I32)
         nc.sync.dma_start(first_words[:, :HEAD_COLUMNS], first_rows[:, :HEAD_COLUMNS])
 
-        def load_table_scales(name, scales, clearing_engine, place=None):
+        def load_table_scales(name, scales, clearing_engine, joint_quadrants, place=None):
             rows = sbuf(name, [P, T], U8, place)
             clearing_engine.memset(rows[:].bitcast(I32), 0)
             for q in range(QUADRANTS):
-                nc.sync.dma_start(
-                    rows[QUADRANT * q : QUADRANT * q + K_PASSES * SCALE_ROWS, :].bitcast(I32),
-                    scales[:, SCALE_ROWS * q : SCALE_ROWS * (q + 1), :].bitcast(I32),
-                )
+                step = K_PASSES if q < joint_quadrants else 1
+                for a in range(0, K_PASSES, step):
+                    nc.sync.dma_start(
+                        rows[QUADRANT * q + SCALE_ROWS * a : QUADRANT * q + SCALE_ROWS * (a + step), :].bitcast(I32),
+                        scales[a : a + step, SCALE_ROWS * q : SCALE_ROWS * (q + 1), :].bitcast(I32),
+                    )
             return rows
 
         def load_table_words(name, words, a, place=None):
@@ -86,12 +88,14 @@ def tile_list_motion_energy_pool_kernel(
             nc.sync.dma_start(raw[:], x[a * PASS : (a + 1) * PASS, :].rearrange("(p i) m -> p i m", i=PACK))
             return raw
 
-        even_scale_rows = load_table_scales("even_scale_rows", tab_scales, nc.gpsimd)
+        even_scale_rows = load_table_scales("even_scale_rows", tab_scales, nc.gpsimd, QUADRANTS)
         x_raw = [load_x(0)]
         warm = sbuf("warm", [P, 1], F32)
         nc.vector.memset(warm[:], 1.0)
         nc.scalar.activation(warm[:], warm[:], ACT.Sqrt)
-        odd_scale_rows = load_table_scales("odd_scale_rows", tab2_scales, nc.vector, ODD_ROWS)
+        odd_scale_rows = load_table_scales("odd_scale_rows", tab2_scales, nc.vector, QUADRANTS // 2, ODD_ROWS)
+        nc.sync.dma_start(first_words[:, HEAD_COLUMNS:], first_rows[:, HEAD_COLUMNS:])
+        x_raw.append(load_x(1, LAST_X_ROWS))
         gain_rows = sbuf("gain_rows", [P, P], F32)
         nc.vector.memset(gain_rows[:], 0.0)
         for jp in range(J_PASSES):
@@ -99,13 +103,9 @@ def tile_list_motion_energy_pool_kernel(
                 gain_rows[jp * PACK : (jp + 1) * PACK, :].rearrange("t (b r) -> t b r", r=RUN),
                 g[jp * PASS : (jp + 1) * PASS].rearrange("(b t r) -> t b r", t=PACK, r=RUN),
             )
-        nc.sync.dma_start(first_words[:, HEAD_COLUMNS:], first_rows[:, HEAD_COLUMNS:])
-        x_raw.append(load_x(1, LAST_X_ROWS))
         even_words = [first_words, load_table_words("even_words", tab_words, 1)]
         odd_words = [load_table_words("odd_words", tab2_words, a) for a in range(K_PASSES)]
 
-        ws_codes = sbuf("ws_codes", [P, K_PASSES, 2 * N], U8)
-        nc.sync.dma_start(ws_codes[:].bitcast(I32), ws_words.rearrange("a p c -> p a c").bitcast(I32))
         ws_planes = sbuf("ws_planes", [P, K_PASSES, N], U8)
         nc.vector.memset(ws_planes[:].bitcast(I32), 0)
         for q in range(QUADRANTS):
@@ -119,6 +119,9 @@ def tile_list_motion_energy_pool_kernel(
             rows = sbuf("wd_rows%d" % nb, [P, T], F32, LAST_WD_ROWS if nb == N_BLOCKS - 1 else None)
             nc.sync.dma_start(rows[:], wdT[nb * P : (nb + 1) * P, :])
             wd_rows.append(rows)
+
+        ws_codes = sbuf("ws_codes", [P, K_PASSES, 2 * N], U8)
+        nc.sync.dma_start(ws_codes[:].bitcast(I32), ws_words.rearrange("a p c -> p a c").bitcast(I32))
 
         identity = sbuf("identity", [P, P], F32)
         nc.vector.memset(identity[:], 0.0)
@@ -179,11 +182,11 @@ def tile_list_motion_energy_pool_kernel(
         round_x(0, M)
         x_mx = [quantise("x0", x_bf[0][:], M, ODD_ROWS)]
         even_picked = [gather_words("even_picked0", even_words[0], 0, 1) + gather_words("even_picked0", even_words[0], 1, 2)]
+        round_x(1, SCALAR_COLUMNS)
         turned_gains = bank("turned_gains", GAIN_BANK, [P, P])
         nc.tensor.transpose(turned_gains[:], gain_rows[:], identity[:])
         slot_gains = sbuf("slot_gains", [P, J_PASSES, PACK], F32)
         nc.scalar.copy(slot_gains[:].rearrange("p h t -> p (h t)"), turned_gains[:, : J_PASSES * PACK])
-        round_x(1, SCALAR_COLUMNS)
         signs = sbuf("signs", [P, J_PASSES, PACK], BF16)
         nc.scalar.activation(signs[:], slot_gains[:], ACT.Sign)
 

@@ -128,16 +128,8 @@ def tile_list_motion_energy_pool_kernel(
         make_identity(nc, identity[:], nomemset=True)
 
         def gather_scales(name, rows):
-            listed = sbuf(name, [P, S], U8)
-            nc.vector.tensor_copy(listed[:], rows[:].indirect(offsets[:]))
-            return listed
-
-        def deal_scales(name, listed, place):
-            dealt = sbuf(name, [P, J_PASSES, PASS], U8, place)
-            nc.vector.tensor_copy(
-                dealt[:].rearrange("p h c -> p (h c)").bitcast(I32).rearrange("p (h t b k) -> p h t b k", h=J_PASSES, t=PACK, k=RUN // 4),
-                listed[:].bitcast(I32).rearrange("p (h b t k) -> p h t b k", h=J_PASSES, t=PACK, k=RUN // 4),
-            )
+            dealt = sbuf(name, [P, J_PASSES, PASS], U8)
+            nc.vector.tensor_copy(dealt[:].rearrange("p h (t b r) -> p h b t r", t=PACK, r=RUN), rows[:].indirect(offsets[:]))
             return dealt
 
         def gather_words(name, words, first, last, place=None):
@@ -176,8 +168,8 @@ def tile_list_motion_energy_pool_kernel(
                     ADD,
                 )
 
-        even_planes = deal_scales("even_planes", gather_scales("even_listed", even_scale_rows), None)
-        odd_listed = gather_scales("odd_listed", odd_scale_rows)
+        even_planes = gather_scales("even_planes", even_scale_rows)
+        odd_planes = gather_scales("odd_planes", odd_scale_rows)
         x_bf = [sbuf("x_bf%d" % a, [P, M * PACK], BF16, LAST_X) for a in range(K_PASSES)]
         round_x(0, M)
         x_mx = [quantise("x0", x_bf[0][:], M, ODD_ROWS)]
@@ -191,7 +183,6 @@ def tile_list_motion_energy_pool_kernel(
         nc.scalar.activation(signs[:], slot_gains[:], ACT.Sign)
 
         x_mx.append(quantise("x1", x_bf[1][:], M))
-        odd_planes = deal_scales("odd_planes", odd_listed, LAST_X_ROWS)
         even_picked.append(gather_words("even_picked1", even_words[1], 0, 1) + gather_words("even_picked1", even_words[1], 1, 2, LAST_X))
 
         units = [(jp, t) for jp in range(J_PASSES) for t in range(PACK)]
@@ -346,11 +337,14 @@ def tile_list_motion_energy_pool_kernel(
                 wd_mx[nb, jp] = codes[:, cols], plane[:, cols]
 
         wd_mx, h_mx = {}, []
-        for u, (jp, t) in enumerate(units):
+        for u in (0, 1, PACK, 2, 3, PACK + 1):
             odd_part(u)
-            if jp == 1:
-                add_squares(slice(t, t + 1), 0, M // 2)
-        add_squares(slice(0, PACK), M // 2, M)
+            if u >= PACK:
+                add_squares(slice(u - PACK, u - PACK + 1), 0, M)
+        for u in (PACK + 2, PACK + 3):
+            odd_part(u)
+        for half in range(2):
+            add_squares(slice(2, PACK), half * M // 2, (half + 1) * M // 2)
         energies = [bank("energy%d" % mb, ENERGY_BANKS[mb], [P, PACK, P]) for mb in range(M_BLOCKS)]
         for mb in range(M_BLOCKS):
             turn_squares(energies[mb], even_squares[0], mb, True)

@@ -30,7 +30,6 @@ QUADRANT = P // QUADRANTS
 SCALE_ROWS = 4
 LIST_GROUP = 16
 LINE = 4
-HEAD_COLUMNS = T // 4
 BANK_BYTES = 2048
 ENERGY_BANKS = (4, 5, 6, 7)
 GAIN_BANK = 7
@@ -38,9 +37,10 @@ RETURN_BANKS = (3, 4)
 TURN_BANKS = (0, 1, 2)
 SUM_BANKS = (5, 6, 7, 3, 4, 0)
 REGION = 4 * T
-ODD_ROWS, LAST_WD_ROWS, LAST_X_ROWS, LAST_X, LAST_ROOTS = (REGION * i for i in range(5))
+FIRST_X_ROWS, LAST_WD_ROWS, LAST_ROOTS = (REGION * i for i in range(3))
 RUN = 8
 SCALAR_COLUMNS = 352
+TABLE_ROWS = K_PASSES * QUADRANTS * SCALE_ROWS
 
 
 def tile_list_motion_energy_pool_kernel(
@@ -62,20 +62,13 @@ def tile_list_motion_energy_pool_kernel(
 
         offsets = keep.tile([P, S // LIST_GROUP], U16, name="offsets")
         nc.sync.dma_start(offsets[:], offs)
-        first_words = sbuf("even_words0", [P, T], I32)
-        first_rows = tab_words[0].rearrange("p t i -> p (t i)").bitcast(I32)
-        nc.sync.dma_start(first_words[:, :HEAD_COLUMNS], first_rows[:, :HEAD_COLUMNS])
 
-        def load_table_scales(name, scales, clearing_engine, joint_quadrants, place=None):
-            rows = sbuf(name, [P, T], U8, place)
-            clearing_engine.memset(rows[:].bitcast(I32), 0)
-            for q in range(QUADRANTS):
-                step = K_PASSES if q < joint_quadrants else 1
-                for a in range(0, K_PASSES, step):
-                    nc.sync.dma_start(
-                        rows[QUADRANT * q + SCALE_ROWS * a : QUADRANT * q + SCALE_ROWS * (a + step), :].bitcast(I32),
-                        scales[a : a + step, SCALE_ROWS * q : SCALE_ROWS * (q + 1), :].bitcast(I32),
-                    )
+        def load_table_scales(name, scales, first, clearing_engine):
+            rows = sbuf(name, [P, T], U8)
+            other_half = (first + P // 2) % P
+            clearing_engine.memset(rows[first + TABLE_ROWS : first + P // 2, :].bitcast(I32), 0)
+            clearing_engine.memset(rows[other_half : other_half + P // 2, :].bitcast(I32), 0)
+            nc.sync.dma_start(rows[first : first + TABLE_ROWS, :].bitcast(I32), scales.rearrange("a q t -> (a q) t").bitcast(I32))
             return rows
 
         def load_table_words(name, words, a, place=None):
@@ -88,26 +81,23 @@ def tile_list_motion_energy_pool_kernel(
             nc.sync.dma_start(raw[:], x[a * PASS : (a + 1) * PASS, :].rearrange("(p i) m -> p i m", i=PACK))
             return raw
 
-        even_scale_rows = load_table_scales("even_scale_rows", tab_scales, nc.gpsimd, QUADRANTS)
-        x_raw = [load_x(0)]
+        gain_rows = sbuf("gain_rows", [P, J_PASSES * P], F32)
+        nc.vector.memset(gain_rows[:], 0.0)
+        even_scale_rows = load_table_scales("even_scale_rows", tab_scales, 0, nc.gpsimd)
+        odd_scale_rows = load_table_scales("odd_scale_rows", tab2_scales, P // 2, nc.vector)
+        nc.sync.dma_start(
+            gain_rows[:PACK, :].rearrange("t (b r) -> t b r", r=RUN), g.rearrange("(b t r) -> t b r", t=PACK, r=RUN)
+        )
         warm = sbuf("warm", [P, 1], F32)
         nc.vector.memset(warm[:], 1.0)
         nc.scalar.activation(warm[:], warm[:], ACT.Sqrt)
-        odd_scale_rows = load_table_scales("odd_scale_rows", tab2_scales, nc.vector, QUADRANTS // 2, ODD_ROWS)
-        nc.sync.dma_start(first_words[:, HEAD_COLUMNS:], first_rows[:, HEAD_COLUMNS:])
-        x_raw.append(load_x(1, LAST_X_ROWS))
-        gain_rows = sbuf("gain_rows", [P, P], F32)
-        nc.vector.memset(gain_rows[:], 0.0)
-        for jp in range(J_PASSES):
-            nc.sync.dma_start(
-                gain_rows[jp * PACK : (jp + 1) * PACK, :].rearrange("t (b r) -> t b r", r=RUN),
-                g[jp * PASS : (jp + 1) * PASS].rearrange("(b t r) -> t b r", t=PACK, r=RUN),
-            )
-        even_words = [first_words, load_table_words("even_words", tab_words, 1)]
+        x_raw = [load_x(0, FIRST_X_ROWS)]
+        even_words = [load_table_words("even_words", tab_words, 0)]
+        x_raw.append(load_x(1))
+        even_words.append(load_table_words("even_words", tab_words, 1))
         odd_words = [load_table_words("odd_words", tab2_words, a) for a in range(K_PASSES)]
 
         ws_planes = sbuf("ws_planes", [P, K_PASSES, N], U8)
-        nc.vector.memset(ws_planes[:].bitcast(I32), 0)
         for q in range(QUADRANTS):
             nc.sync.dma_start(
                 ws_planes[QUADRANT * q : QUADRANT * q + SCALE_ROWS, :, :].bitcast(I32),
@@ -159,31 +149,43 @@ def tile_list_motion_energy_pool_kernel(
                 x_raw[a][:, :, :last].rearrange("p i (c e) -> p c i e", e=LINE),
             )
             if last < M:
-                nc.gpsimd.tensor_scalar(
-                    x_bf[a][:, PACK * last :].rearrange("p (m i) -> p m i", i=PACK),
-                    x_raw[a][:, :, last:].rearrange("p i m -> p m i"),
-                    1.0,
-                    0.0,
-                    MULT,
-                    ADD,
+                nc.vector.tensor_copy(
+                    x_bf[a][:, PACK * last :].rearrange("p (c e i) -> p c i e", e=LINE, i=PACK),
+                    x_raw[a][:, :, last:].rearrange("p i (c e) -> p c i e", e=LINE),
                 )
 
-        even_planes = gather_scales("even_planes", even_scale_rows)
-        odd_planes = gather_scales("odd_planes", odd_scale_rows)
-        x_bf = [sbuf("x_bf%d" % a, [P, M * PACK], BF16, LAST_X) for a in range(K_PASSES)]
-        round_x(0, M)
-        x_mx = [quantise("x0", x_bf[0][:], M, ODD_ROWS)]
-        even_picked = [gather_words("even_picked0", even_words[0], 0, 1) + gather_words("even_picked0", even_words[0], 1, 2)]
-        round_x(1, SCALAR_COLUMNS)
-        turned_gains = bank("turned_gains", GAIN_BANK, [P, P])
-        nc.tensor.transpose(turned_gains[:], gain_rows[:], identity[:])
+        def place_planes(name, picked, first, a, row, queue, place=None):
+            plane = sbuf("%s%d" % (name, a), [P, S], U8, place)
+            for q in range(QUADRANTS):
+                source = first + SCALE_ROWS * (QUADRANTS * a + q)
+                queue.dma_start(
+                    plane[QUADRANT * q + row : QUADRANT * q + row + SCALE_ROWS, :].bitcast(I32),
+                    picked[source : source + SCALE_ROWS, :, :].rearrange("p h c -> p (h c)").bitcast(I32),
+                )
+            return plane[row:, :]
+
+        even_scales = gather_scales("even_scales", even_scale_rows)
+        odd_scales = gather_scales("odd_scales", odd_scale_rows)
+        turned_gains = bank("turned_gains", GAIN_BANK, [P, J_PASSES, P])
+        for jp in range(J_PASSES):
+            nc.tensor.transpose(turned_gains[:, jp, :], gain_rows[:, jp * P : (jp + 1) * P], identity[:])
         slot_gains = sbuf("slot_gains", [P, J_PASSES, PACK], F32)
-        nc.scalar.copy(slot_gains[:].rearrange("p h t -> p (h t)"), turned_gains[:, : J_PASSES * PACK])
+        nc.scalar.copy(slot_gains[:], turned_gains[:, :, :PACK])
         signs = sbuf("signs", [P, J_PASSES, PACK], BF16)
         nc.scalar.activation(signs[:], slot_gains[:], ACT.Sign)
 
+        even_planes = [place_planes("even_planes", even_scales, 0, 0, 0, nc.gpsimd)]
+        odd_planes = [place_planes("odd_planes", odd_scales, P // 2, 0, 2 * SCALE_ROWS, nc.gpsimd)]
+
+        x_bf = [sbuf("x_bf%d" % a, [P, M * PACK], BF16) for a in range(K_PASSES)]
+        round_x(0, M)
+        x_mx = [quantise("x0", x_bf[0][:], M)]
+        even_planes.append(place_planes("even_planes", even_scales, 0, 1, SCALE_ROWS, nc.scalar, FIRST_X_ROWS))
+        even_picked = [gather_words("even_picked0", even_words[0], 0, 1) + gather_words("even_picked0", even_words[0], 1, 2)]
+        round_x(1, SCALAR_COLUMNS)
         x_mx.append(quantise("x1", x_bf[1][:], M))
-        even_picked.append(gather_words("even_picked1", even_words[1], 0, 1) + gather_words("even_picked1", even_words[1], 1, 2, LAST_X))
+        even_picked.append(gather_words("even_picked1", even_words[1], 0, 1) + gather_words("even_picked1", even_words[1], 1, 2))
+        odd_planes.append(place_planes("odd_planes", odd_scales, P // 2, 1, 3 * SCALE_ROWS, nc.scalar, FIRST_X_ROWS + S))
 
         units = [(jp, t) for jp in range(J_PASSES) for t in range(PACK)]
 
@@ -192,7 +194,7 @@ def tile_list_motion_energy_pool_kernel(
             nc.tensor.matmul_mx(
                 out=target[:],
                 lhsT=picked[a][jp][:, t * P : (t + 1) * P].bitcast(FP8X4),
-                lhsT_scale=planes[SCALE_ROWS * a :, jp, t * P : (t + 1) * P],
+                lhsT_scale=planes[a][:, jp * PASS + t * P : jp * PASS + (t + 1) * P],
                 rhs=x_codes[:].bitcast(FP8X4),
                 rhs_scale=x_plane[:],
                 start=(a == 0),
@@ -217,13 +219,13 @@ def tile_list_motion_energy_pool_kernel(
                 )
 
         for u, (jp, t) in enumerate(units):
-            response = bank("even%d" % u, t, [P, M])
+            response = bank("even%d" % u, (u + PACK) % len(units), [P, M])
             for a in range(K_PASSES):
                 response_pass(response, even_picked, even_planes, jp, t, a)
             square(even_squares, response, jp, t)
 
         odd_picked = [
-            gather_words("odd_picked0", odd_words[0], 0, J_PASSES),
+            gather_words("odd_picked0", odd_words[0], 0, 1) + gather_words("odd_picked0", odd_words[0], 1, 2),
             gather_words("odd_picked1", odd_words[1], 0, 1) + gather_words("odd_picked1", odd_words[1], 1, 2),
         ]
 

@@ -37,10 +37,10 @@ RETURN_BANKS = (3, 4)
 TURN_BANKS = (0, 1, 2)
 SUM_BANKS = (5, 6, 7, 3, 4, 0)
 REGION = 4 * T
-FIRST_X_ROWS, LAST_WD_ROWS, LAST_ROOTS = (REGION * i for i in range(3))
+FIRST_X_ROWS, LAST_X_ROWS, LAST_WD_ROWS, LAST_ROOTS = (REGION * i for i in range(4))
 RUN = 8
 SCALAR_COLUMNS = 352
-TABLE_ROWS = K_PASSES * QUADRANTS * SCALE_ROWS
+FIRST_ROW = P - K_PASSES * QUADRANTS * SCALE_ROWS
 
 
 def tile_list_motion_energy_pool_kernel(
@@ -63,12 +63,10 @@ def tile_list_motion_energy_pool_kernel(
         offsets = keep.tile([P, S // LIST_GROUP], U16, name="offsets")
         nc.sync.dma_start(offsets[:], offs)
 
-        def load_table_scales(name, scales, first, clearing_engine):
+        def load_table_scales(name, scales):
             rows = sbuf(name, [P, T], U8)
-            other_half = (first + P // 2) % P
-            clearing_engine.memset(rows[first + TABLE_ROWS : first + P // 2, :].bitcast(I32), 0)
-            clearing_engine.memset(rows[other_half : other_half + P // 2, :].bitcast(I32), 0)
-            nc.sync.dma_start(rows[first : first + TABLE_ROWS, :].bitcast(I32), scales.rearrange("a q t -> (a q) t").bitcast(I32))
+            nc.vector.memset(rows[:FIRST_ROW, :].bitcast(I32), 0)
+            nc.sync.dma_start(rows[FIRST_ROW:, :].bitcast(I32), scales.rearrange("a q t -> (a q) t").bitcast(I32))
             return rows
 
         def load_table_words(name, words, a, place=None):
@@ -83,8 +81,8 @@ def tile_list_motion_energy_pool_kernel(
 
         gain_rows = sbuf("gain_rows", [P, J_PASSES * P], F32)
         nc.vector.memset(gain_rows[:], 0.0)
-        even_scale_rows = load_table_scales("even_scale_rows", tab_scales, 0, nc.gpsimd)
-        odd_scale_rows = load_table_scales("odd_scale_rows", tab2_scales, P // 2, nc.vector)
+        even_scale_rows = load_table_scales("even_scale_rows", tab_scales)
+        odd_scale_rows = load_table_scales("odd_scale_rows", tab2_scales)
         nc.sync.dma_start(
             gain_rows[:PACK, :].rearrange("t (b r) -> t b r", r=RUN), g.rearrange("(b t r) -> t b r", t=PACK, r=RUN)
         )
@@ -93,22 +91,23 @@ def tile_list_motion_energy_pool_kernel(
         nc.scalar.activation(warm[:], warm[:], ACT.Sqrt)
         x_raw = [load_x(0, FIRST_X_ROWS)]
         even_words = [load_table_words("even_words", tab_words, 0)]
-        x_raw.append(load_x(1))
+        x_raw.append(load_x(1, LAST_X_ROWS))
         even_words.append(load_table_words("even_words", tab_words, 1))
         odd_words = [load_table_words("odd_words", tab2_words, a) for a in range(K_PASSES)]
 
         ws_planes = sbuf("ws_planes", [P, K_PASSES, N], U8)
-        for q in range(QUADRANTS):
-            nc.sync.dma_start(
-                ws_planes[QUADRANT * q : QUADRANT * q + SCALE_ROWS, :, :].bitcast(I32),
-                ws_scales[:, SCALE_ROWS * q : SCALE_ROWS * (q + 1), :].rearrange("a r c -> r a c").bitcast(I32),
-            )
 
         wd_rows = []
         for nb in range(N_BLOCKS):
             rows = sbuf("wd_rows%d" % nb, [P, T], F32, LAST_WD_ROWS if nb == N_BLOCKS - 1 else None)
             nc.sync.dma_start(rows[:], wdT[nb * P : (nb + 1) * P, :])
             wd_rows.append(rows)
+            if nb == 0:
+                for q in range(QUADRANTS):
+                    nc.sync.dma_start(
+                        ws_planes[QUADRANT * q : QUADRANT * q + SCALE_ROWS, :, :].bitcast(I32),
+                        ws_scales[:, SCALE_ROWS * q : SCALE_ROWS * (q + 1), :].rearrange("a r c -> r a c").bitcast(I32),
+                    )
 
         ws_codes = sbuf("ws_codes", [P, K_PASSES, 2 * N], U8)
         nc.sync.dma_start(ws_codes[:].bitcast(I32), ws_words.rearrange("a p c -> p a c").bitcast(I32))
@@ -154,10 +153,10 @@ def tile_list_motion_energy_pool_kernel(
                     x_raw[a][:, :, last:].rearrange("p i (c e) -> p c i e", e=LINE),
                 )
 
-        def place_planes(name, picked, first, a, row, queue, place=None):
+        def place_planes(name, picked, a, row, queue, place=None):
             plane = sbuf("%s%d" % (name, a), [P, S], U8, place)
             for q in range(QUADRANTS):
-                source = first + SCALE_ROWS * (QUADRANTS * a + q)
+                source = FIRST_ROW + SCALE_ROWS * (QUADRANTS * a + q)
                 queue.dma_start(
                     plane[QUADRANT * q + row : QUADRANT * q + row + SCALE_ROWS, :].bitcast(I32),
                     picked[source : source + SCALE_ROWS, :, :].rearrange("p h c -> p (h c)").bitcast(I32),
@@ -174,18 +173,18 @@ def tile_list_motion_energy_pool_kernel(
         signs = sbuf("signs", [P, J_PASSES, PACK], BF16)
         nc.scalar.activation(signs[:], slot_gains[:], ACT.Sign)
 
-        even_planes = [place_planes("even_planes", even_scales, 0, 0, 0, nc.gpsimd)]
-        odd_planes = [place_planes("odd_planes", odd_scales, P // 2, 0, 2 * SCALE_ROWS, nc.gpsimd)]
+        even_closing = place_planes("even_planes", even_scales, 1, SCALE_ROWS, nc.gpsimd)
+        odd_closing = place_planes("odd_planes", odd_scales, 1, 3 * SCALE_ROWS, nc.gpsimd)
 
         x_bf = [sbuf("x_bf%d" % a, [P, M * PACK], BF16) for a in range(K_PASSES)]
         round_x(0, M)
         x_mx = [quantise("x0", x_bf[0][:], M)]
-        even_planes.append(place_planes("even_planes", even_scales, 0, 1, SCALE_ROWS, nc.scalar, FIRST_X_ROWS))
+        even_planes = [place_planes("even_planes", even_scales, 0, 0, nc.scalar, FIRST_X_ROWS), even_closing]
         even_picked = [gather_words("even_picked0", even_words[0], 0, 1) + gather_words("even_picked0", even_words[0], 1, 2)]
         round_x(1, SCALAR_COLUMNS)
         x_mx.append(quantise("x1", x_bf[1][:], M))
         even_picked.append(gather_words("even_picked1", even_words[1], 0, 1) + gather_words("even_picked1", even_words[1], 1, 2))
-        odd_planes.append(place_planes("odd_planes", odd_scales, P // 2, 1, 3 * SCALE_ROWS, nc.scalar, FIRST_X_ROWS + S))
+        odd_planes = [place_planes("odd_planes", odd_scales, 0, 2 * SCALE_ROWS, nc.scalar, LAST_X_ROWS), odd_closing]
 
         units = [(jp, t) for jp in range(J_PASSES) for t in range(PACK)]
 

@@ -37,9 +37,9 @@ RETURN_BANKS = (3, 4)
 TURN_BANKS = (0, 1, 2)
 SUM_BANKS = (5, 6, 7, 3, 4, 0)
 REGION = 4 * T
-FIRST_X_ROWS, LAST_X_ROWS, LAST_WD_ROWS, LAST_ROOTS = (REGION * i for i in range(4))
+LAST_X_ROWS, LAST_WD_ROWS, LAST_ROOTS = (REGION * i for i in range(3))
 RUN = 8
-SCALAR_COLUMNS = 352
+SCALAR_COLUMNS = 288
 FIRST_ROW = P - K_PASSES * QUADRANTS * SCALE_ROWS
 
 
@@ -89,8 +89,8 @@ def tile_list_motion_energy_pool_kernel(
         warm = sbuf("warm", [P, 1], F32)
         nc.vector.memset(warm[:], 1.0)
         nc.scalar.activation(warm[:], warm[:], ACT.Sqrt)
-        x_raw = [load_x(0, FIRST_X_ROWS)]
         even_words = [load_table_words("even_words", tab_words, 0)]
+        x_raw = [load_x(0)]
         x_raw.append(load_x(1, LAST_X_ROWS))
         even_words.append(load_table_words("even_words", tab_words, 1))
         odd_words = [load_table_words("odd_words", tab2_words, a) for a in range(K_PASSES)]
@@ -173,18 +173,20 @@ def tile_list_motion_energy_pool_kernel(
         signs = sbuf("signs", [P, J_PASSES, PACK], BF16)
         nc.scalar.activation(signs[:], slot_gains[:], ACT.Sign)
 
-        even_closing = place_planes("even_planes", even_scales, 1, SCALE_ROWS, nc.gpsimd)
-        odd_closing = place_planes("odd_planes", odd_scales, 1, 3 * SCALE_ROWS, nc.gpsimd)
+        even_planes = [
+            place_planes("even_planes", even_scales, 0, 0, nc.scalar),
+            place_planes("even_planes", even_scales, 1, SCALE_ROWS, nc.gpsimd),
+        ]
+        odd_planes = [place_planes("odd_planes", odd_scales, 0, 2 * SCALE_ROWS, nc.gpsimd)]
 
         x_bf = [sbuf("x_bf%d" % a, [P, M * PACK], BF16) for a in range(K_PASSES)]
+        even_picked = [gather_words("even_picked0", even_words[0], 0, J_PASSES)]
         round_x(0, M)
         x_mx = [quantise("x0", x_bf[0][:], M)]
-        even_planes = [place_planes("even_planes", even_scales, 0, 0, nc.scalar, FIRST_X_ROWS), even_closing]
-        even_picked = [gather_words("even_picked0", even_words[0], 0, 1) + gather_words("even_picked0", even_words[0], 1, 2)]
         round_x(1, SCALAR_COLUMNS)
         x_mx.append(quantise("x1", x_bf[1][:], M))
         even_picked.append(gather_words("even_picked1", even_words[1], 0, 1) + gather_words("even_picked1", even_words[1], 1, 2))
-        odd_planes = [place_planes("odd_planes", odd_scales, 0, 2 * SCALE_ROWS, nc.scalar, LAST_X_ROWS), odd_closing]
+        odd_planes.append(place_planes("odd_planes", odd_scales, 1, 3 * SCALE_ROWS, nc.scalar, LAST_X_ROWS))
 
         units = [(jp, t) for jp in range(J_PASSES) for t in range(PACK)]
 

from contextlib import ExitStack

import concourse.mybir as mybir
from concourse.masks import make_identity

K, T, S, M, N = 1024, 2048, 1024, 512, 384
FLOPS = 2 * (2 * K * S * M + S * N * M + K * N * M)

F32 = mybir.dt.float32
BF16 = mybir.dt.bfloat16
I32 = mybir.dt.int32
U32 = mybir.dt.uint32
U16 = mybir.dt.uint16
U8 = mybir.dt.uint8
FP8X4 = mybir.dt.float8_e4m3fn_x4
FP4X4 = mybir.dt.float4_e2m1fn_x4
ACT = mybir.ActivationFunctionType
MULT = mybir.AluOpType.mult
ADD = mybir.AluOpType.add

P = 128
PACK = 4
PASS = P * PACK
K_PASSES = K // PASS
J_PASSES = S // PASS
M_BLOCKS = M // P
N_BLOCKS = N // P
QUADRANTS = 4
QUADRANT = P // QUADRANTS
SCALE_ROWS = 4
LIST_GROUP = 16
LINE = 4
BANK_BYTES = 2048
ENERGY_BANKS = (4, 5, 6, 7)
GAIN_BANK = 7
RETURN_BANKS = (3, 4)
TURN_BANKS = (0, 1, 2)
SUM_BANKS = (5, 6, 7, 3, 4, 0)
REGION = 4 * T
LAST_X_ROWS, LAST_WD_ROWS, LAST_ROOTS = (REGION * i for i in range(3))
RUN = 8
SCALAR_COLUMNS = 288
FIRST_ROW = P - K_PASSES * QUADRANTS * SCALE_ROWS


def tile_list_motion_energy_pool_kernel(
    tc, x, tab_words, tab_scales, tab2_words, tab2_scales, offs, g, wdT, ws_words, ws_scales, out
):
    nc = tc.nc
    with ExitStack() as ctx:
        keep = ctx.enter_context(tc.tile_pool(name="keep", bufs=1))
        reuse = ctx.enter_context(tc.tile_pool(name="reuse", bufs=1))
        psum = ctx.enter_context(tc.psum_pool(name="psum", bufs=1))

        def sbuf(name, shape, dtype, place=None):
            if place is None:
                return keep.tile(shape, dtype, name=name, align_bytes=64)
            return reuse.tile(shape, dtype, name=name, align_bytes=64, offset=place)

        def bank(name, index, shape):
            return psum.tile(shape, F32, name=name, offset=index * BANK_BYTES)

        offsets = keep.tile([P, S // LIST_GROUP], U16, name="offsets")
        nc.sync.dma_start(offsets[:], offs)

        def load_table_scales(name, scales):
            rows = sbuf(name, [P, T], U8)
            nc.vector.memset(rows[:FIRST_ROW, :].bitcast(I32), 0)
            nc.sync.dma_start(rows[FIRST_ROW:, :].bitcast(I32), scales.rearrange("a q t -> (a q) t").bitcast(I32))
            return rows

        def load_table_words(name, words, a, place=None):
            tile_a = sbuf("%s%d" % (name, a), [P, T], I32, place)
            nc.sync.dma_start(tile_a[:], words[a].rearrange("p t i -> p (t i)").bitcast(I32))
            return tile_a

        def load_x(a, place=None):
            raw = sbuf("x_raw%d" % a, [P, PACK, M], F32, place)
            nc.sync.dma_start(raw[:], x[a * PASS : (a + 1) * PASS, :].rearrange("(p i) m -> p i m", i=PACK))
            return raw

        gain_rows = sbuf("gain_rows", [P, J_PASSES * P], F32)
        nc.vector.memset(gain_rows[:], 0.0)
        even_scale_rows = load_table_scales("even_scale_rows", tab_scales)
        odd_scale_rows = load_table_scales("odd_scale_rows", tab2_scales)
        nc.sync.dma_start(
            gain_rows[:PACK, :].rearrange("t (b r) -> t b r", r=RUN), g.rearrange("(b t r) -> t b r", t=PACK, r=RUN)
        )
        warm = sbuf("warm", [P, 1], F32)
        nc.vector.memset(warm[:], 1.0)
        nc.scalar.activation(warm[:], warm[:], ACT.Sqrt)
        even_words = [load_table_words("even_words", tab_words, 0)]
        x_raw = [load_x(0)]
        x_raw.append(load_x(1, LAST_X_ROWS))
        even_words.append(load_table_words("even_words", tab_words, 1))
        odd_words = [load_table_words("odd_words", tab2_words, a) for a in range(K_PASSES)]

        ws_planes = sbuf("ws_planes", [P, K_PASSES, N], U8)

        wd_rows = []
        for nb in range(N_BLOCKS):
            rows = sbuf("wd_rows%d" % nb, [P, T], F32, LAST_WD_ROWS if nb == N_BLOCKS - 1 else None)
            nc.sync.dma_start(rows[:], wdT[nb * P : (nb + 1) * P, :])
            wd_rows.append(rows)
            if nb == 0:
                for q in range(QUADRANTS):
                    nc.sync.dma_start(
                        ws_planes[QUADRANT * q : QUADRANT * q + SCALE_ROWS, :, :].bitcast(I32),
                        ws_scales[:, SCALE_ROWS * q : SCALE_ROWS * (q + 1), :].rearrange("a r c -> r a c").bitcast(I32),
                    )

        ws_codes = sbuf("ws_codes", [P, K_PASSES, 2 * N], U8)
        nc.sync.dma_start(ws_codes[:].bitcast(I32), ws_words.rearrange("a p c -> p a c").bitcast(I32))

        identity = sbuf("identity", [P, P], F32)
        nc.vector.memset(identity[:], 0.0)
        make_identity(nc, identity[:], nomemset=True)

        def gather_scales(name, rows):
            dealt = sbuf(name, [P, J_PASSES, PASS], U8)
            nc.vector.tensor_copy(dealt[:].rearrange("p h (t b r) -> p h b t r", t=PACK, r=RUN), rows[:].indirect(offsets[:]))
            return dealt

        def gather_words(name, words, first, last, place=None):
            cols = PASS // LIST_GROUP
            part = sbuf("%s%d" % (name, first), [P, last - first, PASS], U32, place)
            nc.vector.tensor_copy(
                part[:].rearrange("p h (t b r) -> p h b t r", t=PACK, r=RUN),
                words[:].bitcast(U32).indirect(offsets[:, first * cols : last * cols]),
            )
            return [part[:, h, :] for h in range(last - first)]

        def quantise(name, values, width, place=None):
            codes = sbuf(name + "_codes", [P, width], U32)
            plane = sbuf(name + "_plane", [P, width], U8, place)
            nc.vector.quantize_mx(out=codes[:].bitcast(FP8X4), scales=plane[:], in_=values)
            return codes, plane

        def quantise_columns(target, values, first, last):
            codes, plane = target
            nc.vector.quantize_mx(
                out=codes[:, first:last].bitcast(FP8X4), scales=plane[:, first:last], in_=values[:, PACK * first : PACK * last]
            )

        def round_x(a, last):
            nc.scalar.copy(
                x_bf[a][:, : PACK * last].rearrange("p (c e i) -> p c i e", e=LINE, i=PACK),
                x_raw[a][:, :, :last].rearrange("p i (c e) -> p c i e", e=LINE),
            )
            if last < M:
                nc.vector.tensor_copy(
                    x_bf[a][:, PACK * last :].rearrange("p (c e i) -> p c i e", e=LINE, i=PACK),
                    x_raw[a][:, :, last:].rearrange("p i (c e) -> p c i e", e=LINE),
                )

        def place_planes(name, picked, a, row, queue, place=None):
            plane = sbuf("%s%d" % (name, a), [P, S], U8, place)
            for q in range(QUADRANTS):
                source = FIRST_ROW + SCALE_ROWS * (QUADRANTS * a + q)
                queue.dma_start(
                    plane[QUADRANT * q + row : QUADRANT * q + row + SCALE_ROWS, :].bitcast(I32),
                    picked[source : source + SCALE_ROWS, :, :].rearrange("p h c -> p (h c)").bitcast(I32),
                )
            return plane[row:, :]

        even_scales = gather_scales("even_scales", even_scale_rows)
        odd_scales = gather_scales("odd_scales", odd_scale_rows)
        turned_gains = bank("turned_gains", GAIN_BANK, [P, J_PASSES, P])
        for jp in range(J_PASSES):
            nc.tensor.transpose(turned_gains[:, jp, :], gain_rows[:, jp * P : (jp + 1) * P], identity[:])
        slot_gains = sbuf("slot_gains", [P, J_PASSES, PACK], F32)
        nc.scalar.copy(slot_gains[:], turned_gains[:, :, :PACK])
        signs = sbuf("signs", [P, J_PASSES, PACK], BF16)
        nc.scalar.activation(signs[:], slot_gains[:], ACT.Sign)

        even_planes = [
            place_planes("even_planes", even_scales, 0, 0, nc.scalar),
            place_planes("even_planes", even_scales, 1, SCALE_ROWS, nc.gpsimd),
        ]
        odd_planes = [place_planes("odd_planes", odd_scales, 0, 2 * SCALE_ROWS, nc.gpsimd)]

        x_bf = [sbuf("x_bf%d" % a, [P, M * PACK], BF16) for a in range(K_PASSES)]
        even_picked = [gather_words("even_picked0", even_words[0], 0, J_PASSES)]
        round_x(0, M)
        x_mx = [quantise("x0", x_bf[0][:], M)]
        round_x(1, SCALAR_COLUMNS)
        x_mx.append(quantise("x1", x_bf[1][:], M))
        even_picked.append(gather_words("even_picked1", even_words[1], 0, 1) + gather_words("even_picked1", even_words[1], 1, 2))
        odd_planes.append(place_planes("odd_planes", odd_scales, 1, 3 * SCALE_ROWS, nc.scalar, LAST_X_ROWS))

        units = [(jp, t) for jp in range(J_PASSES) for t in range(PACK)]

        def response_pass(target, picked, planes, jp, t, a):
            x_codes, x_plane = x_mx[a]
            nc.tensor.matmul_mx(
                out=target[:],
                lhsT=picked[a][jp][:, t * P : (t + 1) * P].bitcast(FP8X4),
                lhsT_scale=planes[a][:, jp * PASS + t * P : jp * PASS + (t + 1) * P],
                rhs=x_codes[:].bitcast(FP8X4),
                rhs_scale=x_plane[:],
                start=(a == 0),
                stop=(a == K_PASSES - 1),
            )

        def square(squares, response, jp, t):
            nc.scalar.activation(squares[jp][:, t, :], response[:], ACT.Square, scale=slot_gains[:, jp, t : t + 1])

        even_squares = [sbuf("even_squares%d" % jp, [P, PACK, M], F32) for jp in range(J_PASSES)]
        odd_squares = [sbuf("odd_squares%d" % jp, [P, PACK, M], F32) for jp in range(J_PASSES)]

        def turn_squares(energy, squares, mb, first):
            for t in range(PACK):
                nc.tensor.matmul(
                    energy[:, t, :],
                    squares[:, t, mb * P : (mb + 1) * P],
                    identity[:],
                    start=(first and t == 0),
                    stop=(not first and t == PACK - 1),
                    is_transpose=True,
                )

        for u, (jp, t) in enumerate(units):
            response = bank("even%d" % u, (u + PACK) % len(units), [P, M])
            for a in range(K_PASSES):
                response_pass(response, even_picked, even_planes, jp, t, a)
            square(even_squares, response, jp, t)

        odd_picked = [
            gather_words("odd_picked0", odd_words[0], 0, 1) + gather_words("odd_picked0", odd_words[0], 1, 2),
            gather_words("odd_picked1", odd_words[1], 0, 1) + gather_words("odd_picked1", odd_words[1], 1, 2),
        ]

        def odd_part(u):
            jp, t = units[u]
            response = bank("odd%d" % u, (u + PACK) % len(units), [P, M])
            for a in range(K_PASSES):
                response_pass(response, odd_picked, odd_planes, jp, t, a)
            square(odd_squares, response, jp, t)

        h_bf = [sbuf("h_bf0", [P, M * PACK], BF16)]

        def turned_amplitude(mb):
            roots = sbuf("roots%d" % mb, [P, PASS], BF16, LAST_ROOTS if mb == M_BLOCKS - 1 else None)
            nc.scalar.activation(
                roots[:].rearrange("p (u q e) -> p u q e", u=2, e=2),
                energies[mb][:].rearrange("p (u e) q -> p u q e", e=2),
                ACT.Sqrt,
            )
            return roots

        def turn_back(half, roots):
            returned = bank("returned%d" % half, RETURN_BANKS[half], [P, 2, 2, P])
            for b in range(2):
                pairs = roots[2 * half + b][:].bitcast(F32)
                for u in range(2):
                    nc.tensor.transpose(returned[:, b, u, :], pairs[:, u * P : (u + 1) * P], identity[:])
            nc.scalar.copy(
                h_bf[0][:, half * 2 * PASS : (half + 1) * 2 * PASS].bitcast(F32).rearrange("p (b m u) -> p b m u", b=2, u=2),
                returned[:].rearrange("p b u m -> p b m u"),
            )

        second_energy = sbuf("second_energy", [P, PACK, M], F32)

        def add_squares(slots, first, last):
            nc.gpsimd.tensor_tensor(
                second_energy[:, slots, first:last], even_squares[1][:, slots, first:last], odd_squares[1][:, slots, first:last], ADD
            )

        def amplitude(half):
            nc.scalar.activation(
                h_bf[1][:, half * 2 * PASS : (half + 1) * 2 * PASS].rearrange("p (c e t) -> p c t e", e=LINE, t=PACK),
                second_energy[:, :, half * M // 2 : (half + 1) * M // 2].rearrange("p t (c e) -> p c t e", e=LINE),
                ACT.Sqrt,
            )

        def pick_pooling_weights(nb):
            picked = sbuf("wd_picked%d" % nb, [P, S], BF16)
            nc.vector.tensor_copy(
                picked[:].rearrange("p (u c r e) -> p c u e r", u=2, r=RUN, e=2), wd_rows[nb][:].indirect(offsets[:])
            )
            pairs = picked[:].bitcast(F32)
            turned = bank("turned%d" % nb, TURN_BANKS[nb], [P, 2, J_PASSES, P])
            for jp in range(J_PASSES):
                for u in range(2):
                    nc.tensor.transpose(turned[:, u, jp, :], pairs[:, P * (2 * u + jp) : P * (2 * u + jp + 1)], identity[:])
            return turned

        def sign_pooling_weights(nb, place=None):
            wd_bf = sbuf("wd_bf%d" % nb, [P, J_PASSES * PASS], BF16, place)
            nc.vector.tensor_tensor(
                wd_bf[:].rearrange("p (h n u e) -> p h n u e", h=J_PASSES, u=2, e=2),
                turned[nb][:].bitcast(BF16).rearrange("p u h (n e) -> p h n u e", e=2),
                signs[:].rearrange("p h (u e) -> p h u e", e=2).unsqueeze(2).to_broadcast([P, J_PASSES, P, 2, 2]),
                MULT,
            )
            return wd_bf

        pieces = [(nb, half * M // 2, (half + 1) * M // 2) for half in range(2) for nb in range(N_BLOCKS)]

        def drive_piece(piece):
            nb, first, last = pieces[piece]
            sums = bank("sums%d" % piece, SUM_BANKS[piece], [P, last - first])
            for a in range(K_PASSES):
                x_codes, x_plane = x_mx[a]
                nc.tensor.matmul_mx(
                    out=sums[:],
                    lhsT=ws_codes[:, a, 2 * P * nb : 2 * P * (nb + 1)].bitcast(FP4X4),
                    lhsT_scale=ws_planes[:, a, nb * P : (nb + 1) * P],
                    rhs=x_codes[:, first:last].bitcast(FP8X4),
                    rhs_scale=x_plane[:, first:last],
                    start=(a == 0),
                    stop=False,
                )
            return sums

        def pool_pass(piece, jp):
            nb, first, last = pieces[piece]
            wd_codes, wd_plane = wd_mx[nb, jp]
            h_codes, h_plane = h_mx[jp]
            nc.tensor.matmul_mx(
                out=sums[piece][:],
                lhsT=wd_codes.bitcast(FP8X4),
                lhsT_scale=wd_plane,
                rhs=h_codes[:, first:last].bitcast(FP8X4),
                rhs_scale=h_plane[:, first:last],
                start=False,
                stop=(jp == J_PASSES - 1),
            )

        def store_piece(piece, copy, queue):
            nb, first, last = pieces[piece]
            result = sbuf("result%d" % piece, [P, last - first], F32)
            copy(result[:], sums[piece][:])
            queue.dma_start(out[nb * P : (nb + 1) * P, first:last], result[:])

        def quantise_wd(nb, first, last, place=None):
            codes, plane = quantise("wd%d%d" % (nb, first), wd_bf[nb][:, first * PASS : last * PASS], (last - first) * P, place)
            for jp in range(first, last):
                cols = slice((jp - first) * P, (jp - first + 1) * P)
                wd_mx[nb, jp] = codes[:, cols], plane[:, cols]

        wd_mx, h_mx = {}, []
        for u in (0, 1, PACK, 2, 3, PACK + 1):
            odd_part(u)
            if u >= PACK:
                add_squares(slice(u - PACK, u - PACK + 1), 0, M)
        for u in (PACK + 2, PACK + 3):
            odd_part(u)
        for half in range(2):
            add_squares(slice(2, PACK), half * M // 2, (half + 1) * M // 2)
        energies = [bank("energy%d" % mb, ENERGY_BANKS[mb], [P, PACK, P]) for mb in range(M_BLOCKS)]
        for mb in range(M_BLOCKS):
            turn_squares(energies[mb], even_squares[0], mb, True)
            turn_squares(energies[mb], odd_squares[0], mb, False)
        roots = [turned_amplitude(mb) for mb in range(M_BLOCKS)]
        turned = [pick_pooling_weights(nb) for nb in range(N_BLOCKS)]
        for half in range(2):
            turn_back(half, roots)
        h_bf.append(sbuf("h_bf1", [P, M * PACK], BF16, LAST_ROOTS))
        for half in range(2):
            amplitude(half)
        wd_bf = [sign_pooling_weights(nb, LAST_WD_ROWS + 2 * S * nb) for nb in range(2)]
        sums = [drive_piece(piece) for piece in range(len(pieces))]
        quantise_wd(0, 0, J_PASSES)
        h_mx.append(quantise("h0", h_bf[0][:], M, LAST_WD_ROWS + 2 * S * N_BLOCKS))
        h_mx.append((sbuf("h1_codes", [P, M], U32), sbuf("h1_plane", [P, M], U8, LAST_WD_ROWS)))

        def finish_piece(piece, copy, queue):
            pool_pass(piece, 1)
            store_piece(piece, copy, queue)

        def open_block(nb, last):
            quantise_wd(nb, 0, last)
            for half in range(2):
                pool_pass(half * N_BLOCKS + nb, 0)

        for half in range(2):
            pool_pass(half * N_BLOCKS, 0)
        open_block(1, J_PASSES)
        wd_bf.append(sign_pooling_weights(2, LAST_WD_ROWS + 2 * S))
        for half in range(2):
            quantise_columns(h_mx[1], h_bf[1], half * M // 2, (half + 1) * M // 2)
            for nb in range(2):
                finish_piece(half * N_BLOCKS + nb, nc.scalar.copy, nc.sync)
        open_block(2, 1)
        quantise_wd(2, 1, J_PASSES)
        finish_piece(2, nc.scalar.copy, nc.sync)
        finish_piece(N_BLOCKS + 2, nc.vector.tensor_copy, nc.sync)
